import numpy as np, ml_dtypes
CORES = [2,6,10,14,18,22,26,30]
N = 8
BF = ml_dtypes.bfloat16
def gentries(a):
    return np.ascontiguousarray(a.reshape(8, 16, -1).transpose(0, 2, 1)).reshape(8, -1)
def gtable(e):
    e = np.asarray(e); return np.ascontiguousarray(e.reshape(8, -1, 16).transpose(0, 2, 1)).reshape(128, -1).astype(np.int32)
W, TB, K, DE = 4096, 512, 2, 2
def parts(rng):
    b = rng.integers(0, 128, (N, 8, 1, W)) + rng.integers(0, 129, (N, 8, 16, W))
    return np.minimum(b, 255), rng.integers(0, W, (N, 8, TB, 16)), rng.integers(0, N, (8, TB))
def pack(b, h, first):
    return {"bk": np.ascontiguousarray(b.reshape(N, 128, W)).astype(np.float32).astype(BF), "hand": np.stack([gtable(a.reshape(8, -1)) for a in h]),
            "ld": np.ascontiguousarray(np.tile(first[None], (N, 1, 1))).astype(np.int32)}
def setup_inputs(rng):
    b, h, first = parts(rng)
    return pack(b, h, first)
def setup_inputs_suits(rng):
    b, h, first = parts(rng); q = rng.integers(0, 4, (1, 8, TB, 1)); s = np.arange(N)[:, None, None, None]
    m = rng.integers(0, 4, (1, 8, TB, 1)); m[0, :, :4, 0] = np.arange(4)
    one = np.arange(16) == rng.integers(0, 16, (N, 8, TB, 1))
    su = np.where(m == 0, q, np.where(m == 1, (q + s) & 3, np.where(m == 2, np.where(one, q, (q + 1 + (h >> 2) % 3) & 3), h & 3)))
    return pack(b, (h >> 2) * 4 + su, first)
def setup_inputs_ties(rng):
    b, h, first = parts(rng); base = rng.integers(1, 255, (1, 8, 16, 1)); rot = rng.integers(0, 16, (N, 8, 1, W))
    m = rng.choice(np.array([0, 7, 8, 9, 9, 10, 16]), (N, 8, 1, W)); less = rng.integers(0, 2, (N, 8, 1, W))
    v = base + np.where(((np.arange(16)[:, None] + rot) & 15) < m, 1, -less)
    return pack(np.where(rng.random((N, 8, 1, W)) < 0.5, base, v), h, first)
def setup_inputs_alike(rng):
    b, h, first = parts(rng)
    h[:, 0] = (W - 1) * rng.integers(0, 2, (N, TB, 16)); h[:, 1] = h[:1, 1]; h[:, 2] = h[:, 2, :, :1]; h[:, 3] = h[:, 3, :1]
    h[:, 4] = rng.integers(0, 32, (N, TB, 16)); h[:, 5] = W - 1 - rng.integers(0, 16, (N, TB, 16))
    first[6] = 0; first[7] = N - 1
    return pack(b, h, first)
def setup_inputs_lords(rng):
    b, h, first = parts(rng); s = np.arange(N)[:, None, None, None]
    b[:, 0:2] = 7; b[:, 1, int(rng.integers(0, 16))] += rng.integers(0, 2, (N, W))
    b[:, 2:4] = 20 * s + rng.integers(0, 10, (N, 2, 16, W)); b[:, 4] = 255 * rng.integers(0, 2, (N, 1, W))
    b[:, 5] = 255 * (rng.random((N, 16, W)) < rng.random((N, 1, W)))
    m = rng.permutation(TB)[:, None]
    h = np.where(m < TB // 4, h | 255, np.where(m < TB // 2, h | 240, h))
    first[:] = rng.integers(0, N)
    return pack(b, h, first)
def setup_inputs_spread(rng):
    b, h, first = parts(rng)
    b = np.minimum((rng.random((N, 8, 16, W)) * np.exp2(rng.integers(0, 9, (N, 8, 1, W)))).astype(np.int64), 255)
    h = np.minimum((W * rng.random((N, 8, TB, 16)) ** 3).astype(np.int64), W - 1)
    return pack(b, h, np.minimum(first, rng.integers(0, N, (8, TB))))
def check_inputs(d):
    bad = []
    b = np.asarray(d["bk"]).astype(np.float32)
    if not np.all((b >= 0) & (b <= 255) & (b == np.floor(b))): bad.append("numbers of bk")
    for k, hi in (("hand", W - 1), ("ld", N - 1)):
        if np.min(d[k]) < 0 or np.max(d[k]) > hi: bad.append("range of " + k)
    if np.any(d["ld"] != d["ld"][:1]): bad.append("ld alike on all ranks")
    return bad
def reference(bk, hand, ld):
    B = np.asarray(bk).astype(np.float32).astype(np.int16).reshape(N, 8, 16, W)
    c = np.stack([gentries(a) for a in hand]).astype(np.int64).reshape(N, 8, TB, 16)
    lead = np.array(ld[0], np.int64); T = np.zeros(TB, np.int64); won = np.zeros((N, 8, TB), np.int64)
    e = np.zeros((N, 8, TB, 16), np.int64); beat = np.zeros((N, 8, TB, 16), bool); live = np.ones((N, 8, TB, 16), bool)
    S = np.arange(N)[:, None, None]; g = np.arange(8)[:, None]; t = np.arange(TB)[None, :]; R = np.arange(16)
    for deal in range(DE):
        rows, cards, wins = [], [], []
        for k in range(K):
            lr = np.argmax(np.where(live, e, -1), axis=3)[lead, g, t]
            L = c[lead, g, t, lr]; y = B[lead, g, :, L].transpose(0, 2, 1)[..., None]
            isl = S == lead
            live = live & ~(isl[..., None] & (R == lr[..., None]))
            a = ((c * L[..., None] >> 5) + c + 13 * T[:, None]) & (W - 1)
            for s in range(N):
                d = np.take_along_axis(B[s], a[s].reshape(8, 1, -1), 2).reshape(8, 16, TB, 16) - y
                e[s] = np.add.reduce(np.abs(d), axis=1, dtype=np.int64)
                beat[s] = np.add.reduce(d > 0, axis=1, dtype=np.int64) >= 9
            legal = live & ((c & 3) == (L & 3)[..., None])
            legal = np.where(np.any(legal, axis=3, keepdims=True), legal, live)
            good = legal & beat; has = np.any(good, axis=3) & ~isl
            row = np.where(has, np.argmin(np.where(good, e, 2 ** 20), axis=3), np.argmax(np.where(legal, e, -1), axis=3))
            row = np.where(isl, lr, row)[..., None]
            card = np.take_along_axis(c, row, 3)[..., 0]; score = np.where(has, np.take_along_axis(e, row, 3)[..., 0], -1)
            win = np.where(np.any(has, axis=0), np.argmax(score, axis=0), lead)
            live = live & (R != row)
            won = won + (S == win)
            T = np.add.reduce(card[win, g, t] & 255, axis=0)
            lead = win; rows.append(row); cards.append(card); wins.append(win)
        o = np.argsort(np.stack(wins) * K + np.arange(K)[:, None, None], axis=0)
        pile = np.take_along_axis(np.stack(cards), o[:, None], 0).reshape(N, K, 8, TB)
        for k in range(K):
            np.put_along_axis(c, rows[k], pile[:, k][..., None], 3)
            np.put_along_axis(e, rows[k], 0, 3)
        live = np.ones((N, 8, TB, 16), bool)
    return {"yc": np.stack([gtable(a.reshape(8, -1)) for a in c]).astype(np.float32), "yw": won.astype(np.float32)}

@@ -1,0 +1,669 @@
+from concourse.bass import DstId, RemoteDMATransfer
+from concourse.mybir import AluOpType as A, AxisListType, ActivationFunctionType as F
+
+NS, NC, W = 8, 4, 144
+KSL = [8, 10, 10, 10]
+H16 = "float16"
+f32, i32, u16, bf = "float32", "int32", "uint16", "bfloat16"
+SB = {
+    "book": (4096, bf), "handi": (512, i32), "handf": (512, f32), "ldi": (512, i32), "ldf": (512, f32),
+    "phi": (NC * 2048, f32), "xd": (NC * 2048, bf), "ybf": (NC * 256, bf),
+    "ck": (NC * W, f32), "cki": (NC * W, i32), "cs": (NC * W, i32), "co": (NC * 128, f32),
+    "v1": (NC * 128, f32), "v2": (NC * 128, i32), "v3": (NC * 128, i32), "offa": (NC * 128, u16),
+    "ee": (NC * W, H16), "be": (NC * W, H16), "beat": (NC * W, bf), "mat": (NC * W, bf), "oh": (2 * NC * W, bf),
+    "nn": (NC * W, f32), "m3": (NC * W, f32), "k3": (NC * W, f32), "so": (NC * 576, f32), "isl": (5 * NC * 8, bf),
+    "zz": (NC * 128, f32), "zi": (NC * 16, i32), "zj": (NC * 16, i32), "offy": (NC * 16, u16),
+    "ma": (16 * 16, f32), "la": (4 * 128, f32),
+    "ms": (16 * 144, f32), "lb": (4 * 640, f32), "bc": (16 * 160, f32), "al": (NC * 192, f32), "pl": (NC * 32, f32),
+    "ci": (NC * 16, i32), "cj": (NC * 16, i32), "cf": (NC * 16, f32), "fd": (NC * 32, f32), "dl": (NC * 16, f32),
+    "sm": (NC * 48, f32), "x0": (NC * W, f32), "x1": (NC * W, f32), "cb": (NC * 128, f32), "dup": (NC * 256, f32),
+    "tr": (NC * 256, f32), "yo": (512, f32), "wo": (512, f32),
+    "ow": (NC * 192, f32), "mi": (NC * 64, i32), "mz": (NC * 64, i32), "mf": (NC * 64, f32), "mn": (NC * 64, f32),
+    "mq": (NC * 64, f32), "rs": (NC * 128, f32), "ri": (16, i32), "wl": (16, i32), "wm": (8, i32), "wf": (8, f32),
+    "tt": (8, f32), "z2": (256, f32), "offs": (8, u16),
+    "ia": (128, i32), "ib": (128, i32), "ic": (W, i32), "idd": (256, i32), "ie": (W, i32), "iff": (128, i32),
+    "ig": (64, i32), "ih": (16, i32), "ij": (16, i32), "ik": (16, i32), "il": (16, i32), "im": (16, i32), "inn": (16, i32),
+    "pi": (8, i32), "pj": (8, i32), "pf": (24, f32), "c0": (W, f32), "c1": (W, f32),
+    "i32": (128, f32), "ibf": (6 * 128, bf), "i16": (3 * 128, H16), "gh": (8, f32), "hh": (16, f32),
+    "r2": (16, f32), "hs": (8, f32), "dm": (128, f32), "prm": (W, f32), "dupm": (256, f32), "kt": (W, f32), "kb": (128, f32),
+    "seg": (W, f32), "ckc": (W, bf), "csc": (W, H16), "rst": (64, f32), "sd": (64, f32), "lst": (128, u16),
+}
+SCRATCH = {k: ("sbuf", [128, n], d) for k, (n, d) in SB.items()}
+for _b in range(8):
+    SCRATCH["ps%d" % _b] = ("psum", [128, 512], f32)
+SEMAPHORES = (["nv", "ns", "nt", "ng", "loc", "dbk0", "dbk1", "dh", "dld", "dw"] + ["dy%d" % c for c in range(NC)]
+              + ["rl%d" % n for n in range(4)] + ["rm%d" % n for n in range(4)] + ["rb%d" % n for n in range(16)]
+              + ["rp%d" % c for c in range(NC)] + ["ra%d" % c for c in range(NC)])
+CNT = {"v": "nv", "s": "ns", "t": "nt", "g": "ng"}
+CY, PCY, GAT, CALL, HOP, ROW, SAME, CROSS = 1.04, 0.52, 1.56, 800, 2000, 35, 60.0, 120.0
+WTS = (2000.0, 2500.0, 3000.0)
+PLAN = {}
+
+
+def R(b, c0, c1, st=1, p=128):
+    return (b, c0, c1, st, p)
+
+
+def ap(T, r):
+    if not isinstance(r, tuple):
+        return r
+    if r[0] == "ind":
+        return ap(T, r[1]).indirect(ap(T, r[2]))
+    b, c0, c1, st, p = r
+    return T[b][0:p, c0:c1:st] if st > 1 else T[b][0:p, c0:c1]
+
+
+def width(r):
+    return 16 * (r[2][2] - r[2][1]) if r[0] == "ind" else (r[2] - r[1] + r[3] - 1) // r[3]
+
+
+def dty(r):
+    r = r[1] if r[0] == "ind" else r
+    return f32 if r[0].startswith("ps") else SB[r[0]][1]
+
+
+def bits(engs):
+    return sum(1 << e for e in engs)
+
+
+def owner_pairs(cores, topo):
+    free, pairs = list(range(len(cores))), []
+    while free:
+        a = free.pop(0)
+        good = [b for b in free if topo.same_plane(topo.chip(cores[a]), topo.chip(cores[b])) and topo.die(cores[a]) == topo.die(cores[b])]
+        b = good[0] if good else free[0]
+        free.remove(b)
+        pairs.append((a, b))
+    return pairs
+
+
+def build(s, cores, topo, ops, sends, arrive):
+    me = cores[s]
+    pairs = owner_pairs(cores, topo)
+    hist, bank, land, stage = {}, {}, [], [99]
+
+    def op(eng, cost, outs, ins, fn, kind="c", sem=None, lat=0.0):
+        o = {"s": s, "eng": eng, "cost": cost, "fn": fn, "kind": kind, "sem": sem, "lat": lat, "deps": {}, "rw": set(),
+             "id": len(ops), "st": stage[0]}
+        rd = []
+        for r in ins:
+            if isinstance(r, tuple):
+                rd += [r[1], r[2]] if r[0] == "ind" else [r]
+        for wr, rs in ((0, rd), (1, outs)):
+            for r in rs:
+                b, c0, c1 = r[0], r[1], r[2]
+                for (lb_, l0, l1, sm_) in land:
+                    if lb_ == b and c0 < l1 and l0 < c1:
+                        o["rw"].add(sm_)
+                keep = []
+                for (d0, d1, w, q) in hist.get(b, []):
+                    if c0 < d1 and d0 < c1 and (w or wr) and q is not o:
+                        o["deps"][q["id"]] = not (eng == "t" and q["eng"] == "t")
+                    if not (wr and r[3] == 1 and c0 <= d0 and d1 <= c1):
+                        keep.append((d0, d1, w, q))
+                keep.append((c0, c1, wr, o))
+                hist[b] = keep
+                if b.startswith("ps"):
+                    run = bank.setdefault(b, [[], []])
+                    if run[1] and run[1][-1]["eng"] != eng:
+                        run[0], run[1] = run[1], []
+                    for q in run[0]:
+                        o["deps"][q["id"]] = True
+                    if eng == "t" and run[1] and run[1][-1] is not o:
+                        o["deps"].setdefault(run[1][-1]["id"], False)
+                    if not run[1] or run[1][-1] is not o:
+                        run[1].append(o)
+        ops.append(o)
+        return o
+
+    def vcost(out, in0, two=False):
+        n = width(in0)
+        if in0[0] == "ind":
+            return 60 + n * GAT * CY
+        half = dty(out) in (bf, "float16", u16) and dty(in0) in (bf, "float16", u16)
+        return max(64, n * (2 if two else 1) * (0.5 if half else 1)) * CY
+
+    def tt(out, a, b, o_):
+        two = not (a[0].startswith("ps") or b[0].startswith("ps"))
+        op("v", vcost(out, a, two), [out], [a, b], lambda g, T: g.vector.tensor_tensor(ap(T, out), ap(T, a), ap(T, b), o_))
+
+    def ts(out, a, s1, o0, s2=None, o1=None):
+        if o1 is None:
+            fn = lambda g, T: g.vector.tensor_scalar(ap(T, out), ap(T, a), ap(T, s1), None, o0)
+        else:
+            fn = lambda g, T: g.vector.tensor_scalar(ap(T, out), ap(T, a), ap(T, s1), ap(T, s2), o0, o1)
+        op("v", vcost(out, a), [out], [a, s1, s2], fn)
+
+    def cp(out, a):
+        op("v", vcost(out, a), [out], [a], lambda g, T: g.vector.tensor_copy(ap(T, out), ap(T, a)))
+
+    def scan(out, d0, d1, o0, o1):
+        op("v", vcost(out, d1), [out], [d0, d1], lambda g, T: g.vector.tensor_tensor_scan(ap(T, out), ap(T, d0), ap(T, d1), 0.0, o0, o1))
+
+    def mset(out, v):
+        op("v", max(64, width(out)) * CY, [out], [], lambda g, T: g.vector.memset(ap(T, out), v))
+
+    def act(out, a, f=F.Copy, bias=None):
+        c = 80 + width(a) * CY * (GAT if a[0] == "ind" else 1)
+        if bias is None:
+            op("s", c, [out], [a], lambda g, T: g.scalar.activation(ap(T, out), ap(T, a), f))
+        else:
+            op("s", c, [out], [a, bias], lambda g, T: g.scalar.activation(ap(T, out), ap(T, a), f, bias=ap(T, bias)))
+
+    def mm(out, l, r, st, sp):
+        c = max(min(64, width(l)), width(r)) * (4 if dty(l) == f32 else 1) * PCY
+        op("t", c, [out], [l, r], lambda g, T: g.tensor.matmul(ap(T, out), ap(T, l), ap(T, r), st, sp))
+
+    def iota(out, pat, base=0, cm=0):
+        op("g", 160 + 2 * width(out) * CY, [out], [], lambda g, T: g.iota(ap(T, out), pat, base, cm))
+
+    def dma(q, sem, outs, ins, fn, lat):
+        op(q, 60, outs, ins, fn, "d", sem, lat)
+
+    def ind(win, c0, n):
+        return ("ind", win, R("lst", c0, c0 + n))
+
+    def send(parts, sem):
+        shared = None
+        for q in range(NS):
+            if topo.chip(cores[q]) != topo.chip(me):
+                e = topo.engines(me, cores[q])
+                shared = e if shared is None else [x for x in shared if x in e]
+        trs = []
+        for (src, dst, qs) in parts:
+            near = [q for q in qs if topo.chip(cores[q]) == topo.chip(me)]
+            far = [q for q in qs if q not in near]
+            trs += [(src, dst, x, x is near) for x in (near, far) if x]
+        nf = len([t for t in trs if not t[3]])
+        final, kf, rows = [], 0, 0
+        for (src, dst, qs, isnear) in trs:
+            if isnear:
+                e = [x for x in topo.engines(me, cores[qs[0]]) if x not in shared]
+            else:
+                k = len(shared) // nf
+                e = shared[kf * k:(kf + 1) * k]
+                kf += 1
+            final.append((src, dst, qs, e))
+            rows = max(rows, 128 * len(qs) // len(e))
+            for q in qs:
+                arrive[(q, sem)] = arrive.get((q, sem), 0) + len(e)
+
+        def fn(g, T):
+            tl = [RemoteDMATransfer(dst_ids=[DstId(rid=topo.addr(cores[q])[0], pnc=topo.addr(cores[q])[1]) for q in qs],
+                                    dma_engine_mask=bits(e), remote_sem=T.sem[sem], srcs=[ap(T, src)], dsts=[ap(T, dst) for q in qs])
+                  for (src, dst, qs, e) in final]
+            return g.remote_dma_fused(tl, local_sem=T.sem.loc)
+        o = op("g", CALL, [], [p[0] for p in parts], fn, "r", sem, HOP + rows * (ROW + width(parts[0][0]) * 0.2))
+        o["loc"] = sum(len(t[3]) for t in final)
+        for t in final:
+            for q in t[2]:
+                sends.setdefault((q, sem), []).append(o)
+
+    own = [(c, h) for c in range(NC) for h in range(2) if pairs[c][h] == s][0]
+    oc, ohf = own
+    others = [q for q in range(NS) if q != s]
+    for n in range(4):
+        for q in others:
+            land.append(("lb", 640 * n + 80 * q, 640 * n + 80 * q + 80, "rl%d" % n))
+            land.append(("la", 128 * n + 16 * q, 128 * n + 16 * q + 16, "rm%d" % n))
+        for c in range(NC):
+            for h in range(2):
+                if own != (c, h):
+                    land.append(("bc", 160 * (4 * n + c) + 80 * h, 160 * (4 * n + c) + 80 * h + 80, "rb%d" % (4 * n + c)))
+    for c in range(NC):
+        for q in others:
+            land.append(("al", 192 * c + 24 * q, 192 * c + 24 * q + 24, "ra%d" % c))
+        for j in range(2):
+            if (2 * s + j) % NS != s:
+                land.append(("pl", 32 * c + 16 * j, 32 * c + 16 * j + 16, "rp%d" % c))
+
+    dma("y", "dh", [R("handi", 0, 512)], [], lambda g, T: g.sync.dma_start(T.handi[:], T.hand[:]), 2300)
+    dma("s", "dld", [R("ldi", 0, 512)], [], lambda g, T: g.scalar.dma_start(T.ldi[0:8, :], T.ld[:]), 2000)
+    dma("y", "dbk0", [R("book", 0, 2048)], [], lambda g, T: g.sync.dma_start(T.book[:, 0:2048], T.bk[:, 0:2048]), 5500)
+    dma("s", "dbk1", [R("book", 2048, 4096)], [], lambda g, T: g.scalar.dma_start(T.book[:, 2048:4096], T.bk[:, 2048:4096]), 5500)
+    BOOK = R("book", 0, 4096)
+
+    def col(k):
+        return R("pf", k, k + 1)
+    iota(R("pi", 0, 1), [[0, 1]], 0, 1)
+    P = R("pi", 0, 1)
+    ts(R("pj", 0, 1), P, 15, A.bitwise_and)
+    ts(R("pj", 1, 2), P, 7, A.bitwise_and)
+    ts(R("pj", 2, 3), P, 3, A.arith_shift_right, 1, A.bitwise_and)
+    ts(R("pj", 3, 4), P, 4, A.arith_shift_right, 1, A.bitwise_and)
+    ts(R("pj", 4, 5), P, 4, A.arith_shift_right)
+    cp(R("pf", 0, 5), R("pj", 0, 5))
+    cp(col(5), P)
+    soff, yoff = (64, 0) if ohf == 0 else (0, 16)
+    ts(col(6), col(4), 18.0, A.mult, 15.0, A.add)
+    tt(col(7), col(6), col(0), A.subtract)
+    ts(col(8), col(1), -80.0, A.mult, col(2), A.add)
+    ts(col(9), col(1), -24.0, A.mult, col(2), A.add)
+    ts(col(10), col(1), 32.0, A.mult, col(2), A.add)
+    ts(col(11), col(3), 16.0, A.mult, col(10), A.add)
+    ts(col(12), col(1), 18.0, A.mult, 16.0, A.add)
+    ts(col(13), col(5), float(yoff - 64 * ohf), A.add)
+    ts(col(14), col(1), -16.0, A.mult, col(2), A.add)
+    mset(col(15), -1.0 / 64)
+    mset(col(16), float(2 ** 18 + s * 2 ** 19))
+    iota(R("ih", 0, 16), [[1, 16]])
+    IH = lambda n: R("ih", 0, n)
+    L_OB, L_Z, L_M0, L_M1, L_L, L_PA, L_PB, L_AP, L_CP, L_OC, L_DUP, L_G, L_OH, L_I = 0, 8, 16, 18, 20, 22, 30, 34, 38, 46, 54, 70, 80, 90
+    ts(R("lst", L_OB, L_OB + 8), IH(8), 0.0, A.mult, col(1), A.add)
+    ts(R("lst", L_Z, L_Z + 8), IH(8), 18.0, A.mult, 15.0, A.add)
+    ts(R("lst", L_M0, L_M0 + 1), col(2), 144.0, A.mult, col(12), A.add)
+    ts(R("lst", L_M1, L_M1 + 1), col(2), 288.0, A.mult, col(12), A.add)
+    ts(R("lst", L_L, L_L + 1), col(12), -1.0, A.add)
+    ts(R("ij", 0, 16), IH(16), 2.0, A.mult)
+    ts(R("lst", L_PA, L_PA + 8), R("ij", 0, 8), col(14), A.add, 112.0, A.add)
+    ts(R("lst", L_PB, L_PB + 4), R("ij", 0, 4), col(8), A.add, float(560 + soff), A.add)
+    ts(R("lst", L_AP, L_AP + 4), R("ij", 0, 4), col(9), A.add, 168.0, A.add)
+    ts(R("lst", L_OC, L_OC + 8), R("ij", 0, 8), col(11), A.add)
+    ts(R("ik", 0, 8), IH(8), 18.0, A.mult, 15.0, A.add)
+    ts(R("lst", L_CP, L_CP + 8), R("ik", 0, 8), col(0), A.subtract)
+    iota(R("il", 0, 16), [[16, 8], [0, 2]])
+    ts(R("lst", L_DUP, L_DUP + 16), R("il", 0, 16), col(0), A.add)
+    ts(R("im", 0, 9), IH(9), 16.0, A.mult, col(0), A.add)
+    ts(R("inn", 0, 9), R("im", 0, 9), 3641.0, A.mult)
+    ts(R("im", 0, 9), R("inn", 0, 9), 16, A.arith_shift_right)
+    cp(R("lst", L_G, L_G + 9), R("im", 0, 9))
+    ts(R("lst", L_OH, L_OH + 9), R("im", 0, 9), 18.0, A.mult, 16.0, A.add)
+    cp(R("lst", L_I, L_I + 8), IH(8))
+    iota(R("ia", 0, 128), [[-1, 128]], 0, 1)
+    IA = R("ia", 0, 128)
+    I32 = R("i32", 0, 128)
+    ts(I32, IA, 0.0, A.is_equal)
+    IB = [R("ibf", 128 * k, 128 * k + 128) for k in range(6)]
+    for k, w in enumerate((1.0, -1.0, 2.0 ** 18, 2.0 ** 20, -2.0 ** 21, 2.0 ** 23)):
+        ts(IB[k], IA, 0.0, A.is_equal, w, A.mult)
+    IH16 = [R("i16", 128 * k, 128 * k + 128) for k in range(3)]
+    for k, w in enumerate((1.0, 64.0, -128.0)):
+        ts(IH16[k], IA, 0.0, A.is_equal, w, A.mult)
+    GH = R("gh", 0, 8)
+    ts(GH, IH(8), col(4), A.is_equal)
+    ts(R("hs", 0, 4), R("gh", 4 * ohf, 4 * ohf + 4), 80.0, A.mult)
+    ts(R("hs", 4, 8), R("gh", 4 * ohf, 4 * ohf + 4), col(13), A.mult)
+    iota(R("ib", 0, 128), [[0, 8], [1, 16]])
+    DM = R("dm", 0, 128)
+    ts(DM, R("ib", 0, 128), col(0), A.is_equal)
+    if ohf == 0:
+        cp(R("hh", 0, 8), GH)
+        ts(R("hh", 8, 16), GH, 2048.0, A.mult)
+        ts(R("r2", 0, 8), GH, 32.0, A.mult)
+    iota(R("ic", 0, W), [[1, W]])
+    ts(R("prm", 0, W), R("ic", 0, W), col(7), A.is_equal)
+    iota(R("ie", 0, W), [[0, 8], [1, 18]])
+    IE = R("ie", 0, W)
+    ts(R("c0", 0, W), IE, -4096.0, A.mult, 61440.0, A.add)
+    ts(R("c1", 0, W), IE, 16.0, A.is_lt)
+    ts(R("kt", 0, W), R("c0", 0, W), 0.0, A.max)
+    SEG = R("seg", 0, W)
+    ts(SEG, IE, 1.0, A.min)
+    ts(R("ckc", 0, W), R("c1", 0, W), 2.0 ** 21, A.mult, 2.0 ** 17, A.add)
+    ts(R("csc", 0, W), R("c1", 0, W), 15.0, A.mult, -2048.0, A.add)
+    iota(R("ig", 0, 64), [[0, 8], [1, 8]])
+    ts(R("rst", 0, 64), R("ig", 0, 64), 0.0, A.is_equal, 65536.0, A.mult)
+    ts(R("sd", 0, 64), R("ig", 0, 64), -1.0, A.mult, 7.0, A.add)
+    iota(R("idd", 0, 256), [[16, 8], [0, 2], [1, 16]], 0, -1)
+    ts(R("dupm", 0, 256), R("idd", 0, 256), 0.0, A.is_equal)
+    iota(R("iff", 0, 128), [[0, 8], [4096, 16]])
+    cp(R("kb", 0, 128), R("iff", 0, 128))
+    cp(R("ldf", 0, 512, 1, 8), R("ldi", 0, 512, 1, 8))
+
+    def B(b, c, n, a=0, e=None, st=1, k=0):
+        return R(b, (k * NC + c) * n + a, (k * NC + c) * n + (n if e is None else e), st)
+
+    def PS(c, a, e, st=1, p=128):
+        return R("ps%d" % (3 + c), a, e, st, p)
+
+    def SO(c, j, a=0, e=W, st=1):
+        return B("so", c, 576, W * j + a, W * j + e, st)
+
+    def suits(c):
+        cp(B("cki", c, W), B("ck", c, W))
+        ts(B("cs", c, W), B("cki", c, W), 3, A.bitwise_and)
+
+    def to_o(c, src):
+        op("v", 256 * CY, [B("tr", c, 256)], [src], lambda g, T: g.vector.transpose(ap(T, B("tr", c, 256)), ap(T, src)))
+        ts(B("co", c, 128), ind(B("tr", c, 256), L_OC, 8), -2048.0, A.add)
+
+    def pick(c, src):
+        cp(B("mi", c, 64), src)
+        ts(B("mz", c, 64), B("mi", c, 64), 6, A.arith_shift_right, 8191, A.bitwise_and)
+        cp(B("mf", c, 64), B("mz", c, 64))
+        scan(B("mn", c, 64), R("rst", 0, 64), B("mf", c, 64), A.add, A.min)
+        tt(B("mq", c, 64), B("mf", c, 64), B("mn", c, 64), A.is_gt)
+
+    def play(n, c):
+        dst = R("la", 128 * n + 16 * s, 128 * n + 16 * s + 16)
+        src = dst if c == oc else B("ma", c, 16, k=n)
+        act(src, ind(B("so", c, 576, 0, 432), L_M1 if n % 2 == 0 else L_M0, 1), F.Identity, col(16))
+        send([(src, dst, [q for q in pairs[c] if q != s])], "rm%d" % n)
+        if c != oc:
+            return
+        act(R("ow", 0, 128), ind(R("la", 128 * n, 128 * n + 128), L_PA, 8))
+        pick(0, R("ow", 0, 64))
+        scan(R("rs", 0, 64), R("mq", 0, 64), R("ow", 64, 128), A.mult, A.max)
+        cp(R("ri", 0, 8), R("rs", 7, 64, 8))
+        ts(R("wl", 8, 16), R("ri", 0, 8), 19, A.arith_shift_right)
+        tt(R("z2", 0, 128), ind(R("wl", 8, 16), L_I, 8), DM, A.mult)
+        mm(R("ps7", 0, 4), R("z2", 0, 128), R("hs", 0, 4), True, False)
+        mm(R("ps7", 0, 4), DM, R("hs", 4, 8), False, True)
+        cp(R("offs", 0, 4), R("ps7", 0, 4))
+        if ohf == 0:
+            ts(R("wm", 0, 8), R("ri", 0, 8), 255, A.bitwise_and)
+            cp(R("wf", 0, 8), R("wm", 0, 8))
+            op("v", 64 * CY, [R("tt", 0, 1)], [R("wf", 0, 8)],
+               lambda g, T: g.vector.tensor_reduce(T.tt[:, 0:1], T.wf[:, 0:8], AxisListType.X, A.add))
+            ts(R("tt", 1, 2), R("tt", 0, 1), 416.0, A.mult, float(65536 - 2 ** 23), A.add)
+            ts(R("r2", 8, 16), GH, R("tt", 1, 2), A.mult)
+
+    def offer(n, c):
+        m, b0 = 144 * (4 * n + c), 160 * (4 * n + c)
+        act(R("ms", m + 64, m + 80), ind(SO(c, 3), L_L, 1), F.Identity, col(16))
+        tt(B("zz", c, 128), ind(SO(c, 3), L_Z, 8), DM, A.mult)
+        mm(PS(c, 432, 440), B("zz", c, 128), GH, True, True)
+        cp(B("zi", c, 16, 0, 8), PS(c, 432, 440))
+        ts(B("zj", c, 16, 0, 8), B("zi", c, 16, 0, 8), 4095, A.bitwise_and)
+        cp(B("offy", c, 16, 0, 8), B("zj", c, 16, 0, 8))
+        for h in range(2):
+            act(R("ms", m + 80 * h, m + 80 * h + 64), ("ind", BOOK, B("offy", c, 16, 4 * h, 4 * h + 4)))
+        dst = R("lb", 640 * n + 80 * s, 640 * n + 80 * s + 80)
+        send([(R("ms", m + 64 * h, m + 64 * h + 80), dst, [pairs[c][h]]) for h in range(2) if pairs[c][h] != s], "rl%d" % n)
+        if c != oc:
+            return
+        act(dst, R("ms", m + 64 * ohf, m + 64 * ohf + 80))
+        lb = R("lb", 640 * n, 640 * n + 640)
+        act(R("ow", 128, 192), ind(lb, L_PB, 4))
+        act(R("bc", b0 + 16 + 64 * ohf, b0 + 80 + 64 * ohf), ("ind", lb, R("offs", 0, 4)))
+        scan(R("rs", 64, 128), R("mq", 0, 64), R("ow", 128, 192), A.mult, A.max)
+        cp(R("ri", 8, 16), R("rs", 71, 128, 8))
+        ts(R("wl", 0, 8), R("ri", 8, 16), 4095 if ohf == 0 else 3, A.bitwise_and)
+        if ohf == 0:
+            tt(R("z2", 128, 256), ind(R("wl", 0, 8), L_I, 8), DM, A.mult)
+            mm(R("ps7", 16, 32), DM, R("r2", 0, 16), True, False)
+            mm(R("ps7", 16, 32), R("z2", 128, 256), R("hh", 0, 16), False, True)
+            cp(R("bc", b0, b0 + 16), R("ps7", 16, 32))
+        else:
+            cp(R("bc", b0 + 144, b0 + 160), R("wl", 0, 16))
+        src = R("bc", b0 + 80 * ohf, b0 + 80 * ohf + 80)
+        send([(src, src, others)], "rb%d" % (4 * n + c))
+
+    def cards(c, dst):
+        cp(B("ci", c, 16), SO(c, 1, 16, 2 * W, 18))
+        ts(B("cj", c, 16), B("ci", c, 16), 4095, A.bitwise_and)
+        cp(dst, B("cj", c, 16))
+
+    def diffs(c, mine, got):
+        for j in range(2):
+            g0, g1 = (R(got[j][0], got[j][1] + 8 * k, got[j][1] + 8 * k + 8) for k in range(2))
+            tt(B("fd", c, 32, 8 * j, 8 * j + 8), g1, R(mine[0], mine[1] + 8 * j, mine[1] + 8 * j + 8), A.subtract)
+            tt(B("fd", c, 32, 16 + 8 * j, 24 + 8 * j), g0, g1, A.subtract)
+
+    def deltas(c, src0):
+        for j in range(2):
+            tt(B("sm", c, 48, 8 + 8 * j, 16 + 8 * j), B("fd", c, 32, 16 + 8 * j, 24 + 8 * j), src0, A.mult)
+        tt(B("dl", c, 16), B("sm", c, 48, 8, 24), B("fd", c, 32, 0, 16), A.add)
+
+    order = A.is_le if s < NS // 2 else A.is_gt
+
+    def redeal(c, w0, w1):
+        tt(B("sm", c, 48, 0, 8), w0, w1, order)
+        deltas(c, B("sm", c, 48, 0, 8))
+        for j, x in enumerate(("x0", "x1")):
+            tt(B(x, c, W), ind(B("dl", c, 16, 8 * j, 8 * j + 8), L_G, 9), B("oh", c, W, k=j), A.mult)
+            mm(PS(c, 256, 256 + W), I32, B(x, c, W), j == 0, j == 1)
+        tt(B("ck", c, W), PS(c, 256, 256 + W), B("ck", c, W), A.add)
+        tt(B("cb", c, 128), ind(B("ck", c, W), L_CP, 8), R("kb", 0, 128), A.subtract)
+
+    for c in range(NC):
+        stage[0] = c
+        hf = R("handf", 128 * c, 128 * c + 128)
+        cp(hf, R("handi", 128 * c, 128 * c + 128))
+        mset(B("so", c, 576), 0.0)
+        mm(PS(c, 0, W), hf, R("prm", 0, W), True, True)
+        mm(PS(c, W, W + 8), R("ldf", 128 * c, 128 * c + 128, 1, 8), R("i32", 0, 8, 1, 8), True, True)
+        tt(B("ck", c, W), PS(c, 0, W), R("kt", 0, W), A.add)
+        ts(SO(c, 0, 16, W, 18), PS(c, W, W + 8), float(s), A.not_equal, 960.0, A.mult)
+        cp(SO(c, 3, 15, W, 18), B("ck", c, W, 15, W, 18))
+        play(0, c)
+        offer(0, c)
+        stage[0] = 4 + c
+        suits(c)
+        cp(B("dup", c, 256), ind(hf, L_DUP, 16))
+        to_o(c, B("dup", c, 256))
+
+    MAG = 1.5 * 2.0 ** 23
+    dbank = [0]
+    for n in range(4):
+        KS = KSL[n]
+        for c in range(NC):
+            stage[0] = 4 + 4 * n + c
+            m = 160 * (4 * n + c)
+            win = R("bc", m + 152, m + 160)
+            isl = B("isl", c, 8, k=n)
+            ts(isl, win, float(s), A.is_equal)
+            if n == 2:
+                redeal(c, R("bc", m - 640 + 152, m - 640 + 160), win)
+                mm(PS(c, 0, 256), B("cb", c, 128), R("dupm", 0, 256), True, True)
+                to_o(c, PS(c, 0, 256))
+                suits(c)
+            tt(B("ck", c, W, 16, W, 18), isl, SO(c, 3, 15, W, 18), A.mult)
+            tt(B("v1", c, 128), ind(R("bc", m, m + 8), L_OB, 8), B("co", c, 128), A.mult)
+            tt(B("v2", c, 128), ind(R("bc", m + 8, m + 16), L_OB, 8), B("v1", c, 128), A.add)
+            ts(B("v3", c, 128), B("v2", c, 128), 5, A.arith_shift_right, 4095, A.bitwise_and)
+            cp(B("offa", c, 128), B("v3", c, 128))
+            act(B("ybf", c, 256, 0, 128), R("bc", m + 16, m + 144))
+            cp(B("ybf", c, 256, 128, 256), B("ybf", c, 256, 0, 128))
+            tt(B("mat", c, W), ind(R("bc", m + 144, m + 152), L_G, 9), B("cs", c, W), A.is_equal)
+            mm(PS(c, 0, W), IH16[0], R("csc", 0, W), True, False)
+            us = [(k, min(k + 4, KS), True) for k in range(0, KS, 4)]
+            uv = [(k, min(k + 4, 16), False) for k in range(KS, 16, 4)]
+            units = us[:1] + uv[:1] + us[1:2] + uv[1:] + us[2:]
+            for iu, (k0, k1, onS) in enumerate(units):
+                xd = lambda a, e: B("xd", c, 2048, 128 * a, 128 * e)
+                off = lambda a, e: ("ind", BOOK, B("offa", c, 128, 8 * a, 8 * e))
+                ph = B("phi", c, 2048, 128 * k0, 128 * k1)
+                if onS:
+                    d = "ps%d" % dbank[0]
+                    dbank[0] = (dbank[0] + 1) % 3
+                    act(xd(k0, k1), off(k0, k1))
+                    mm(R(d, 0, 128 * (k1 - k0)), IB[0], xd(k0, k1), True, False)
+                    for k in range(k0, k1, 2):
+                        e = min(k + 2, k1)
+                        mm(R(d, 128 * (k - k0), 128 * (e - k0)), IB[1], B("ybf", c, 256, 0, 128 * (e - k)), False, e == k1)
+                    act(ph, R(d, 0, 128 * (k1 - k0)), F.Abs, col(15))
+                else:
+                    for k in range(k0, k1, 2):
+                        e = min(k + 2, k1)
+                        tt(xd(k, e), off(k, e), B("ybf", c, 256, 0, 128 * (e - k)), A.subtract)
+                    act(ph, xd(k0, k1), F.Abs, col(15))
+                for k in range(k0, k1):
+                    mm(PS(c, 15 - k, W, 18), B("phi", c, 2048, 128 * k, 128 * k + 128), GH, False, iu == len(units) - 1 and k == k1 - 1)
+            ee, beat, ck, nn = B("ee", c, W), B("beat", c, W), B("ck", c, W), B("nn", c, W)
+            ts(ee, PS(c, 0, W), MAG, A.add, MAG, A.subtract)
+            tt(beat, PS(c, 0, W), ee, A.is_lt)
+            tt(B("be", c, W), beat, ee, A.mult)
+            K = PS(c, W, 2 * W)
+            mm(K, IB[0], R("ckc", 0, W), True, False)
+            mm(K, IB[3], B("mat", c, W), False, False)
+            mm(PS(c, W + 16, 2 * W, 18), IB[5], isl, False, False)
+            if n % 2:
+                mm(K, IB[4], B("oh", c, W, k=0), False, False)
+            mm(K, IH16[1], ee, False, False)
+            mm(K, IB[2], beat, False, False)
+            mm(K, IH16[2], B("be", c, W), False, True)
+            scan(SO(c, 0), SEG, K, A.mult, A.max)
+            tt(nn, K, SO(c, 0), A.is_lt)
+            scan(SO(c, 1 + n % 2), nn, ck, A.mult, A.max)
+            if n == 3:
+                a0 = 192 * c + 24 * s
+                ts(R("al", a0, a0 + 8), SO(c, 0, 16, W, 18), float(2 ** 18), A.add)
+                cards(c, R("al", a0 + 8, a0 + 24))
+                send([(R("al", a0, a0 + 24), R("al", a0, a0 + 24), others)], "ra%d" % c)
+            if n == 1:
+                cf = B("cf", c, 16)
+                cards(c, cf)
+                to = [s // 2, NS // 2 + s // 2]
+                dst = B("pl", c, 32, 16 * (s % 2), 16 * (s % 2) + 16)
+                send([(cf, dst, [q for q in to if q != s])], "rp%d" % c)
+                if s in to:
+                    cp(dst, cf)
+            if n < 3:
+                play(n + 1, c)
+            oh = B("oh", c, W, k=n % 2)
+            tt(oh, ind(SO(c, 1 + n % 2), L_OH, 9), ck, A.is_equal)
+            if n == 3:
+                u = [192 * c + 24 * ((2 * s + j) % NS) + 8 for j in range(2)]
+                diffs(c, ("al", a0 + 8), [("al", x) for x in u])
+                act(B("ow", c, 192, 0, 64), ind(B("al", c, 192), L_AP, 4))
+                pick(c, B("ow", c, 192, 0, 64))
+                scan(B("rs", c, 128, 0, 64), B("mq", c, 64), R("sd", 0, 64), A.mult, A.max)
+                w1 = B("rs", c, 128, 7, 64, 8)
+                redeal(c, win, w1)
+                ts(B("isl", c, 8, k=4), w1, float(s), A.is_equal)
+                mm(PS(c, 0, 128), B("cb", c, 128), I32, True, True)
+                for k in range(1, 5):
+                    mm(PS(c, 128, 256, 1, 8), B("isl", c, 8, k=k), IB[0], k == 1, k == 4)
+                act(B("yo", c, 128), PS(c, 0, 128))
+                act(R("wo", 128 * c, 128 * c + 128, 1, 8), PS(c, 128, 256, 1, 8))
+                dma("y", "dy%d" % c, [], [B("yo", c, 128)],
+                    lambda g, T, c=c: g.sync.dma_start(T.yc[:, 128 * c:128 * c + 128], T.yo[:, 128 * c:128 * c + 128]), 2000)
+                continue
+            K3 = PS(c, 2 * W, 3 * W)
+            mm(K3, IB[0], R("ckc", 0, W), True, False)
+            mm(K3, IH16[1], ee, False, False)
+            if n == 1:
+                mm(K3, IB[4], B("oh", c, W, k=0), False, False)
+            mm(K3, IB[4], oh, False, True)
+            row0 = B("ck", c, W, 15, W, 18)
+            if n == 1:
+                ts(B("k3", c, W), K3, float(2 ** 21 + 960), A.max)
+                K3 = B("k3", c, W)
+                diffs(c, ("cf", 16 * c), [("pl", 32 * c), ("pl", 32 * c + 16)])
+                ts(B("sm", c, 48, 0, 8), win, float(s), order)
+                deltas(c, B("sm", c, 48, 0, 8))
+                for j in range(2):
+                    tt(B("sm", c, 48, 24 + 8 * j, 32 + 8 * j), B("dl", c, 16, 8 * j, 8 * j + 8), B("oh", c, W, 15, W, 18, k=j), A.mult)
+                tt(B("sm", c, 48, 40, 48), B("sm", c, 48, 24, 32), B("sm", c, 48, 32, 40), A.add)
+                tt(row0, row0, B("sm", c, 48, 40, 48), A.add)
+            scan(B("m3", c, W), SEG, K3, A.mult, A.max)
+            tt(nn, K3, B("m3", c, W), A.is_lt)
+            scan(SO(c, 3), nn, ck, A.mult, A.max)
+            if n == 1:
+                tt(row0, row0, B("sm", c, 48, 40, 48), A.subtract)
+            offer(n + 1, c)
+    dma("s", "dw", [], [R("wo", 0, 512)], lambda g, T: g.scalar.dma_start(T.yw[:], T.wo[0:8, :]), 2000)
+
+
+def place(res, cost, pre, suc, head, key):
+    left, at, t0, lines = [len(p) for p in pre], list(head), [0.0] * len(res), {}
+    todo = [(key[i], i) for i in range(len(res)) if not left[i]]
+    while todo:
+        x = min(todo)
+        todo.remove(x)
+        i = x[1]
+        S, E = lines.setdefault(res[i], ([], []))
+        t, c, pos = at[i], cost[i], len(S)
+        while pos and E[pos - 1] > t:
+            pos -= 1
+        while pos < len(S) and S[pos] < t + c:
+            t = max(t, E[pos])
+            pos += 1
+        S.insert(pos, t)
+        E.insert(pos, t + c)
+        t0[i] = t
+        for j, l in suc[i]:
+            at[j] = max(at[j], t + c + l)
+            left[j] -= 1
+            if not left[j]:
+                todo.append((key[j], j))
+    return t0
+
+
+def plan(cores, topo):
+    ops, sends, arrive = [], {}, {}
+    for s in range(NS):
+        build(s, cores, topo, ops, sends, arrive)
+    res, cost, st = [(o["s"], o["eng"]) for o in ops], [o["cost"] for o in ops], [o["st"] for o in ops]
+    pre, dn = [[] for _ in ops], {}
+    for o in ops:
+        if o["kind"] == "r":
+            dn[o["id"]] = len(res)
+            res.append((o["s"], "d"))
+            cost.append(o["lat"] - HOP)
+            st.append(o["st"])
+            pre.append([(o["id"], 500.0)])
+    for o in ops:
+        p = pre[o["id"]]
+        for q, w in o["deps"].items():
+            p.append((q, 0.0 if not w else (ops[q]["lat"] if ops[q]["kind"] == "d" else (SAME if ops[q]["eng"] == o["eng"] else CROSS))))
+        for sm_ in o["rw"]:
+            p += [(dn[q["id"]], HOP - 500.0) for q in sends[(o["s"], sm_)]]
+    n = len(res)
+    tail = [o["lat"] if o["kind"] == "d" else 0.0 for o in ops] + [0.0] * (n - len(ops))
+    suc = [[] for _ in res]
+    for i, p in enumerate(pre):
+        for q, l in p:
+            suc[q].append((i, l))
+    b = place(list(range(n)), cost, suc, pre, tail, list(range(n)))
+    rank = [b[i] + cost[i] for i in range(n)]
+    for i in sorted(range(n), key=lambda i: rank[i]):
+        st[i] = min([st[i]] + [st[j] for j, l in suc[i]])
+    best = None
+    for wt in WTS:
+        t0 = place(res, cost, pre, suc, [0.0] * n, [wt * st[i] - rank[i] for i in range(n)])
+        for _ in range(3):
+            b = place(res, cost, suc, pre, tail, [-(t0[i] + cost[i]) for i in range(n)])
+            t0 = place(res, cost, pre, suc, [0.0] * n, [-(b[i] + cost[i]) for i in range(n)])
+            end = max(t0[i] + cost[i] + tail[i] for i in range(n))
+            if best is None or end < best[0]:
+                best = (end, t0)
+    queue, cnt = {}, {}
+    for i in sorted(range(len(ops)), key=lambda i: (best[1][i], i)):
+        ops[i]["t0"] = best[1][i]
+        queue.setdefault(res[i], []).append(i)
+        if ops[i]["kind"] == "c":
+            cnt[res[i]] = cnt.get(res[i], 0) + 1
+            ops[i]["n"] = cnt[res[i]]
+    return ops, queue, arrive, best[0]
+
+
+def rank_program(g, core, T, topo):
+    s = T.rank_of(core)
+    if s is None:
+        return
+    if "p" not in PLAN:
+        PLAN["p"] = plan(list(T.cores), topo)
+    ops, queue, arrive, end = PLAN["p"]
+    eng = {"v": g.vector, "s": g.scalar, "t": g.tensor, "g": g, "y": g.sync}
+    total = {}
+    for e in "ygvst":
+        seen = {}
+        for i in queue.get((s, e), []):
+            o = ops[i]
+            need = {sm_: arrive[(s, sm_)] for sm_ in o["rw"]}
+            for q, w in o["deps"].items():
+                p = ops[q]
+                if w and p["kind"] == "c":
+                    need[CNT[p["eng"]]] = max(need.get(CNT[p["eng"]], 0), p["n"])
+                elif w and p["kind"] == "d":
+                    need[p["sem"]] = 16
+            for sm_, v in sorted(need.items()):
+                if seen.get(sm_, 0) < v:
+                    eng[e].wait_ge(T.sem[sm_], v)
+                    seen[sm_] = v
+            ins = o["fn"](g, T)
+            if o["kind"] == "c":
+                ins.then_inc(T.sem[CNT[e]], 1)
+                total[CNT[e]] = o["n"]
+            elif o["kind"] == "d":
+                ins.then_inc(T.sem[o["sem"]], 16)
+                total[o["sem"]] = 16
+            else:
+                total["loc"] = total.get("loc", 0) + o["loc"]
+    for (q, sm_), v in arrive.items():
+        if q == s:
+            total[sm_] = v
+    for sm_, v in sorted(total.items()):
+        g.wait_ge(T.sem[sm_], v)

@@ -1,42 +1,40 @@
 from concourse.bass import DstId, RemoteDMATransfer
-from concourse.mybir import AluOpType as A, AxisListType, ActivationFunctionType as F
+from concourse.mybir import AluOpType as A, ActivationFunctionType as F
 
 NS, NC, W = 8, 4, 144
-KSL = [8, 10, 10, 10]
+KSL = [10, 10, 10, 10]
 H16 = "float16"
 f32, i32, u16, bf = "float32", "int32", "uint16", "bfloat16"
 SB = {
-    "book": (4096, bf), "handi": (512, i32), "handf": (512, f32), "ldi": (512, i32), "ldf": (512, f32),
-    "phi": (NC * 2048, f32), "xd": (NC * 2048, bf), "ybf": (NC * 256, bf),
+    "book": (4096, bf), "handi": (512, i32), "hp": (512, H16), "ht": (512, H16), "ldi": (32, i32),
+    "phi": (NC * 2048, f32), "xd": (NC * 2048, bf), "ybf": (NC * 128, bf),
     "ck": (NC * W, f32), "cki": (NC * W, i32), "cs": (NC * W, i32), "co": (NC * 128, f32),
     "v1": (NC * 128, f32), "v2": (NC * 128, i32), "v3": (NC * 128, i32), "offa": (NC * 128, u16),
-    "ee": (NC * W, H16), "be": (NC * W, H16), "beat": (NC * W, bf), "mat": (NC * W, bf), "oh": (2 * NC * W, bf),
+    "ee": (NC * 128, H16), "be": (NC * 128, H16), "beat": (NC * 128, bf), "mat": (NC * W, bf), "oh": (2 * NC * W, bf),
     "nn": (NC * W, f32), "m3": (NC * W, f32), "k3": (NC * W, f32), "so": (NC * 576, f32), "isl": (5 * NC * 8, bf),
-    "zz": (NC * 128, f32), "zi": (NC * 16, i32), "zj": (NC * 16, i32), "offy": (NC * 16, u16),
-    "ma": (16 * 16, f32), "la": (4 * 128, f32),
-    "ms": (16 * 144, f32), "lb": (4 * 640, f32), "bc": (16 * 160, f32), "al": (NC * 192, f32), "pl": (NC * 32, f32),
+    "wd": (5 * NC * 16, f32), "zi": (NC * 16, i32), "zj": (NC * 16, i32), "offy": (NC * 16, u16),
+    "ms": (16 * 160, f32), "lb": (4 * 640, f32), "bc": (16 * 160, f32), "al": (NC * 192, f32), "pl": (NC * 32, f32),
     "ci": (NC * 16, i32), "cj": (NC * 16, i32), "cf": (NC * 16, f32), "fd": (NC * 32, f32), "dl": (NC * 16, f32),
-    "sm": (NC * 48, f32), "x0": (NC * W, f32), "x1": (NC * W, f32), "cb": (NC * 128, f32), "dup": (NC * 256, f32),
-    "tr": (NC * 256, f32), "yo": (512, f32), "wo": (512, f32),
-    "ow": (NC * 192, f32), "mi": (NC * 64, i32), "mz": (NC * 64, i32), "mf": (NC * 64, f32), "mn": (NC * 64, f32),
-    "mq": (NC * 64, f32), "rs": (NC * 128, f32), "ri": (16, i32), "wl": (16, i32), "wm": (8, i32), "wf": (8, f32),
-    "tt": (8, f32), "z2": (256, f32), "offs": (8, u16),
-    "ia": (128, i32), "ib": (128, i32), "ic": (W, i32), "idd": (256, i32), "ie": (W, i32), "iff": (128, i32),
-    "ig": (64, i32), "ih": (16, i32), "ij": (16, i32), "ik": (16, i32), "il": (16, i32), "im": (16, i32), "inn": (16, i32),
-    "pi": (8, i32), "pj": (8, i32), "pf": (24, f32), "c0": (W, f32), "c1": (W, f32),
-    "i32": (128, f32), "ibf": (6 * 128, bf), "i16": (3 * 128, H16), "gh": (8, f32), "hh": (16, f32),
-    "r2": (16, f32), "hs": (8, f32), "dm": (128, f32), "prm": (W, f32), "dupm": (256, f32), "kt": (W, f32), "kb": (128, f32),
-    "seg": (W, f32), "ckc": (W, bf), "csc": (W, H16), "rst": (64, f32), "sd": (64, f32), "lst": (128, u16),
+    "sm": (NC * 48, f32), "x0": (NC * W, f32), "x1": (NC * W, f32), "cb": (NC * W, f32), "cc": (NC * W, H16),
+    "tr": (NC * 128, f32), "yo": (512, f32), "wo": (NC * 24, f32),
+    "ow": (64, f32), "mi": (NC * 64, i32), "mz": (NC * 64, i32), "mf": (NC * 64, f32), "mn": (NC * 64, f32),
+    "mq": (NC * 64, f32), "rs": (NC * 64, f32), "ri": (8, i32), "wl": (16, i32), "wm": (4, bf), "xx": (4, f32), "offs": (4, u16),
+    "ia": (128, i32), "ib": (128, i32), "ic": (W, i32), "ie": (W, i32), "iff": (128, i32), "ig": (64, i32), "ih": (16, i32),
+    "ij": (16, i32), "ik": (16, i32), "il": (16, i32), "im": (16, i32), "inn": (16, i32), "io1": (W, i32),
+    "pi": (8, i32), "pj": (16, i32), "pf": (40, f32), "c0": (W, f32), "c1": (W, f32),
+    "i32": (128, f32), "ibf": (5 * 128, bf), "sw": (4 * 128, H16), "gh": (8, f32), "same": (128, bf),
+    "pe": (W, H16), "pb": (W, bf), "pd": (W, H16), "kt": (W, f32), "ktc": (128, f32), "k0": (W, f32), "myc": (16, f32),
+    "seg": (W, f32), "ckc": (W, bf), "one": (128, bf), "cen": (128, bf), "rst": (64, f32), "sd": (64, f32), "lst": (128, u16),
 }
 SCRATCH = {k: ("sbuf", [128, n], d) for k, (n, d) in SB.items()}
 for _b in range(8):
     SCRATCH["ps%d" % _b] = ("psum", [128, 512], f32)
-SEMAPHORES = (["nv", "ns", "nt", "ng", "loc", "dbk0", "dbk1", "dh", "dld", "dw"] + ["dy%d" % c for c in range(NC)]
-              + ["rl%d" % n for n in range(4)] + ["rm%d" % n for n in range(4)] + ["rb%d" % n for n in range(16)]
+SEMAPHORES = (["nv", "ns", "nt", "ng", "loc", "dbk0", "dbk1", "dh0", "dh1", "dld"] + ["dy%d" % c for c in range(NC)]
+              + ["dw%d" % c for c in range(NC)] + ["rl%d" % n for n in range(4)] + ["rb%d" % n for n in range(16)]
               + ["rp%d" % c for c in range(NC)] + ["ra%d" % c for c in range(NC)])
 CNT = {"v": "nv", "s": "ns", "t": "nt", "g": "ng"}
-CY, PCY, GAT, CALL, HOP, ROW, SAME, CROSS = 1.04, 0.52, 1.56, 800, 2000, 35, 60.0, 120.0
-WTS = (2000.0, 2500.0, 3000.0)
+CY, PCY, GAT, CALL, HOP, ROW, SAME, CROSS = 1.04, 0.52, 1.56, 900, 2200, 40, 200.0, 250.0
+WTS = (2000.0, 3000.0, 4000.0)
 PLAN = {}
 
 
@@ -84,7 +82,8 @@ def build(s, cores, topo, ops, sends, arrive):
 
     def op(eng, cost, outs, ins, fn, kind="c", sem=None, lat=0.0):
         o = {"s": s, "eng": eng, "cost": cost, "fn": fn, "kind": kind, "sem": sem, "lat": lat, "deps": {}, "rw": set(),
-             "id": len(ops), "st": stage[0]}
+             "id": len(ops), "st": stage[0], "gat": cost if any(isinstance(r, tuple) and r[0] == "ind" for r in ins) else 0,
+             "out": outs[0] if outs else None}
         rd = []
         for r in ins:
             if isinstance(r, tuple):
@@ -120,7 +119,7 @@ def build(s, cores, topo, ops, sends, arrive):
         n = width(in0)
         if in0[0] == "ind":
             return 60 + n * GAT * CY
-        half = dty(out) in (bf, "float16", u16) and dty(in0) in (bf, "float16", u16)
+        half = dty(out) in (bf, H16, u16) and dty(in0) in (bf, H16, u16)
         return max(64, n * (2 if two else 1) * (0.5 if half else 1)) * CY
 
     def tt(out, a, b, o_):
@@ -139,6 +138,9 @@ def build(s, cores, topo, ops, sends, arrive):
 
     def scan(out, d0, d1, o0, o1):
         op("v", vcost(out, d1), [out], [d0, d1], lambda g, T: g.vector.tensor_tensor_scan(ap(T, out), ap(T, d0), ap(T, d1), 0.0, o0, o1))
+
+    def turn(out, a):
+        op("v", vcost(out, a), [out], [a], lambda g, T: g.vector.transpose(ap(T, out), ap(T, a)))
 
     def mset(out, v):
         op("v", max(64, width(out)) * CY, [out], [], lambda g, T: g.vector.memset(ap(T, out), v))
@@ -195,6 +197,7 @@ def build(s, cores, topo, ops, sends, arrive):
             return g.remote_dma_fused(tl, local_sem=T.sem.loc)
         o = op("g", CALL, [], [p[0] for p in parts], fn, "r", sem, HOP + rows * (ROW + width(parts[0][0]) * 0.2))
         o["loc"] = sum(len(t[3]) for t in final)
+        o["rows"], o["bytes"] = rows, 4 * width(parts[0][0])
         for t in final:
             for q in t[2]:
                 sends.setdefault((q, sem), []).append(o)
@@ -205,7 +208,6 @@ def build(s, cores, topo, ops, sends, arrive):
     for n in range(4):
         for q in others:
             land.append(("lb", 640 * n + 80 * q, 640 * n + 80 * q + 80, "rl%d" % n))
-            land.append(("la", 128 * n + 16 * q, 128 * n + 16 * q + 16, "rm%d" % n))
         for c in range(NC):
             for h in range(2):
                 if own != (c, h):
@@ -217,98 +219,119 @@ def build(s, cores, topo, ops, sends, arrive):
             if (2 * s + j) % NS != s:
                 land.append(("pl", 32 * c + 16 * j, 32 * c + 16 * j + 16, "rp%d" % c))
 
-    dma("y", "dh", [R("handi", 0, 512)], [], lambda g, T: g.sync.dma_start(T.handi[:], T.hand[:]), 2300)
-    dma("s", "dld", [R("ldi", 0, 512)], [], lambda g, T: g.scalar.dma_start(T.ldi[0:8, :], T.ld[:]), 2000)
-    dma("y", "dbk0", [R("book", 0, 2048)], [], lambda g, T: g.sync.dma_start(T.book[:, 0:2048], T.bk[:, 0:2048]), 5500)
-    dma("s", "dbk1", [R("book", 2048, 4096)], [], lambda g, T: g.scalar.dma_start(T.book[:, 2048:4096], T.bk[:, 2048:4096]), 5500)
+    for h, q in enumerate("ys"):
+        eng = lambda g, q=q: g.sync if q == "y" else g.scalar
+        dma(q, "dh%d" % h, [R("handi", 256 * h, 256 * h + 256)], [],
+            lambda g, T, h=h, eng=eng: eng(g).dma_start(T.handi[:, 256 * h:256 * h + 256], T.hand[:, 256 * h:256 * h + 256]), 2300)
+        dma(q, "dbk%d" % h, [R("book", 2048 * h, 2048 * h + 2048)], [],
+            lambda g, T, h=h, eng=eng: eng(g).dma_start(T.book[:, 2048 * h:2048 * h + 2048], T.bk[:, 2048 * h:2048 * h + 2048]), 5500)
+    for c in range(NC):
+        dma("y", "dld", [R("ldi", 8 * c, 8 * c + 8)], [],
+            lambda g, T, c=c: g.sync.dma_start(T.ldi[:, 8 * c:8 * c + 8], T.ld[:, 128 * c:128 * c + 128]), 5500)
+    LD = R("ldi", 0, 32)
     BOOK = R("book", 0, 4096)
 
     def col(k):
         return R("pf", k, k + 1)
     iota(R("pi", 0, 1), [[0, 1]], 0, 1)
     P = R("pi", 0, 1)
-    ts(R("pj", 0, 1), P, 15, A.bitwise_and)
-    ts(R("pj", 1, 2), P, 7, A.bitwise_and)
-    ts(R("pj", 2, 3), P, 3, A.arith_shift_right, 1, A.bitwise_and)
-    ts(R("pj", 3, 4), P, 4, A.arith_shift_right, 1, A.bitwise_and)
-    ts(R("pj", 4, 5), P, 4, A.arith_shift_right)
-    cp(R("pf", 0, 5), R("pj", 0, 5))
-    cp(col(5), P)
-    soff, yoff = (64, 0) if ohf == 0 else (0, 16)
-    ts(col(6), col(4), 18.0, A.mult, 15.0, A.add)
-    tt(col(7), col(6), col(0), A.subtract)
-    ts(col(8), col(1), -80.0, A.mult, col(2), A.add)
-    ts(col(9), col(1), -24.0, A.mult, col(2), A.add)
-    ts(col(10), col(1), 32.0, A.mult, col(2), A.add)
-    ts(col(11), col(3), 16.0, A.mult, col(10), A.add)
-    ts(col(12), col(1), 18.0, A.mult, 16.0, A.add)
-    ts(col(13), col(5), float(yoff - 64 * ohf), A.add)
-    ts(col(14), col(1), -16.0, A.mult, col(2), A.add)
-    mset(col(15), -1.0 / 64)
-    mset(col(16), float(2 ** 18 + s * 2 ** 19))
+    for k, (sh, m) in enumerate(((0, 15), (0, 7), (3, 1), (4, 1), (4, 7), (0, 3), (2, 1), (2, 3), (3, 15))):
+        ts(R("pj", k, k + 1), P, sh, A.arith_shift_right, m, A.bitwise_and)
+    cp(R("pf", 0, 9), R("pj", 0, 9))
+    PB, P8, B3, B4, PG, P4, B2, Q4, PK = [col(k) for k in range(9)]
+    soff, yoff = (0, 16) if ohf == 0 else (64, 0)
+    ts(col(9), B2, 140.0, A.mult, P8, A.add)
+    ts(col(10), P8, 18.0, A.mult, B3, A.add)
+    ts(col(11), P8, 16.0, A.mult, B3, A.add)
+    ts(col(12), P8, -80.0, A.mult, B3, A.add)
+    ts(col(13), P8, -24.0, A.mult, B3, A.add)
+    ts(col(14), P8, 18.0, A.mult, PK, A.add)
+    ts(col(15), PB, float(yoff - 16), A.add)
+    ts(col(16), B4, -1.0, A.mult, 1.0, A.add)
+    ts(col(17), PB, 8.0, A.mult)
+    ts(col(18), P4, 18.0, A.mult, 17.0, A.add)
+    ts(col(19), Q4, 1.0, A.is_equal)
+    ts(col(20), Q4, 2.0, A.is_equal, 430.0, A.mult)
+    tt(col(21), col(18), col(20), A.add)
+    mset(col(22), -1.0 / 64)
+    mset(col(23), 2048.0)
+    ts(col(24), P, 0.0, A.is_equal)
+    ts(col(25), P, 1.0, A.is_equal)
     iota(R("ih", 0, 16), [[1, 16]])
     IH = lambda n: R("ih", 0, n)
-    L_OB, L_Z, L_M0, L_M1, L_L, L_PA, L_PB, L_AP, L_CP, L_OC, L_DUP, L_G, L_OH, L_I = 0, 8, 16, 18, 20, 22, 30, 34, 38, 46, 54, 70, 80, 90
-    ts(R("lst", L_OB, L_OB + 8), IH(8), 0.0, A.mult, col(1), A.add)
-    ts(R("lst", L_Z, L_Z + 8), IH(8), 18.0, A.mult, 15.0, A.add)
-    ts(R("lst", L_M0, L_M0 + 1), col(2), 144.0, A.mult, col(12), A.add)
-    ts(R("lst", L_M1, L_M1 + 1), col(2), 288.0, A.mult, col(12), A.add)
-    ts(R("lst", L_L, L_L + 1), col(12), -1.0, A.add)
+    L_HP, L_L, L_T, L_CO, L_YO, L_S, L_G, L_OH, L_W, L_M, L_K, L_P, L_AP = 0, 8, 16, 24, 32, 40, 50, 60, 70, 72, 80, 84, 88
+    lst = lambda a, n: R("lst", a, a + n)
+    ts(lst(L_HP, 8), IH(8), col(17), A.add)
+    ts(lst(L_L, 8), IH(8), 0.0, A.mult, col(9), A.add)
+    ts(lst(L_T, 8), lst(L_L, 8), 4.0, A.add)
+    ts(lst(L_W, 1), col(9), 12.0, A.add)
     ts(R("ij", 0, 16), IH(16), 2.0, A.mult)
-    ts(R("lst", L_PA, L_PA + 8), R("ij", 0, 8), col(14), A.add, 112.0, A.add)
-    ts(R("lst", L_PB, L_PB + 4), R("ij", 0, 4), col(8), A.add, float(560 + soff), A.add)
-    ts(R("lst", L_AP, L_AP + 4), R("ij", 0, 4), col(9), A.add, 168.0, A.add)
-    ts(R("lst", L_OC, L_OC + 8), R("ij", 0, 8), col(11), A.add)
-    ts(R("ik", 0, 8), IH(8), 18.0, A.mult, 15.0, A.add)
-    ts(R("lst", L_CP, L_CP + 8), R("ik", 0, 8), col(0), A.subtract)
-    iota(R("il", 0, 16), [[16, 8], [0, 2]])
-    ts(R("lst", L_DUP, L_DUP + 16), R("il", 0, 16), col(0), A.add)
-    ts(R("im", 0, 9), IH(9), 16.0, A.mult, col(0), A.add)
+    ts(lst(L_CO, 8), R("ij", 0, 8), col(10), A.add)
+    ts(lst(L_YO, 8), R("ij", 0, 8), col(11), A.add)
+    ts(lst(L_AP, 4), R("ij", 0, 4), col(13), A.add, 168.0, A.add)
+    for par in range(2):
+        ts(col(26 + par), col(19), 144.0 * (1 + par), A.mult, col(21), A.add)
+        for h in range(2):
+            ts(lst(L_M + 4 * par + 2 * h, 1), col(26 + par), 72.0 * h, A.add)
+    iota(R("ik", 0, 4), [[0, 2], [2, 2]], 560 + soff)
+    iota(R("il", 0, 4), [[4, 2], [2, 2]], 564 + soff)
+    ts(lst(L_K, 4), R("ik", 0, 4), col(12), A.add)
+    ts(lst(L_P, 4), R("il", 0, 4), col(12), A.add)
+    ts(R("im", 0, 9), IH(9), 16.0, A.mult, PB, A.add)
     ts(R("inn", 0, 9), R("im", 0, 9), 3641.0, A.mult)
     ts(R("im", 0, 9), R("inn", 0, 9), 16, A.arith_shift_right)
-    cp(R("lst", L_G, L_G + 9), R("im", 0, 9))
-    ts(R("lst", L_OH, L_OH + 9), R("im", 0, 9), 18.0, A.mult, 16.0, A.add)
-    cp(R("lst", L_I, L_I + 8), IH(8))
+    cp(lst(L_G, 9), R("im", 0, 9))
+    ts(lst(L_OH, 9), R("im", 0, 9), 18.0, A.mult, 17.0, A.add)
+    ts(R("inn", 0, 9), R("im", 0, 9), 4.0, A.is_ge, 140.0, A.mult)
+    tt(R("ij", 0, 9), R("inn", 0, 9), R("im", 0, 9), A.add)
+    ts(lst(L_S, 9), R("ij", 0, 9), 8.0, A.add)
     iota(R("ia", 0, 128), [[-1, 128]], 0, 1)
     IA = R("ia", 0, 128)
     I32 = R("i32", 0, 128)
     ts(I32, IA, 0.0, A.is_equal)
-    IB = [R("ibf", 128 * k, 128 * k + 128) for k in range(6)]
-    for k, w in enumerate((1.0, -1.0, 2.0 ** 18, 2.0 ** 20, -2.0 ** 21, 2.0 ** 23)):
+    IB = [R("ibf", 128 * k, 128 * k + 128) for k in range(5)]
+    for k, w in enumerate((1.0, -1.0, 2.0 ** 18, -2.0 ** 19, 2.0 ** 22)):
         ts(IB[k], IA, 0.0, A.is_equal, w, A.mult)
-    IH16 = [R("i16", 128 * k, 128 * k + 128) for k in range(3)]
-    for k, w in enumerate((1.0, 64.0, -128.0)):
-        ts(IH16[k], IA, 0.0, A.is_equal, w, A.mult)
+    SW = {}
+    for a in range(2):
+        for b in range(2):
+            SW[a, b] = R("sw", 128 * (2 * a + b), 128 * (2 * a + b) + 128)
+            ts(SW[a, b], IA, 16.0 * (a - b), A.is_equal, B4 if a else col(16), A.mult)
     GH = R("gh", 0, 8)
-    ts(GH, IH(8), col(4), A.is_equal)
-    ts(R("hs", 0, 4), R("gh", 4 * ohf, 4 * ohf + 4), 80.0, A.mult)
-    ts(R("hs", 4, 8), R("gh", 4 * ohf, 4 * ohf + 4), col(13), A.mult)
+    ts(GH, IH(8), PG, A.is_equal)
     iota(R("ib", 0, 128), [[0, 8], [1, 16]])
-    DM = R("dm", 0, 128)
-    ts(DM, R("ib", 0, 128), col(0), A.is_equal)
-    if ohf == 0:
-        cp(R("hh", 0, 8), GH)
-        ts(R("hh", 8, 16), GH, 2048.0, A.mult)
-        ts(R("r2", 0, 8), GH, 32.0, A.mult)
+    ts(R("same", 0, 128), R("ib", 0, 128), PB, A.is_equal, 416.0, A.mult)
     iota(R("ic", 0, W), [[1, W]])
-    ts(R("prm", 0, W), R("ic", 0, W), col(7), A.is_equal)
+    for b, w in (("pe", 16.0), ("pb", 65536.0), ("pd", -32.0)):
+        ts(R(b, 0, W), R("ic", 0, W), col(14), A.is_equal, w, A.mult)
     iota(R("ie", 0, W), [[0, 8], [1, 18]])
+    iota(R("io1", 0, W), [[0, 2], [16, 4], [-1, 18]], 16 * (5 * s + 1) + 15)
     IE = R("ie", 0, W)
-    ts(R("c0", 0, W), IE, -4096.0, A.mult, 61440.0, A.add)
     ts(R("c1", 0, W), IE, 16.0, A.is_lt)
-    ts(R("kt", 0, W), R("c0", 0, W), 0.0, A.max)
+    ts(R("c0", 0, W), R("io1", 0, W), 4096.0, A.mult, 2048.0, A.add)
+    tt(R("kt", 0, W), R("c0", 0, W), R("c1", 0, W), A.mult)
+    iota(R("iff", 0, 128), [[-1, 16], [0, 2], [16, 4]], 16 * (5 * s + 1) + 15)
+    ts(R("ktc", 0, 128), R("iff", 0, 128), 4096.0, A.mult, 2048.0, A.add)
     SEG = R("seg", 0, W)
     ts(SEG, IE, 1.0, A.min)
-    ts(R("ckc", 0, W), R("c1", 0, W), 2.0 ** 21, A.mult, 2.0 ** 17, A.add)
-    ts(R("csc", 0, W), R("c1", 0, W), 15.0, A.mult, -2048.0, A.add)
+    ts(R("c0", 0, W), IE, -1.0, A.mult, float(2 ** 19 + 65536 + 15), A.add)
+    tt(R("k0", 0, W), R("c0", 0, W), R("c1", 0, W), A.mult)
+    ts(R("c0", 0, W), IE, -1.0, A.mult, -113.0, A.add)
+    ts(R("x0", 0, W), R("c0", 0, W), col(25), A.mult)
+    ts(R("x1", 0, W), col(24) and R("c1", 0, W), 622592.0, A.mult, col(24), A.mult)
+    tt(R("c0", 0, W), R("x0", 0, W), R("c1", 0, W), A.mult)
+    ts(R("x0", 0, W), IE, 16.0, A.is_equal, 65280.0, A.mult)
+    ts(R("m3", 0, W), R("x0", 0, W), col(24), A.mult)
+    tt(R("nn", 0, W), R("c0", 0, W), R("x1", 0, W), A.add)
+    tt(R("ckc", 0, W), R("nn", 0, W), R("m3", 0, W), A.add)
+    mset(R("one", 0, 128), 1.0)
+    mset(R("cen", 0, 128), -2040.0)
     iota(R("ig", 0, 64), [[0, 8], [1, 8]])
     ts(R("rst", 0, 64), R("ig", 0, 64), 0.0, A.is_equal, 65536.0, A.mult)
-    ts(R("sd", 0, 64), R("ig", 0, 64), -1.0, A.mult, 7.0, A.add)
-    iota(R("idd", 0, 256), [[16, 8], [0, 2], [1, 16]], 0, -1)
-    ts(R("dupm", 0, 256), R("idd", 0, 256), 0.0, A.is_equal)
-    iota(R("iff", 0, 128), [[0, 8], [4096, 16]])
-    cp(R("kb", 0, 128), R("iff", 0, 128))
-    cp(R("ldf", 0, 512, 1, 8), R("ldi", 0, 512, 1, 8))
+    ts(R("sd", 0, 64), R("ig", 0, 64), -5.0, A.mult, float(35 - 5 * s + 64), A.add)
+    iota(R("ik", 8, 16), [[0, 2], [1, 4]], 5 * s + 1 - 64)
+    cp(R("myc", 0, 8), R("ik", 8, 16))
+    cp(R("myc", 8, 16), R("ik", 8, 16))
 
     def B(b, c, n, a=0, e=None, st=1, k=0):
         return R(b, (k * NC + c) * n + a, (k * NC + c) * n + (n if e is None else e), st)
@@ -319,78 +342,55 @@ def build(s, cores, topo, ops, sends, arrive):
     def SO(c, j, a=0, e=W, st=1):
         return B("so", c, 576, W * j + a, W * j + e, st)
 
-    def suits(c):
+    def derive(c):
+        tt(B("co", c, 128), ind(B("ck", c, W), L_CO, 8), R("ktc", 0, 128), A.subtract)
         cp(B("cki", c, W), B("ck", c, W))
         ts(B("cs", c, W), B("cki", c, W), 3, A.bitwise_and)
 
-    def to_o(c, src):
-        op("v", 256 * CY, [B("tr", c, 256)], [src], lambda g, T: g.vector.transpose(ap(T, B("tr", c, 256)), ap(T, src)))
-        ts(B("co", c, 128), ind(B("tr", c, 256), L_OC, 8), -2048.0, A.add)
-
     def pick(c, src):
         cp(B("mi", c, 64), src)
-        ts(B("mz", c, 64), B("mi", c, 64), 6, A.arith_shift_right, 8191, A.bitwise_and)
+        ts(B("mz", c, 64), B("mi", c, 64), 4, A.arith_shift_right, 8191, A.bitwise_and)
         cp(B("mf", c, 64), B("mz", c, 64))
         scan(B("mn", c, 64), R("rst", 0, 64), B("mf", c, 64), A.add, A.min)
         tt(B("mq", c, 64), B("mf", c, 64), B("mn", c, 64), A.is_gt)
 
-    def play(n, c):
-        dst = R("la", 128 * n + 16 * s, 128 * n + 16 * s + 16)
-        src = dst if c == oc else B("ma", c, 16, k=n)
-        act(src, ind(B("so", c, 576, 0, 432), L_M1 if n % 2 == 0 else L_M0, 1), F.Identity, col(16))
-        send([(src, dst, [q for q in pairs[c] if q != s])], "rm%d" % n)
-        if c != oc:
-            return
-        act(R("ow", 0, 128), ind(R("la", 128 * n, 128 * n + 128), L_PA, 8))
-        pick(0, R("ow", 0, 64))
-        scan(R("rs", 0, 64), R("mq", 0, 64), R("ow", 64, 128), A.mult, A.max)
-        cp(R("ri", 0, 8), R("rs", 7, 64, 8))
-        ts(R("wl", 8, 16), R("ri", 0, 8), 19, A.arith_shift_right)
-        tt(R("z2", 0, 128), ind(R("wl", 8, 16), L_I, 8), DM, A.mult)
-        mm(R("ps7", 0, 4), R("z2", 0, 128), R("hs", 0, 4), True, False)
-        mm(R("ps7", 0, 4), DM, R("hs", 4, 8), False, True)
-        cp(R("offs", 0, 4), R("ps7", 0, 4))
-        if ohf == 0:
-            ts(R("wm", 0, 8), R("ri", 0, 8), 255, A.bitwise_and)
-            cp(R("wf", 0, 8), R("wm", 0, 8))
-            op("v", 64 * CY, [R("tt", 0, 1)], [R("wf", 0, 8)],
-               lambda g, T: g.vector.tensor_reduce(T.tt[:, 0:1], T.wf[:, 0:8], AxisListType.X, A.add))
-            ts(R("tt", 1, 2), R("tt", 0, 1), 416.0, A.mult, float(65536 - 2 ** 23), A.add)
-            ts(R("r2", 8, 16), GH, R("tt", 1, 2), A.mult)
-
     def offer(n, c):
-        m, b0 = 144 * (4 * n + c), 160 * (4 * n + c)
-        act(R("ms", m + 64, m + 80), ind(SO(c, 3), L_L, 1), F.Identity, col(16))
-        tt(B("zz", c, 128), ind(SO(c, 3), L_Z, 8), DM, A.mult)
-        mm(PS(c, 432, 440), B("zz", c, 128), GH, True, True)
-        cp(B("zi", c, 16, 0, 8), PS(c, 432, 440))
+        m = 160 * (4 * n + c)
+        cp(B("zi", c, 16, 0, 8), SO(c, 3, 15, W, 18))
         ts(B("zj", c, 16, 0, 8), B("zi", c, 16, 0, 8), 4095, A.bitwise_and)
         cp(B("offy", c, 16, 0, 8), B("zj", c, 16, 0, 8))
         for h in range(2):
-            act(R("ms", m + 80 * h, m + 80 * h + 64), ("ind", BOOK, B("offy", c, 16, 4 * h, 4 * h + 4)))
+            act(R("ms", m + 144 * h, m + 144 * h + 16), ind(B("so", c, 576), L_M + 4 * ((n + 1) % 2) + 2 * h, 1))
+        act(R("ms", m + 16, m + 144), ("ind", BOOK, B("offy", c, 16, 0, 8)))
         dst = R("lb", 640 * n + 80 * s, 640 * n + 80 * s + 80)
-        send([(R("ms", m + 64 * h, m + 64 * h + 80), dst, [pairs[c][h]]) for h in range(2) if pairs[c][h] != s], "rl%d" % n)
+        send([(R("ms", m + 80 * h, m + 80 * h + 80), dst, [pairs[c][h]]) for h in range(2) if pairs[c][h] != s], "rl%d" % n)
         if c != oc:
             return
-        act(dst, R("ms", m + 64 * ohf, m + 64 * ohf + 80))
+        act(dst, R("ms", m + 80 * ohf, m + 80 * ohf + 80))
         lb = R("lb", 640 * n, 640 * n + 640)
-        act(R("ow", 128, 192), ind(lb, L_PB, 4))
-        act(R("bc", b0 + 16 + 64 * ohf, b0 + 80 + 64 * ohf), ("ind", lb, R("offs", 0, 4)))
-        scan(R("rs", 64, 128), R("mq", 0, 64), R("ow", 128, 192), A.mult, A.max)
-        cp(R("ri", 8, 16), R("rs", 71, 128, 8))
-        ts(R("wl", 0, 8), R("ri", 8, 16), 4095 if ohf == 0 else 3, A.bitwise_and)
-        if ohf == 0:
-            tt(R("z2", 128, 256), ind(R("wl", 0, 8), L_I, 8), DM, A.mult)
-            mm(R("ps7", 16, 32), DM, R("r2", 0, 16), True, False)
-            mm(R("ps7", 16, 32), R("z2", 128, 256), R("hh", 0, 16), False, True)
-            cp(R("bc", b0, b0 + 16), R("ps7", 16, 32))
-        else:
-            cp(R("bc", b0 + 144, b0 + 160), R("wl", 0, 16))
-        src = R("bc", b0 + 80 * ohf, b0 + 80 * ohf + 80)
+        sm = m + 144 * ohf
+        act(R("ow", 0, 64), ind(lb, L_P, 4))
+        pick(0, ind(lb, L_K, 4))
+        scan(R("rs", 0, 64), R("mq", 0, 64), R("ow", 0, 64), A.mult, A.max)
+        cp(R("ri", 0, 8), R("rs", 7, 64, 8))
+        ts(R("wl", 12, 16), R("ri", 4, 8), 16, A.arith_shift_right)
+        ts(R("offs", 0, 4), R("wl", 12, 16), 16.0, A.mult, col(15), A.add)
+        act(R("bc", m + 16 + 64 * ohf, m + 80 + 64 * ohf), ("ind", lb, R("offs", 0, 4)))
+        ts(R("wl", 0, 4), R("ri", 4, 8), 4095, A.bitwise_and)
+        ts(R("wl", 8, 12), R("ri", 4, 8), 3, A.bitwise_and)
+        ts(R("bc", sm, sm + 4), R("wl", 0, 4), 32.0, A.add)
+        cp(R("bc", sm + 8, sm + 16), R("wl", 8, 16))
+        ts(R("xx", 0, 4) if n else R("bc", sm + 4, sm + 8), R("wl", 0, 4), 2048.0, A.mult, float(65536 - 2 ** 23), A.add)
+        if n:
+            ts(R("wl", 4, 8), R("ri", 0, 4), 255, A.bitwise_and)
+            cp(R("wm", 0, 4), R("wl", 4, 8))
+            mm(R("ps7", 0, 4), R("same", 0, 128), R("wm", 0, 4), True, True)
+            tt(R("bc", sm + 4, sm + 8), R("ps7", 0, 4), R("xx", 0, 4), A.add)
+        src = R("bc", m + 80 * ohf, m + 80 * ohf + 80)
         send([(src, src, others)], "rb%d" % (4 * n + c))
 
     def cards(c, dst):
-        cp(B("ci", c, 16), SO(c, 1, 16, 2 * W, 18))
+        cp(B("ci", c, 16), SO(c, 1, 17, 2 * W, 18))
         ts(B("cj", c, 16), B("ci", c, 16), 4095, A.bitwise_and)
         cp(dst, B("cj", c, 16))
 
@@ -407,31 +407,31 @@ def build(s, cores, topo, ops, sends, arrive):
 
     order = A.is_le if s < NS // 2 else A.is_gt
 
-    def redeal(c, w0, w1):
+    def redeal(c, w0, w1, out, old):
         tt(B("sm", c, 48, 0, 8), w0, w1, order)
         deltas(c, B("sm", c, 48, 0, 8))
         for j, x in enumerate(("x0", "x1")):
             tt(B(x, c, W), ind(B("dl", c, 16, 8 * j, 8 * j + 8), L_G, 9), B("oh", c, W, k=j), A.mult)
-            mm(PS(c, 256, 256 + W), I32, B(x, c, W), j == 0, j == 1)
-        tt(B("ck", c, W), PS(c, 256, 256 + W), B("ck", c, W), A.add)
-        tt(B("cb", c, 128), ind(B("ck", c, W), L_CP, 8), R("kb", 0, 128), A.subtract)
+            mm(PS(c, 2 * W, 3 * W), I32, B(x, c, W), j == 0, j == 1)
+        tt(out, PS(c, 2 * W, 3 * W), old, A.add)
 
     for c in range(NC):
         stage[0] = c
-        hf = R("handf", 128 * c, 128 * c + 128)
-        cp(hf, R("handi", 128 * c, 128 * c + 128))
+        ts(B("hp", c, 128), ind(B("handi", c, 128), L_HP, 8), -2048.0, A.add)
+        turn(B("ht", c, 128), B("hp", c, 128))
         mset(B("so", c, 576), 0.0)
-        mm(PS(c, 0, W), hf, R("prm", 0, W), True, True)
-        mm(PS(c, W, W + 8), R("ldf", 128 * c, 128 * c + 128, 1, 8), R("i32", 0, 8, 1, 8), True, True)
-        tt(B("ck", c, W), PS(c, 0, W), R("kt", 0, W), A.add)
-        ts(SO(c, 0, 16, W, 18), PS(c, W, W + 8), float(s), A.not_equal, 960.0, A.mult)
-        cp(SO(c, 3, 15, W, 18), B("ck", c, W, 15, W, 18))
-        play(0, c)
+        mm(PS(c, W, 2 * W), I32, R("kt", 0, W), True, False)
+        for n in range(8):
+            for g_ in range(2):
+                mm(PS(c, W + 18 * n, W + 18 * n + 16), SW[n % 2, g_], B("ht", c, 128, 32 * (n // 2) + 16 * g_, 32 * (n // 2) + 16 * g_ + 16),
+                   False, n == 7 and g_ == 1)
+        act(B("ck", c, W), PS(c, W, 2 * W))
+        op("v", 64 * CY, [SO(c, 0, 17, W, 18)], [LD],
+           lambda g, T, c=c: g.vector.tensor_scalar(ap(T, SO(c, 0, 17, W, 18)), T.ldi[:, 8 * c:8 * c + 8], float(s), 16.0, A.not_equal, A.mult))
+        cp(SO(c, 3, 15, W, 18), B("ck", c, W, 0, W, 18))
         offer(0, c)
         stage[0] = 4 + c
-        suits(c)
-        cp(B("dup", c, 256), ind(hf, L_DUP, 16))
-        to_o(c, B("dup", c, 256))
+        derive(c)
 
     MAG = 1.5 * 2.0 ** 23
     dbank = [0]
@@ -440,27 +440,25 @@ def build(s, cores, topo, ops, sends, arrive):
         for c in range(NC):
             stage[0] = 4 + 4 * n + c
             m = 160 * (4 * n + c)
-            win = R("bc", m + 152, m + 160)
+            bc, y = R("bc", m, m + 160), R("bc", m + 16, m + 144)
+            wd = lambda k: B("wd", c, 16, 0, 8, k=k)
             isl = B("isl", c, 8, k=n)
-            ts(isl, win, float(s), A.is_equal)
+            tt(B("wd", c, 16, k=n), ind(bc, L_W, 1), R("myc", 0, 16), A.subtract)
+            ts(isl, wd(n), 64.0, A.is_equal)
             if n == 2:
-                redeal(c, R("bc", m - 640 + 152, m - 640 + 160), win)
-                mm(PS(c, 0, 256), B("cb", c, 128), R("dupm", 0, 256), True, True)
-                to_o(c, PS(c, 0, 256))
-                suits(c)
+                redeal(c, wd(1), wd(2), B("ck", c, W), B("ck", c, W))
+                derive(c)
             tt(B("ck", c, W, 16, W, 18), isl, SO(c, 3, 15, W, 18), A.mult)
-            tt(B("v1", c, 128), ind(R("bc", m, m + 8), L_OB, 8), B("co", c, 128), A.mult)
-            tt(B("v2", c, 128), ind(R("bc", m + 8, m + 16), L_OB, 8), B("v1", c, 128), A.add)
+            tt(B("v1", c, 128), ind(bc, L_L, 8), B("co", c, 128), A.mult)
+            tt(B("v2", c, 128), ind(bc, L_T, 8), B("v1", c, 128), A.add)
             ts(B("v3", c, 128), B("v2", c, 128), 5, A.arith_shift_right, 4095, A.bitwise_and)
             cp(B("offa", c, 128), B("v3", c, 128))
-            act(B("ybf", c, 256, 0, 128), R("bc", m + 16, m + 144))
-            cp(B("ybf", c, 256, 128, 256), B("ybf", c, 256, 0, 128))
-            tt(B("mat", c, W), ind(R("bc", m + 144, m + 152), L_G, 9), B("cs", c, W), A.is_equal)
-            mm(PS(c, 0, W), IH16[0], R("csc", 0, W), True, False)
+            act(B("ybf", c, 128), y)
+            tt(B("mat", c, W), ind(bc, L_S, 9), B("cs", c, W), A.is_equal)
             us = [(k, min(k + 4, KS), True) for k in range(0, KS, 4)]
             uv = [(k, min(k + 4, 16), False) for k in range(KS, 16, 4)]
             units = us[:1] + uv[:1] + us[1:2] + uv[1:] + us[2:]
-            for iu, (k0, k1, onS) in enumerate(units):
+            for (k0, k1, onS) in units:
                 xd = lambda a, e: B("xd", c, 2048, 128 * a, 128 * e)
                 off = lambda a, e: ("ind", BOOK, B("offa", c, 128, 8 * a, 8 * e))
                 ph = B("phi", c, 2048, 128 * k0, 128 * k1)
@@ -469,36 +467,37 @@ def build(s, cores, topo, ops, sends, arrive):
                     dbank[0] = (dbank[0] + 1) % 3
                     act(xd(k0, k1), off(k0, k1))
                     mm(R(d, 0, 128 * (k1 - k0)), IB[0], xd(k0, k1), True, False)
-                    for k in range(k0, k1, 2):
-                        e = min(k + 2, k1)
-                        mm(R(d, 128 * (k - k0), 128 * (e - k0)), IB[1], B("ybf", c, 256, 0, 128 * (e - k)), False, e == k1)
-                    act(ph, R(d, 0, 128 * (k1 - k0)), F.Abs, col(15))
+                    for k in range(k0, k1):
+                        mm(R(d, 128 * (k - k0), 128 * (k + 1 - k0)), IB[1], B("ybf", c, 128), False, k + 1 == k1)
+                    act(ph, R(d, 0, 128 * (k1 - k0)), F.Abs, col(22))
                 else:
-                    for k in range(k0, k1, 2):
-                        e = min(k + 2, k1)
-                        tt(xd(k, e), off(k, e), B("ybf", c, 256, 0, 128 * (e - k)), A.subtract)
-                    act(ph, xd(k0, k1), F.Abs, col(15))
-                for k in range(k0, k1):
-                    mm(PS(c, 15 - k, W, 18), B("phi", c, 2048, 128 * k, 128 * k + 128), GH, False, iu == len(units) - 1 and k == k1 - 1)
-            ee, beat, ck, nn = B("ee", c, W), B("beat", c, W), B("ck", c, W), B("nn", c, W)
-            ts(ee, PS(c, 0, W), MAG, A.add, MAG, A.subtract)
-            tt(beat, PS(c, 0, W), ee, A.is_lt)
-            tt(B("be", c, W), beat, ee, A.mult)
+                    for k in range(k0, k1):
+                        tt(xd(k, k + 1), off(k, k + 1), y, A.subtract)
+                    act(ph, xd(k0, k1), F.Abs, col(22))
+            P1 = PS(c, 0, 128)
+            mm(P1, IB[0], R("cen", 0, 128), True, False)
+            for b in range(16):
+                mm(PS(c, b, 128, 16), B("phi", c, 2048, b, 2048, 16), GH, False, b == 15)
+            ee, beat, ck, nn = B("ee", c, 128), B("beat", c, 128), B("ck", c, W), B("nn", c, W)
+            ts(ee, P1, MAG, A.add, MAG, A.subtract)
+            tt(beat, P1, ee, A.is_lt)
+            tt(B("be", c, 128), beat, ee, A.mult)
             K = PS(c, W, 2 * W)
-            mm(K, IB[0], R("ckc", 0, W), True, False)
-            mm(K, IB[3], B("mat", c, W), False, False)
-            mm(PS(c, W + 16, 2 * W, 18), IB[5], isl, False, False)
+            const = lambda k: mm(k, R("one", 0, 128, 1, 2), R("ckc", 0, W, 1, 2), True, False)
+            const(K)
+            mm(K, IB[2], B("mat", c, W), False, False)
+            mm(PS(c, W + 16, 2 * W, 18), IB[4], isl, False, False)
             if n % 2:
-                mm(K, IB[4], B("oh", c, W, k=0), False, False)
-            mm(K, IH16[1], ee, False, False)
-            mm(K, IB[2], beat, False, False)
-            mm(K, IH16[2], B("be", c, W), False, True)
+                mm(K, IB[3], B("oh", c, W, k=0), False, False)
+            mm(K, ee, R("pe", 0, W), False, False)
+            mm(K, beat, R("pb", 0, W), False, False)
+            mm(K, B("be", c, 128), R("pd", 0, W), False, True)
             scan(SO(c, 0), SEG, K, A.mult, A.max)
             tt(nn, K, SO(c, 0), A.is_lt)
             scan(SO(c, 1 + n % 2), nn, ck, A.mult, A.max)
             if n == 3:
                 a0 = 192 * c + 24 * s
-                ts(R("al", a0, a0 + 8), SO(c, 0, 16, W, 18), float(2 ** 18), A.add)
+                cp(R("al", a0, a0 + 8), SO(c, 0, 17, W, 18))
                 cards(c, R("al", a0 + 8, a0 + 24))
                 send([(R("al", a0, a0 + 24), R("al", a0, a0 + 24), others)], "ra%d" % c)
             if n == 1:
@@ -509,42 +508,48 @@ def build(s, cores, topo, ops, sends, arrive):
                 send([(cf, dst, [q for q in to if q != s])], "rp%d" % c)
                 if s in to:
                     cp(dst, cf)
-            if n < 3:
-                play(n + 1, c)
             oh = B("oh", c, W, k=n % 2)
             tt(oh, ind(SO(c, 1 + n % 2), L_OH, 9), ck, A.is_equal)
             if n == 3:
+                wo = lambda k: B("wo", c, 24, 8 * k, 8 * k + 8)
+                tt(wo(0), B("isl", c, 8, k=1), B("isl", c, 8, k=2), A.add)
+                tt(wo(1), wo(0), isl, A.add)
+                tt(B("cb", c, W), ck, R("kt", 0, W), A.subtract)
                 u = [192 * c + 24 * ((2 * s + j) % NS) + 8 for j in range(2)]
                 diffs(c, ("al", a0 + 8), [("al", x) for x in u])
-                act(B("ow", c, 192, 0, 64), ind(B("al", c, 192), L_AP, 4))
-                pick(c, B("ow", c, 192, 0, 64))
-                scan(B("rs", c, 128, 0, 64), B("mq", c, 64), R("sd", 0, 64), A.mult, A.max)
-                w1 = B("rs", c, 128, 7, 64, 8)
-                redeal(c, win, w1)
-                ts(B("isl", c, 8, k=4), w1, float(s), A.is_equal)
-                mm(PS(c, 0, 128), B("cb", c, 128), I32, True, True)
-                for k in range(1, 5):
-                    mm(PS(c, 128, 256, 1, 8), B("isl", c, 8, k=k), IB[0], k == 1, k == 4)
-                act(B("yo", c, 128), PS(c, 0, 128))
-                act(R("wo", 128 * c, 128 * c + 128, 1, 8), PS(c, 128, 256, 1, 8))
+                pick(c, ind(B("al", c, 192), L_AP, 4))
+                scan(B("rs", c, 64), B("mq", c, 64), R("sd", 0, 64), A.mult, A.max)
+                w1 = B("rs", c, 64, 7, 64, 8)
+                ts(B("isl", c, 8, k=4), w1, 64.0, A.is_equal)
+                tt(wo(2), wo(1), B("isl", c, 8, k=4), A.add)
+                dma("y", "dw%d" % c, [], [wo(2)],
+                    lambda g, T, c=c: g.sync.dma_start(T.yw[:, 128 * c:128 * c + 128], T.wo[:, 24 * c + 16:24 * c + 24]), 2000)
+                mset(B("cb", c, W, 16, W, 18), 0.0)
+                redeal(c, wd(3), w1, B("cc", c, W), B("cb", c, W))
+                for k in range(8):
+                    for v in range(2):
+                        a = 18 * (2 * (k // 2) + v)
+                        mm(PS(c, 16 * k, 16 * k + 16), SW[k % 2, v], B("cc", c, W, a, a + 16), v == 0, v == 1)
+                turn(B("tr", c, 128), P1)
+                act(B("yo", c, 128), ind(B("tr", c, 128), L_YO, 8), F.Identity, col(23))
                 dma("y", "dy%d" % c, [], [B("yo", c, 128)],
                     lambda g, T, c=c: g.sync.dma_start(T.yc[:, 128 * c:128 * c + 128], T.yo[:, 128 * c:128 * c + 128]), 2000)
                 continue
             K3 = PS(c, 2 * W, 3 * W)
-            mm(K3, IB[0], R("ckc", 0, W), True, False)
-            mm(K3, IH16[1], ee, False, False)
+            const(K3)
+            mm(K3, ee, R("pe", 0, W), False, False)
             if n == 1:
-                mm(K3, IB[4], B("oh", c, W, k=0), False, False)
-            mm(K3, IB[4], oh, False, True)
-            row0 = B("ck", c, W, 15, W, 18)
+                mm(K3, IB[3], B("oh", c, W, k=0), False, False)
+            mm(K3, IB[3], oh, False, True)
+            row0 = B("ck", c, W, 0, W, 18)
             if n == 1:
-                ts(B("k3", c, W), K3, float(2 ** 21 + 960), A.max)
+                tt(B("k3", c, W), K3, R("k0", 0, W), A.max)
                 K3 = B("k3", c, W)
                 diffs(c, ("cf", 16 * c), [("pl", 32 * c), ("pl", 32 * c + 16)])
-                ts(B("sm", c, 48, 0, 8), win, float(s), order)
+                ts(B("sm", c, 48, 0, 8), wd(1), 64.0, order)
                 deltas(c, B("sm", c, 48, 0, 8))
                 for j in range(2):
-                    tt(B("sm", c, 48, 24 + 8 * j, 32 + 8 * j), B("dl", c, 16, 8 * j, 8 * j + 8), B("oh", c, W, 15, W, 18, k=j), A.mult)
+                    tt(B("sm", c, 48, 24 + 8 * j, 32 + 8 * j), B("dl", c, 16, 8 * j, 8 * j + 8), B("oh", c, W, 0, W, 18, k=j), A.mult)
                 tt(B("sm", c, 48, 40, 48), B("sm", c, 48, 24, 32), B("sm", c, 48, 32, 40), A.add)
                 tt(row0, row0, B("sm", c, 48, 40, 48), A.add)
             scan(B("m3", c, W), SEG, K3, A.mult, A.max)
@@ -553,7 +558,6 @@ def build(s, cores, topo, ops, sends, arrive):
             if n == 1:
                 tt(row0, row0, B("sm", c, 48, 40, 48), A.subtract)
             offer(n + 1, c)
-    dma("s", "dw", [], [R("wo", 0, 512)], lambda g, T: g.scalar.dma_start(T.yw[:], T.wo[0:8, :]), 2000)
 
 
 def place(res, cost, pre, suc, head, key):
@@ -626,7 +630,7 @@ def plan(cores, topo):
         if ops[i]["kind"] == "c":
             cnt[res[i]] = cnt.get(res[i], 0) + 1
             ops[i]["n"] = cnt[res[i]]
-    return ops, queue, arrive, best[0]
+    return ops, queue, arrive, best[0], sends
 
 
 def rank_program(g, core, T, topo):
@@ -635,9 +639,12 @@ def rank_program(g, core, T, topo):
         return
     if "p" not in PLAN:
         PLAN["p"] = plan(list(T.cores), topo)
-    ops, queue, arrive, end = PLAN["p"]
+    ops, queue, arrive, end, sends = PLAN["p"]
     eng = {"v": g.vector, "s": g.scalar, "t": g.tensor, "g": g, "y": g.sync}
-    total = {}
+    total, dmas = {}, {}
+    for o in ops:
+        if o["s"] == s and o["kind"] == "d":
+            dmas[o["sem"]] = dmas.get(o["sem"], 0) + 16
     for e in "ygvst":
         seen = {}
         for i in queue.get((s, e), []):
@@ -648,7 +655,7 @@ def rank_program(g, core, T, topo):
                 if w and p["kind"] == "c":
                     need[CNT[p["eng"]]] = max(need.get(CNT[p["eng"]], 0), p["n"])
                 elif w and p["kind"] == "d":
-                    need[p["sem"]] = 16
+                    need[p["sem"]] = dmas[p["sem"]]
             for sm_, v in sorted(need.items()):
                 if seen.get(sm_, 0) < v:
                     eng[e].wait_ge(T.sem[sm_], v)
@@ -659,9 +666,9 @@ def rank_program(g, core, T, topo):
                 total[CNT[e]] = o["n"]
             elif o["kind"] == "d":
                 ins.then_inc(T.sem[o["sem"]], 16)
-                total[o["sem"]] = 16
             else:
                 total["loc"] = total.get("loc", 0) + o["loc"]
+    total.update(dmas)
     for (q, sm_), v in arrive.items():
         if q == s:
             total[sm_] = v

@@ -2,7 +2,9 @@ from concourse.bass import DstId, RemoteDMATransfer
 from concourse.mybir import AluOpType as A, ActivationFunctionType as F
 
 NS, NC, W = 8, 4, 144
-KSL = [10, 10, 10, 10]
+KSL = [11, 11, 11, 11]
+LAST = 0
+M = 176
 H16 = "float16"
 f32, i32, u16, bf = "float32", "int32", "uint16", "bfloat16"
 SB = {
@@ -12,34 +14,35 @@ SB = {
     "v1": (NC * 128, f32), "v2": (NC * 128, i32), "v3": (NC * 128, i32), "offa": (NC * 128, u16),
     "ee": (NC * 128, H16), "be": (NC * 128, H16), "beat": (NC * 128, bf), "mat": (NC * W, bf), "oh": (2 * NC * W, bf),
     "nn": (NC * W, f32), "m3": (NC * W, f32), "k3": (NC * W, f32), "so": (NC * 576, f32), "isl": (5 * NC * 8, bf),
-    "wd": (5 * NC * 16, f32), "zi": (NC * 16, i32), "zj": (NC * 16, i32), "offy": (NC * 16, u16),
-    "ms": (16 * 160, f32), "lb": (4 * 640, f32), "bc": (16 * 160, f32), "al": (NC * 192, f32), "pl": (NC * 32, f32),
+    "wd": (4 * NC * 8, i32), "zi": (NC * 32, i32), "zj": (NC * 8, i32), "zp": (NC * 48, i32), "offy": (NC * 8, u16),
+    "lb": (16 * NS * M, bf), "pc": (NC * 320, bf), "lt": (NC * 16, f32), "pb3": (NC * 24, bf), "zr": (NC * 192, f32),
+    "ri": (NC * 24, i32), "wl": (NC * 32, i32), "offs": (NC * 8, u16), "al": (NC * 192, f32), "pl": (NC * 32, f32),
     "ci": (NC * 16, i32), "cj": (NC * 16, i32), "cf": (NC * 16, f32), "fd": (NC * 32, f32), "dl": (NC * 16, f32),
     "sm": (NC * 48, f32), "x0": (NC * W, f32), "x1": (NC * W, f32), "cb": (NC * W, f32), "cc": (NC * W, H16),
-    "tr": (NC * 128, f32), "yo": (512, f32), "wo": (NC * 24, f32),
-    "ow": (64, f32), "mi": (NC * 64, i32), "mz": (NC * 64, i32), "mf": (NC * 64, f32), "mn": (NC * 64, f32),
-    "mq": (NC * 64, f32), "rs": (NC * 64, f32), "ri": (8, i32), "wl": (16, i32), "wm": (4, bf), "xx": (4, f32), "offs": (4, u16),
-    "ia": (128, i32), "ib": (128, i32), "ic": (W, i32), "ie": (W, i32), "iff": (128, i32), "ig": (64, i32), "ih": (16, i32),
-    "ij": (16, i32), "ik": (16, i32), "il": (16, i32), "im": (16, i32), "inn": (16, i32), "io1": (W, i32),
-    "pi": (8, i32), "pj": (16, i32), "pf": (40, f32), "c0": (W, f32), "c1": (W, f32),
-    "i32": (128, f32), "ibf": (5 * 128, bf), "sw": (4 * 128, H16), "gh": (8, f32), "same": (128, bf),
-    "pe": (W, H16), "pb": (W, bf), "pd": (W, H16), "kt": (W, f32), "ktc": (128, f32), "k0": (W, f32), "myc": (16, f32),
-    "seg": (W, f32), "ckc": (W, bf), "one": (128, bf), "cen": (128, bf), "rst": (64, f32), "sd": (64, f32), "lst": (128, u16),
+    "tr": (NC * 128, f32), "yo": (512, f32), "wo": (NC * 24, f32), "mi": (NC * 64, i32), "mz": (NC * 64, i32),
+    "mf": (NC * 64, f32), "mn": (NC * 64, f32), "mq": (NC * 64, f32), "rs": (NC * 64, f32),
+    "ia": (128, i32), "ib": (128, i32), "ic": (W, i32), "ie": (W, i32), "iff": (128, i32), "ig": (192, i32), "iz": (128, i32),
+    "ih": (16, i32), "ij": (16, i32), "im": (16, i32), "inn": (16, i32), "pi": (8, i32), "pj": (8, i32), "pf": (24, f32),
+    "c0": (W, f32), "c1": (W, f32), "c2": (W, f32), "c3": (W, f32),
+    "i32": (128, f32), "ibf": (8 * 128, bf), "sw": (4 * 128, H16), "gh": (8, f32), "same": (128, bf),
+    "pe": (W, H16), "pb": (W, bf), "pd": (W, H16), "kt": (W, f32), "ktc": (128, f32), "k0": (W, f32), "myc": (8, f32),
+    "zc": (192, bf), "ltc": (16, bf), "seg": (W, f32), "ckc": (W, bf), "one": (128, bf), "cen": (128, bf),
+    "rst": (192, f32), "sd": (64, f32), "lst": (128, u16),
 }
 SCRATCH = {k: ("sbuf", [128, n], d) for k, (n, d) in SB.items()}
 for _b in range(8):
     SCRATCH["ps%d" % _b] = ("psum", [128, 512], f32)
 SEMAPHORES = (["nv", "ns", "nt", "ng", "loc", "dbk0", "dbk1", "dh0", "dh1", "dld"] + ["dy%d" % c for c in range(NC)]
-              + ["dw%d" % c for c in range(NC)] + ["rl%d" % n for n in range(4)] + ["rb%d" % n for n in range(16)]
+              + ["dw%d" % c for c in range(NC)] + ["rl%d" % n for n in range(4 * NC)]
               + ["rp%d" % c for c in range(NC)] + ["ra%d" % c for c in range(NC)])
 CNT = {"v": "nv", "s": "ns", "t": "nt", "g": "ng"}
-CY, PCY, GAT, CALL, HOP, ROW, SAME, CROSS = 1.04, 0.52, 1.56, 900, 2200, 40, 200.0, 250.0
-WTS = (2000.0, 3000.0, 4000.0)
+CY, PCY, GAT, CALL, HOP, ROW, BYTE, WAIT = 0.95, 0.48, 1.56, 750, 2000, 30, 0.05, 220.0
+WTS, SHAKES = (3000.0, 4000.0, 5000.0, 6000.0, 7000.0), 60
 PLAN = {}
 
 
-def R(b, c0, c1, st=1, p=128):
-    return (b, c0, c1, st, p)
+def R(b, c0, c1, st=1, p=128, p0=0):
+    return (b, c0, c1, st, p, p0)
 
 
 def ap(T, r):
@@ -47,8 +50,8 @@ def ap(T, r):
         return r
     if r[0] == "ind":
         return ap(T, r[1]).indirect(ap(T, r[2]))
-    b, c0, c1, st, p = r
-    return T[b][0:p, c0:c1:st] if st > 1 else T[b][0:p, c0:c1]
+    b, c0, c1, st, p, p0 = r
+    return T[b][p0:p, c0:c1:st] if st > 1 else T[b][p0:p, c0:c1]
 
 
 def width(r):
@@ -64,26 +67,21 @@ def bits(engs):
     return sum(1 << e for e in engs)
 
 
-def owner_pairs(cores, topo):
-    free, pairs = list(range(len(cores))), []
-    while free:
-        a = free.pop(0)
-        good = [b for b in free if topo.same_plane(topo.chip(cores[a]), topo.chip(cores[b])) and topo.die(cores[a]) == topo.die(cores[b])]
-        b = good[0] if good else free[0]
-        free.remove(b)
-        pairs.append((a, b))
-    return pairs
+def meet(r, d):
+    if r[1] >= d[1] or d[0] >= r[2]:
+        return False
+    return r[3] != d[4] or (r[1] - d[0]) % r[3] == 0
 
 
 def build(s, cores, topo, ops, sends, arrive):
     me = cores[s]
-    pairs = owner_pairs(cores, topo)
-    hist, bank, land, stage = {}, {}, [], [99]
+    hist, bank, land, stage, seq = {}, {}, [], [99], [0]
 
     def op(eng, cost, outs, ins, fn, kind="c", sem=None, lat=0.0):
         o = {"s": s, "eng": eng, "cost": cost, "fn": fn, "kind": kind, "sem": sem, "lat": lat, "deps": {}, "rw": set(),
              "id": len(ops), "st": stage[0], "gat": cost if any(isinstance(r, tuple) and r[0] == "ind" for r in ins) else 0,
-             "out": outs[0] if outs else None}
+             "out": outs[0] if outs else None, "k": seq[0]}
+        seq[0] += 1
         rd = []
         for r in ins:
             if isinstance(r, tuple):
@@ -92,15 +90,16 @@ def build(s, cores, topo, ops, sends, arrive):
             for r in rs:
                 b, c0, c1 = r[0], r[1], r[2]
                 for (lb_, l0, l1, sm_) in land:
-                    if lb_ == b and c0 < l1 and l0 < c1:
+                    if lb_ == b and not wr and kind != "r" and c0 < l1 and l0 < c1:
                         o["rw"].add(sm_)
                 keep = []
-                for (d0, d1, w, q) in hist.get(b, []):
-                    if c0 < d1 and d0 < c1 and (w or wr) and q is not o:
+                for d in hist.get(b, []):
+                    d0, d1, w, q, st = d
+                    if (w or wr) and q is not o and meet(r, d):
                         o["deps"][q["id"]] = not (eng == "t" and q["eng"] == "t")
                     if not (wr and r[3] == 1 and c0 <= d0 and d1 <= c1):
-                        keep.append((d0, d1, w, q))
-                keep.append((c0, c1, wr, o))
+                        keep.append(d)
+                keep.append((c0, c1, wr, o, r[3]))
                 hist[b] = keep
                 if b.startswith("ps"):
                     run = bank.setdefault(b, [[], []])
@@ -165,59 +164,40 @@ def build(s, cores, topo, ops, sends, arrive):
     def ind(win, c0, n):
         return ("ind", win, R("lst", c0, c0 + n))
 
-    def send(parts, sem):
+    def send(src, dst, to, sem):
         shared = None
         for q in range(NS):
             if topo.chip(cores[q]) != topo.chip(me):
                 e = topo.engines(me, cores[q])
                 shared = e if shared is None else [x for x in shared if x in e]
-        trs = []
-        for (src, dst, qs) in parts:
-            near = [q for q in qs if topo.chip(cores[q]) == topo.chip(me)]
-            far = [q for q in qs if q not in near]
-            trs += [(src, dst, x, x is near) for x in (near, far) if x]
-        nf = len([t for t in trs if not t[3]])
-        final, kf, rows = [], 0, 0
-        for (src, dst, qs, isnear) in trs:
-            if isnear:
-                e = [x for x in topo.engines(me, cores[qs[0]]) if x not in shared]
-            else:
-                k = len(shared) // nf
-                e = shared[kf * k:(kf + 1) * k]
-                kf += 1
-            final.append((src, dst, qs, e))
-            rows = max(rows, 128 * len(qs) // len(e))
-            for q in qs:
-                arrive[(q, sem)] = arrive.get((q, sem), 0) + len(e)
+        near = [q for q in to if topo.chip(cores[q]) == topo.chip(me)]
+        far = [q for q in to if q not in near]
+        final = [(far, shared)] if far else []
+        if near:
+            final.append((near, [x for x in topo.engines(me, cores[near[0]]) if x not in shared]))
+        rows = max(128 * len(qs) // len(e) for qs, e in final)
 
         def fn(g, T):
             tl = [RemoteDMATransfer(dst_ids=[DstId(rid=topo.addr(cores[q])[0], pnc=topo.addr(cores[q])[1]) for q in qs],
                                     dma_engine_mask=bits(e), remote_sem=T.sem[sem], srcs=[ap(T, src)], dsts=[ap(T, dst) for q in qs])
-                  for (src, dst, qs, e) in final]
+                  for (qs, e) in final]
             return g.remote_dma_fused(tl, local_sem=T.sem.loc)
-        o = op("g", CALL, [], [p[0] for p in parts], fn, "r", sem, HOP + rows * (ROW + width(parts[0][0]) * 0.2))
-        o["loc"] = sum(len(t[3]) for t in final)
-        o["rows"], o["bytes"] = rows, 4 * width(parts[0][0])
-        for t in final:
-            for q in t[2]:
+        nb = width(src) * (2 if dty(src) == bf else 4)
+        o = op("g", CALL, [], [src], fn, "r", sem, HOP + rows * (ROW + nb * BYTE))
+        o["loc"] = sum(len(e) for qs, e in final)
+        o["rows"], o["bytes"] = rows, nb
+        for qs, e in final:
+            for q in qs:
+                arrive[(q, sem)] = arrive.get((q, sem), 0) + len(e)
                 sends.setdefault((q, sem), []).append(o)
 
-    own = [(c, h) for c in range(NC) for h in range(2) if pairs[c][h] == s][0]
-    oc, ohf = own
-    others = [q for q in range(NS) if q != s]
-    for n in range(4):
+    others = [(s + k) % NS for k in range(1, NS)]
+    for k in range(4 * NC):
         for q in others:
-            land.append(("lb", 640 * n + 80 * q, 640 * n + 80 * q + 80, "rl%d" % n))
-        for c in range(NC):
-            for h in range(2):
-                if own != (c, h):
-                    land.append(("bc", 160 * (4 * n + c) + 80 * h, 160 * (4 * n + c) + 80 * h + 80, "rb%d" % (4 * n + c)))
+            land.append(("lb", M * (NS * k + q), M * (NS * k + q) + 168, "rl%d" % k))
     for c in range(NC):
-        for q in others:
-            land.append(("al", 192 * c + 24 * q, 192 * c + 24 * q + 24, "ra%d" % c))
-        for j in range(2):
-            if (2 * s + j) % NS != s:
-                land.append(("pl", 32 * c + 16 * j, 32 * c + 16 * j + 16, "rp%d" % c))
+        land.append(("al", 192 * c, 192 * c + 192, "ra%d" % c))
+        land.append(("pl", 32 * c, 32 * c + 32, "rp%d" % c))
 
     for h, q in enumerate("ys"):
         eng = lambda g, q=q: g.sync if q == "y" else g.scalar
@@ -235,62 +215,51 @@ def build(s, cores, topo, ops, sends, arrive):
         return R("pf", k, k + 1)
     iota(R("pi", 0, 1), [[0, 1]], 0, 1)
     P = R("pi", 0, 1)
-    for k, (sh, m) in enumerate(((0, 15), (0, 7), (3, 1), (4, 1), (4, 7), (0, 3), (2, 1), (2, 3), (3, 15))):
+    for k, (sh, m) in enumerate(((0, 15), (0, 7), (3, 1), (4, 1), (4, 7), (3, 15))):
         ts(R("pj", k, k + 1), P, sh, A.arith_shift_right, m, A.bitwise_and)
-    cp(R("pf", 0, 9), R("pj", 0, 9))
-    PB, P8, B3, B4, PG, P4, B2, Q4, PK = [col(k) for k in range(9)]
-    soff, yoff = (0, 16) if ohf == 0 else (64, 0)
-    ts(col(9), B2, 140.0, A.mult, P8, A.add)
+    cp(R("pf", 0, 6), R("pj", 0, 6))
+    PB, P8, B3, B4, PG, PK = [col(k) for k in range(6)]
     ts(col(10), P8, 18.0, A.mult, B3, A.add)
     ts(col(11), P8, 16.0, A.mult, B3, A.add)
-    ts(col(12), P8, -80.0, A.mult, B3, A.add)
+    ts(col(12), P8, float(M), A.mult, B3, A.add)
     ts(col(13), P8, -24.0, A.mult, B3, A.add)
     ts(col(14), P8, 18.0, A.mult, PK, A.add)
-    ts(col(15), PB, float(yoff - 16), A.add)
     ts(col(16), B4, -1.0, A.mult, 1.0, A.add)
     ts(col(17), PB, 8.0, A.mult)
-    ts(col(18), P4, 18.0, A.mult, 17.0, A.add)
-    ts(col(19), Q4, 1.0, A.is_equal)
-    ts(col(20), Q4, 2.0, A.is_equal, 430.0, A.mult)
-    tt(col(21), col(18), col(20), A.add)
-    mset(col(22), -1.0 / 64)
-    mset(col(23), 2048.0)
-    ts(col(24), P, 0.0, A.is_equal)
-    ts(col(25), P, 1.0, A.is_equal)
+    ts(col(18), P8, 18.0, A.mult, 17.0, A.add)
+    mset(col(19), -1.0 / 64)
+    mset(col(20), 2048.0)
+    ts(col(21), P, 0.0, A.is_equal)
+    ts(col(22), P, 1.0, A.is_equal)
     iota(R("ih", 0, 16), [[1, 16]])
     IH = lambda n: R("ih", 0, n)
-    L_HP, L_L, L_T, L_CO, L_YO, L_S, L_G, L_OH, L_W, L_M, L_K, L_P, L_AP = 0, 8, 16, 24, 32, 40, 50, 60, 70, 72, 80, 84, 88
+    L_HP, L_OB, L_CO, L_YO, L_G, L_OH, L_M, L_AP, L_PC = 0, 8, 16, 24, 32, 42, 52, 56, 60
     lst = lambda a, n: R("lst", a, a + n)
     ts(lst(L_HP, 8), IH(8), col(17), A.add)
-    ts(lst(L_L, 8), IH(8), 0.0, A.mult, col(9), A.add)
-    ts(lst(L_T, 8), lst(L_L, 8), 4.0, A.add)
-    ts(lst(L_W, 1), col(9), 12.0, A.add)
+    ts(lst(L_OB, 8), IH(8), 0.0, A.mult, P8, A.add)
     ts(R("ij", 0, 16), IH(16), 2.0, A.mult)
     ts(lst(L_CO, 8), R("ij", 0, 8), col(10), A.add)
     ts(lst(L_YO, 8), R("ij", 0, 8), col(11), A.add)
     ts(lst(L_AP, 4), R("ij", 0, 4), col(13), A.add, 168.0, A.add)
+    ts(col(15), B3, -1.0, A.mult, 1.0, A.add)
     for par in range(2):
-        ts(col(26 + par), col(19), 144.0 * (1 + par), A.mult, col(21), A.add)
-        for h in range(2):
-            ts(lst(L_M + 4 * par + 2 * h, 1), col(26 + par), 72.0 * h, A.add)
-    iota(R("ik", 0, 4), [[0, 2], [2, 2]], 560 + soff)
-    iota(R("il", 0, 4), [[4, 2], [2, 2]], 564 + soff)
-    ts(lst(L_K, 4), R("ik", 0, 4), col(12), A.add)
-    ts(lst(L_P, 4), R("il", 0, 4), col(12), A.add)
+        ts(lst(L_M + 2 * par, 1), col(15), float(W * (1 + par)), A.mult, col(18), A.add)
+        ts(lst(L_M + 2 * par + 1, 1), col(18), 3.0 * W - 2, A.add)
+    for j in range(168, M):
+        mset(R("lb", j, 16 * NS * M, M), 0.0)
+    for k, a in enumerate((136, 152, 128, 144, 160)):
+        ts(lst(L_PC + 4 * k, 4), R("ij", 0, 4), col(12), A.add, float(a), A.add)
     ts(R("im", 0, 9), IH(9), 16.0, A.mult, PB, A.add)
     ts(R("inn", 0, 9), R("im", 0, 9), 3641.0, A.mult)
     ts(R("im", 0, 9), R("inn", 0, 9), 16, A.arith_shift_right)
     cp(lst(L_G, 9), R("im", 0, 9))
     ts(lst(L_OH, 9), R("im", 0, 9), 18.0, A.mult, 17.0, A.add)
-    ts(R("inn", 0, 9), R("im", 0, 9), 4.0, A.is_ge, 140.0, A.mult)
-    tt(R("ij", 0, 9), R("inn", 0, 9), R("im", 0, 9), A.add)
-    ts(lst(L_S, 9), R("ij", 0, 9), 8.0, A.add)
     iota(R("ia", 0, 128), [[-1, 128]], 0, 1)
     IA = R("ia", 0, 128)
     I32 = R("i32", 0, 128)
     ts(I32, IA, 0.0, A.is_equal)
-    IB = [R("ibf", 128 * k, 128 * k + 128) for k in range(5)]
-    for k, w in enumerate((1.0, -1.0, 2.0 ** 18, -2.0 ** 19, 2.0 ** 22)):
+    IB = [R("ibf", 128 * k, 128 * k + 128) for k in range(8)]
+    for k, w in enumerate((1.0, -1.0, 2.0 ** 18, -2.0 ** 19, 2.0 ** 22, 256.0, 2048.0, 2.0 ** 19)):
         ts(IB[k], IA, 0.0, A.is_equal, w, A.mult)
     SW = {}
     for a in range(2):
@@ -305,39 +274,41 @@ def build(s, cores, topo, ops, sends, arrive):
     for b, w in (("pe", 16.0), ("pb", 65536.0), ("pd", -32.0)):
         ts(R(b, 0, W), R("ic", 0, W), col(14), A.is_equal, w, A.mult)
     iota(R("ie", 0, W), [[0, 8], [1, 18]])
-    iota(R("io1", 0, W), [[0, 2], [16, 4], [-1, 18]], 16 * (5 * s + 1) + 15)
-    IE = R("ie", 0, W)
-    ts(R("c1", 0, W), IE, 16.0, A.is_lt)
-    ts(R("c0", 0, W), R("io1", 0, W), 4096.0, A.mult, 2048.0, A.add)
-    tt(R("kt", 0, W), R("c0", 0, W), R("c1", 0, W), A.mult)
-    iota(R("iff", 0, 128), [[-1, 16], [0, 2], [16, 4]], 16 * (5 * s + 1) + 15)
-    ts(R("ktc", 0, 128), R("iff", 0, 128), 4096.0, A.mult, 2048.0, A.add)
+    IE, C0, C1, C2, C3 = R("ie", 0, W), R("c0", 0, W), R("c1", 0, W), R("c2", 0, W), R("c3", 0, W)
+    ts(C1, IE, 16.0, A.is_lt)
+    ts(C0, IE, -8192.0, A.mult, 31 * 8192.0 + 2048, A.add)
+    tt(R("kt", 0, W), C0, C1, A.mult)
+    iota(R("iff", 0, 128), [[-1, 16], [0, 8]], 31)
+    ts(R("ktc", 0, 128), R("iff", 0, 128), 8192.0, A.mult, 2048.0, A.add)
     SEG = R("seg", 0, W)
     ts(SEG, IE, 1.0, A.min)
-    ts(R("c0", 0, W), IE, -1.0, A.mult, float(2 ** 19 + 65536 + 15), A.add)
-    tt(R("k0", 0, W), R("c0", 0, W), R("c1", 0, W), A.mult)
-    ts(R("c0", 0, W), IE, -1.0, A.mult, -113.0, A.add)
-    ts(R("x0", 0, W), R("c0", 0, W), col(25), A.mult)
-    ts(R("x1", 0, W), col(24) and R("c1", 0, W), 622592.0, A.mult, col(24), A.mult)
-    tt(R("c0", 0, W), R("x0", 0, W), R("c1", 0, W), A.mult)
-    ts(R("x0", 0, W), IE, 16.0, A.is_equal, 65280.0, A.mult)
-    ts(R("m3", 0, W), R("x0", 0, W), col(24), A.mult)
-    tt(R("nn", 0, W), R("c0", 0, W), R("x1", 0, W), A.add)
-    tt(R("ckc", 0, W), R("nn", 0, W), R("m3", 0, W), A.add)
+    ts(C2, IE, -1.0, A.mult, float(2 ** 19 + 65536 + 15), A.add)
+    tt(R("k0", 0, W), C2, C1, A.mult)
+    ts(C0, IE, 113.0, A.add, col(22), A.mult)
+    ts(col(23), col(21), 622592.0, A.mult)
+    ts(C2, C0, -1.0, A.mult, col(23), A.add)
+    tt(C3, C2, C1, A.mult)
+    ts(col(9), col(21), 65280.0, A.mult)
+    ts(C0, IE, 16.0, A.is_equal, col(9), A.mult)
+    tt(R("ckc", 0, W), C3, C0, A.add)
     mset(R("one", 0, 128), 1.0)
     mset(R("cen", 0, 128), -2040.0)
-    iota(R("ig", 0, 64), [[0, 8], [1, 8]])
-    ts(R("rst", 0, 64), R("ig", 0, 64), 0.0, A.is_equal, 65536.0, A.mult)
-    ts(R("sd", 0, 64), R("ig", 0, 64), -5.0, A.mult, float(35 - 5 * s + 64), A.add)
-    iota(R("ik", 8, 16), [[0, 2], [1, 4]], 5 * s + 1 - 64)
-    cp(R("myc", 0, 8), R("ik", 8, 16))
-    cp(R("myc", 8, 16), R("ik", 8, 16))
+    iota(R("ig", 0, 192), [[0, 24], [1, 8]])
+    ts(R("rst", 0, 192), R("ig", 0, 192), 0.0, A.is_equal, 2.0 ** 24, A.mult)
+    ts(R("zc", 0, 128), R("ig", 0, 128), 256.0, A.mult)
+    iota(R("iz", 0, 64), [[1, 8], [M // 16, 8]])
+    ts(R("zc", 128, 192), R("iz", 0, 64), 16.0, A.mult)
+    iota(R("iz", 64, 128), [[1, 8], [-M // 16, 8]], 7 * M // 16)
+    cp(R("sd", 0, 64), R("iz", 64, 128))
+    ts(R("myc", 0, 8), IH(8), float(s * M // 16), A.add)
+    mset(R("ltc", 0, 8), 32.0)
+    mset(R("ltc", 8, 16), float(65536 - 2 ** 23))
 
     def B(b, c, n, a=0, e=None, st=1, k=0):
         return R(b, (k * NC + c) * n + a, (k * NC + c) * n + (n if e is None else e), st)
 
-    def PS(c, a, e, st=1, p=128):
-        return R("ps%d" % (3 + c), a, e, st, p)
+    def PS(c, a, e, st=1, p=128, p0=0):
+        return R("ps%d" % (3 + c), a, e, st, p, p0)
 
     def SO(c, j, a=0, e=W, st=1):
         return B("so", c, 576, W * j + a, W * j + e, st)
@@ -347,47 +318,43 @@ def build(s, cores, topo, ops, sends, arrive):
         cp(B("cki", c, W), B("ck", c, W))
         ts(B("cs", c, W), B("cki", c, W), 3, A.bitwise_and)
 
-    def pick(c, src):
-        cp(B("mi", c, 64), src)
-        ts(B("mz", c, 64), B("mi", c, 64), 4, A.arith_shift_right, 8191, A.bitwise_and)
-        cp(B("mf", c, 64), B("mz", c, 64))
-        scan(B("mn", c, 64), R("rst", 0, 64), B("mf", c, 64), A.add, A.min)
-        tt(B("mq", c, 64), B("mf", c, 64), B("mn", c, 64), A.is_gt)
-
     def offer(n, c):
-        m = 160 * (4 * n + c)
-        cp(B("zi", c, 16, 0, 8), SO(c, 3, 15, W, 18))
-        ts(B("zj", c, 16, 0, 8), B("zi", c, 16, 0, 8), 4095, A.bitwise_and)
-        cp(B("offy", c, 16, 0, 8), B("zj", c, 16, 0, 8))
-        for h in range(2):
-            act(R("ms", m + 144 * h, m + 144 * h + 16), ind(B("so", c, 576), L_M + 4 * ((n + 1) % 2) + 2 * h, 1))
-        act(R("ms", m + 16, m + 144), ("ind", BOOK, B("offy", c, 16, 0, 8)))
-        dst = R("lb", 640 * n + 80 * s, 640 * n + 80 * s + 80)
-        send([(R("ms", m + 80 * h, m + 80 * h + 80), dst, [pairs[c][h]]) for h in range(2) if pairs[c][h] != s], "rl%d" % n)
-        if c != oc:
-            return
-        act(dst, R("ms", m + 80 * ohf, m + 80 * ohf + 80))
-        lb = R("lb", 640 * n, 640 * n + 640)
-        sm = m + 144 * ohf
-        act(R("ow", 0, 64), ind(lb, L_P, 4))
-        pick(0, ind(lb, L_K, 4))
-        scan(R("rs", 0, 64), R("mq", 0, 64), R("ow", 0, 64), A.mult, A.max)
-        cp(R("ri", 0, 8), R("rs", 7, 64, 8))
-        ts(R("wl", 12, 16), R("ri", 4, 8), 16, A.arith_shift_right)
-        ts(R("offs", 0, 4), R("wl", 12, 16), 16.0, A.mult, col(15), A.add)
-        act(R("bc", m + 16 + 64 * ohf, m + 80 + 64 * ohf), ("ind", lb, R("offs", 0, 4)))
-        ts(R("wl", 0, 4), R("ri", 4, 8), 4095, A.bitwise_and)
-        ts(R("wl", 8, 12), R("ri", 4, 8), 3, A.bitwise_and)
-        ts(R("bc", sm, sm + 4), R("wl", 0, 4), 32.0, A.add)
-        cp(R("bc", sm + 8, sm + 16), R("wl", 8, 16))
-        ts(R("xx", 0, 4) if n else R("bc", sm + 4, sm + 8), R("wl", 0, 4), 2048.0, A.mult, float(65536 - 2 ** 23), A.add)
-        if n:
-            ts(R("wl", 4, 8), R("ri", 0, 4), 255, A.bitwise_and)
-            cp(R("wm", 0, 4), R("wl", 4, 8))
-            mm(R("ps7", 0, 4), R("same", 0, 128), R("wm", 0, 4), True, True)
-            tt(R("bc", sm + 4, sm + 8), R("ps7", 0, 4), R("xx", 0, 4), A.add)
-        src = R("bc", m + 80 * ohf, m + 80 * ohf + 80)
-        send([(src, src, others)], "rb%d" % (4 * n + c))
+        l0 = M * NS * (4 * n + c)
+        m = l0 + M * s
+        zi, zp, wl, ri, pc, pb = [lambda a, e, b=b: B(b, c, SB[b][0] // NC, a, e) for b in ("zi", "zp", "wl", "ri", "pc", "pb3")]
+        cp(zi(0, 32), ind(B("so", c, 576), L_M + 2 * ((n + 1) % 2), 2))
+        ts(B("zj", c, 8), zi(16, 24), 4095, A.bitwise_and)
+        cp(B("offy", c, 8), B("zj", c, 8))
+        act(R("lb", m, m + 128), ("ind", BOOK, B("offy", c, 8)))
+        ts(zi(8, 16), zi(8, 16), 4, A.arith_shift_right, 8191, A.bitwise_and)
+        ts(zp(0, 24), zi(0, 24), 255, A.bitwise_and)
+        ts(zp(24, 40), zi(8, 24), 8, A.arith_shift_right, 31, A.bitwise_and)
+        cp(R("lb", m + 128, m + 168), zp(0, 40))
+        send(R("lb", m, m + 168), R("lb", m, m + 168), others, "rl%d" % (4 * n + c))
+        lb = R("lb", l0, l0 + M * NS)
+        act(pc(0, 320), ind(lb, L_PC, 20))
+        mm(PS(c, 0, 192), R("one", 0, 128, 1, 1), R("zc", 0, 192, 1, 1), True, False)
+        for k in range(3):
+            mm(PS(c, 64 * k, 64 * k + 64), IB[6], pc(0, 64), False, False)
+            mm(PS(c, 64 * k, 64 * k + 64), IB[7], pc(64, 128), False, False)
+        mm(PS(c, 0, 192), IB[0], pc(128, 320), False, True)
+        scan(B("zr", c, 192), R("rst", 0, 192), PS(c, 0, 192), A.add, A.min)
+        cp(ri(0, 24), B("zr", c, 192, 7, 192, 8))
+        wd = B("wd", c, 8, k=n)
+        ts(wd, ri(16, 24), 4, A.arith_shift_right, 127, A.bitwise_and)
+        ts(B("offs", c, 8), wd, 16.0, A.mult, PB, A.add)
+        act(B("ybf", c, 128), ("ind", lb, B("offs", c, 8)))
+        ts(wl(0, 16), ri(0, 16), 255, A.bitwise_and)
+        ts(wl(16, 24), ri(16, 24), 15, A.bitwise_and)
+        ts(wl(24, 32), ri(8, 16), 3, A.bitwise_and)
+        cp(pb(0, 24), wl(0, 24))
+        mm(PS(c, 432, 448), R("one", 0, 128, 1, 1), R("ltc", 0, 16, 1, 1), True, False)
+        mm(PS(c, 432, 440), IB[0], pb(8, 16), False, False)
+        mm(PS(c, 432, 440), IB[5], pb(16, 24), False, False)
+        mm(PS(c, 440, 448), IB[6], pb(8, 16), False, False)
+        mm(PS(c, 440, 448), IB[7], pb(16, 24), False, False)
+        mm(PS(c, 440, 448), R("same", 0, 128), pb(0, 8), False, True)
+        act(B("lt", c, 16), PS(c, 432, 448))
 
     def cards(c, dst):
         cp(B("ci", c, 16), SO(c, 1, 17, 2 * W, 18))
@@ -420,12 +387,12 @@ def build(s, cores, topo, ops, sends, arrive):
         ts(B("hp", c, 128), ind(B("handi", c, 128), L_HP, 8), -2048.0, A.add)
         turn(B("ht", c, 128), B("hp", c, 128))
         mset(B("so", c, 576), 0.0)
-        mm(PS(c, W, 2 * W), I32, R("kt", 0, W), True, False)
+        mm(PS(c, 2 * W, 3 * W), I32, R("kt", 0, W), True, False)
         for n in range(8):
             for g_ in range(2):
-                mm(PS(c, W + 18 * n, W + 18 * n + 16), SW[n % 2, g_], B("ht", c, 128, 32 * (n // 2) + 16 * g_, 32 * (n // 2) + 16 * g_ + 16),
-                   False, n == 7 and g_ == 1)
-        act(B("ck", c, W), PS(c, W, 2 * W))
+                a = 32 * (n // 2) + 16 * g_
+                mm(PS(c, 2 * W + 18 * n, 2 * W + 18 * n + 16), SW[n % 2, g_], B("ht", c, 128, a, a + 16), False, n == 7 and g_ == 1)
+        act(B("ck", c, W), PS(c, 2 * W, 3 * W))
         op("v", 64 * CY, [SO(c, 0, 17, W, 18)], [LD],
            lambda g, T, c=c: g.vector.tensor_scalar(ap(T, SO(c, 0, 17, W, 18)), T.ldi[:, 8 * c:8 * c + 8], float(s), 16.0, A.not_equal, A.mult))
         cp(SO(c, 3, 15, W, 18), B("ck", c, W, 0, W, 18))
@@ -436,48 +403,45 @@ def build(s, cores, topo, ops, sends, arrive):
     MAG = 1.5 * 2.0 ** 23
     dbank = [0]
     for n in range(4):
-        KS = KSL[n]
+        KV = 16 - KSL[n]
         for c in range(NC):
             stage[0] = 4 + 4 * n + c
-            m = 160 * (4 * n + c)
-            bc, y = R("bc", m, m + 160), R("bc", m + 16, m + 144)
-            wd = lambda k: B("wd", c, 16, 0, 8, k=k)
+            y = B("ybf", c, 128)
+            wd = lambda k: B("wd", c, 8, k=k)
             isl = B("isl", c, 8, k=n)
-            tt(B("wd", c, 16, k=n), ind(bc, L_W, 1), R("myc", 0, 16), A.subtract)
-            ts(isl, wd(n), 64.0, A.is_equal)
+            tt(isl, wd(n), R("myc", 0, 8), A.is_equal)
             if n == 2:
                 redeal(c, wd(1), wd(2), B("ck", c, W), B("ck", c, W))
                 derive(c)
             tt(B("ck", c, W, 16, W, 18), isl, SO(c, 3, 15, W, 18), A.mult)
-            tt(B("v1", c, 128), ind(bc, L_L, 8), B("co", c, 128), A.mult)
-            tt(B("v2", c, 128), ind(bc, L_T, 8), B("v1", c, 128), A.add)
+            tt(B("v1", c, 128), ind(B("lt", c, 16, 0, 8), L_OB, 8), B("co", c, 128), A.mult)
+            tt(B("v2", c, 128), ind(B("lt", c, 16, 8, 16), L_OB, 8), B("v1", c, 128), A.add)
             ts(B("v3", c, 128), B("v2", c, 128), 5, A.arith_shift_right, 4095, A.bitwise_and)
             cp(B("offa", c, 128), B("v3", c, 128))
-            act(B("ybf", c, 128), y)
-            tt(B("mat", c, W), ind(bc, L_S, 9), B("cs", c, W), A.is_equal)
-            us = [(k, min(k + 4, KS), True) for k in range(0, KS, 4)]
-            uv = [(k, min(k + 4, 16), False) for k in range(KS, 16, 4)]
-            units = us[:1] + uv[:1] + us[1:2] + uv[1:] + us[2:]
-            for (k0, k1, onS) in units:
+            tt(B("mat", c, W), ind(B("wl", c, 32, 24, 32), L_G, 9), B("cs", c, W), A.is_equal)
+            us = [(max(k - 4, KV), k, True) for k in range(16, KV, -4)][::-1]
+            uv = [(k, min(k + 4, KV), False) for k in range(0, KV, 4)]
+            for (k0, k1, onS) in us[:1] + uv + us[1:]:
                 xd = lambda a, e: B("xd", c, 2048, 128 * a, 128 * e)
                 off = lambda a, e: ("ind", BOOK, B("offa", c, 128, 8 * a, 8 * e))
                 ph = B("phi", c, 2048, 128 * k0, 128 * k1)
                 if onS:
-                    d = "ps%d" % dbank[0]
-                    dbank[0] = (dbank[0] + 1) % 3
+                    d = "ps%d" % (0, 1, 2, 7)[dbank[0]]
+                    dbank[0] = (dbank[0] + 1) % 4
                     act(xd(k0, k1), off(k0, k1))
                     mm(R(d, 0, 128 * (k1 - k0)), IB[0], xd(k0, k1), True, False)
                     for k in range(k0, k1):
-                        mm(R(d, 128 * (k - k0), 128 * (k + 1 - k0)), IB[1], B("ybf", c, 128), False, k + 1 == k1)
-                    act(ph, R(d, 0, 128 * (k1 - k0)), F.Abs, col(22))
+                        mm(R(d, 128 * (k - k0), 128 * (k + 1 - k0)), IB[1], y, False, k + 1 == k1)
+                    act(ph, R(d, 0, 128 * (k1 - k0)), F.Abs, col(19))
                 else:
                     for k in range(k0, k1):
                         tt(xd(k, k + 1), off(k, k + 1), y, A.subtract)
-                    act(ph, xd(k0, k1), F.Abs, col(22))
+                    act(ph, xd(k0, k1), F.Abs, col(19))
             P1 = PS(c, 0, 128)
             mm(P1, IB[0], R("cen", 0, 128), True, False)
-            for b in range(16):
-                mm(PS(c, b, 128, 16), B("phi", c, 2048, b, 2048, 16), GH, False, b == 15)
+            for k0, k1 in [x for x in ((0, 16 - LAST), (16 - LAST, 16)) if x[0] < x[1]]:
+                for b in range(16):
+                    mm(PS(c, b, 128, 16, 8 * k1, 8 * k0), B("phi", c, 2048, 128 * k0 + b, 128 * k1, 16), GH, False, b == 15 and k1 == 16)
             ee, beat, ck, nn = B("ee", c, 128), B("beat", c, 128), B("ck", c, W), B("nn", c, W)
             ts(ee, P1, MAG, A.add, MAG, A.subtract)
             tt(beat, P1, ee, A.is_lt)
@@ -499,15 +463,17 @@ def build(s, cores, topo, ops, sends, arrive):
                 a0 = 192 * c + 24 * s
                 cp(R("al", a0, a0 + 8), SO(c, 0, 17, W, 18))
                 cards(c, R("al", a0 + 8, a0 + 24))
-                send([(R("al", a0, a0 + 24), R("al", a0, a0 + 24), others)], "ra%d" % c)
+                send(R("al", a0, a0 + 24), R("al", a0, a0 + 24), others, "ra%d" % c)
             if n == 1:
                 cf = B("cf", c, 16)
                 cards(c, cf)
                 to = [s // 2, NS // 2 + s // 2]
                 dst = B("pl", c, 32, 16 * (s % 2), 16 * (s % 2) + 16)
-                send([(cf, dst, [q for q in to if q != s])], "rp%d" % c)
+                send(cf, dst, [q for q in to if q != s], "rp%d" % c)
                 if s in to:
                     cp(dst, cf)
+                else:
+                    seq[0] += 1
             oh = B("oh", c, W, k=n % 2)
             tt(oh, ind(SO(c, 1 + n % 2), L_OH, 9), ck, A.is_equal)
             if n == 3:
@@ -515,23 +481,27 @@ def build(s, cores, topo, ops, sends, arrive):
                 tt(wo(0), B("isl", c, 8, k=1), B("isl", c, 8, k=2), A.add)
                 tt(wo(1), wo(0), isl, A.add)
                 tt(B("cb", c, W), ck, R("kt", 0, W), A.subtract)
+                mset(B("cb", c, W, 16, W, 18), 0.0)
                 u = [192 * c + 24 * ((2 * s + j) % NS) + 8 for j in range(2)]
                 diffs(c, ("al", a0 + 8), [("al", x) for x in u])
-                pick(c, ind(B("al", c, 192), L_AP, 4))
+                cp(B("mi", c, 64), ind(B("al", c, 192), L_AP, 4))
+                ts(B("mz", c, 64), B("mi", c, 64), 4, A.arith_shift_right, 8191, A.bitwise_and)
+                cp(B("mf", c, 64), B("mz", c, 64))
+                scan(B("mn", c, 64), R("rst", 0, 64), B("mf", c, 64), A.add, A.min)
+                tt(B("mq", c, 64), B("mf", c, 64), B("mn", c, 64), A.is_gt)
                 scan(B("rs", c, 64), B("mq", c, 64), R("sd", 0, 64), A.mult, A.max)
                 w1 = B("rs", c, 64, 7, 64, 8)
-                ts(B("isl", c, 8, k=4), w1, 64.0, A.is_equal)
+                tt(B("isl", c, 8, k=4), w1, R("myc", 0, 8), A.is_equal)
                 tt(wo(2), wo(1), B("isl", c, 8, k=4), A.add)
                 dma("y", "dw%d" % c, [], [wo(2)],
                     lambda g, T, c=c: g.sync.dma_start(T.yw[:, 128 * c:128 * c + 128], T.wo[:, 24 * c + 16:24 * c + 24]), 2000)
-                mset(B("cb", c, W, 16, W, 18), 0.0)
                 redeal(c, wd(3), w1, B("cc", c, W), B("cb", c, W))
                 for k in range(8):
                     for v in range(2):
                         a = 18 * (2 * (k // 2) + v)
                         mm(PS(c, 16 * k, 16 * k + 16), SW[k % 2, v], B("cc", c, W, a, a + 16), v == 0, v == 1)
                 turn(B("tr", c, 128), P1)
-                act(B("yo", c, 128), ind(B("tr", c, 128), L_YO, 8), F.Identity, col(23))
+                act(B("yo", c, 128), ind(B("tr", c, 128), L_YO, 8), F.Identity, col(20))
                 dma("y", "dy%d" % c, [], [B("yo", c, 128)],
                     lambda g, T, c=c: g.sync.dma_start(T.yc[:, 128 * c:128 * c + 128], T.yo[:, 128 * c:128 * c + 128]), 2000)
                 continue
@@ -546,7 +516,7 @@ def build(s, cores, topo, ops, sends, arrive):
                 tt(B("k3", c, W), K3, R("k0", 0, W), A.max)
                 K3 = B("k3", c, W)
                 diffs(c, ("cf", 16 * c), [("pl", 32 * c), ("pl", 32 * c + 16)])
-                ts(B("sm", c, 48, 0, 8), wd(1), 64.0, order)
+                tt(B("sm", c, 48, 0, 8), wd(1), R("myc", 0, 8), order)
                 deltas(c, B("sm", c, 48, 0, 8))
                 for j in range(2):
                     tt(B("sm", c, 48, 24 + 8 * j, 32 + 8 * j), B("dl", c, 16, 8 * j, 8 * j + 8), B("oh", c, W, 0, W, 18, k=j), A.mult)
@@ -586,24 +556,24 @@ def place(res, cost, pre, suc, head, key):
 
 
 def plan(cores, topo):
-    ops, sends, arrive = [], {}, {}
+    every, sends, arrive = [], {}, {}
     for s in range(NS):
-        build(s, cores, topo, ops, sends, arrive)
-    res, cost, st = [(o["s"], o["eng"]) for o in ops], [o["cost"] for o in ops], [o["st"] for o in ops]
+        build(s, cores, topo, every, sends, arrive)
+    ops = [o for o in every if o["s"] == 0]
+    res, cost, st = [o["eng"] for o in ops], [o["cost"] for o in ops], [o["st"] for o in ops]
     pre, dn = [[] for _ in ops], {}
     for o in ops:
         if o["kind"] == "r":
-            dn[o["id"]] = len(res)
-            res.append((o["s"], "d"))
+            dn[o["sem"]] = len(res)
+            res.append("d")
             cost.append(o["lat"] - HOP)
             st.append(o["st"])
             pre.append([(o["id"], 500.0)])
     for o in ops:
         p = pre[o["id"]]
         for q, w in o["deps"].items():
-            p.append((q, 0.0 if not w else (ops[q]["lat"] if ops[q]["kind"] == "d" else (SAME if ops[q]["eng"] == o["eng"] else CROSS))))
-        for sm_ in o["rw"]:
-            p += [(dn[q["id"]], HOP - 500.0) for q in sends[(o["s"], sm_)]]
+            p.append((q, 0.0 if not w else (ops[q]["lat"] if ops[q]["kind"] == "d" else WAIT)))
+        p += [(dn[sm_], HOP - 500.0) for sm_ in o["rw"]]
     n = len(res)
     tail = [o["lat"] if o["kind"] == "d" else 0.0 for o in ops] + [0.0] * (n - len(ops))
     suc = [[] for _ in res]
@@ -615,8 +585,12 @@ def plan(cores, topo):
     for i in sorted(range(n), key=lambda i: rank[i]):
         st[i] = min([st[i]] + [st[j] for j, l in suc[i]])
     best = None
-    for wt in WTS:
-        t0 = place(res, cost, pre, suc, [0.0] * n, [wt * st[i] - rank[i] for i in range(n)])
+    for k in range(len(WTS) + SHAKES):
+        if k < len(WTS):
+            key = [WTS[k] * st[i] - rank[i] for i in range(n)]
+        else:
+            key = [best[1][i] + (300, 800, 1500)[k % 3] * ((i * 7919 + k * 104729) ** 2 % 1009) / 1009.0 for i in range(n)]
+        t0 = place(res, cost, pre, suc, [0.0] * n, key)
         for _ in range(3):
             b = place(res, cost, suc, pre, tail, [-(t0[i] + cost[i]) for i in range(n)])
             t0 = place(res, cost, pre, suc, [0.0] * n, [-(b[i] + cost[i]) for i in range(n)])
@@ -624,13 +598,13 @@ def plan(cores, topo):
             if best is None or end < best[0]:
                 best = (end, t0)
     queue, cnt = {}, {}
-    for i in sorted(range(len(ops)), key=lambda i: (best[1][i], i)):
-        ops[i]["t0"] = best[1][i]
-        queue.setdefault(res[i], []).append(i)
-        if ops[i]["kind"] == "c":
-            cnt[res[i]] = cnt.get(res[i], 0) + 1
-            ops[i]["n"] = cnt[res[i]]
-    return ops, queue, arrive, best[0], sends
+    for o in sorted(every, key=lambda o: (best[1][o["k"]], o["id"])):
+        o["t0"] = best[1][o["k"]]
+        e = (o["s"], o["eng"])
+        queue.setdefault(e, []).append(o["id"])
+        if o["kind"] == "c":
+            cnt[e] = o["n"] = cnt.get(e, 0) + 1
+    return every, queue, arrive, best[0], sends
 
 
 def rank_program(g, core, T, topo):

@@ -2,32 +2,32 @@ from concourse.bass import DstId, RemoteDMATransfer
 from concourse.mybir import AluOpType as A, ActivationFunctionType as F
 
 NS, NC, W = 8, 4, 144
-KSL = [11, 11, 11, 11]
-LAST = 0
-M = 176
+KSL = [10, 10, 11, 10]
+KA = 12
+M = 168
 H16 = "float16"
 f32, i32, u16, bf = "float32", "int32", "uint16", "bfloat16"
 SB = {
     "book": (4096, bf), "handi": (512, i32), "hp": (512, H16), "ht": (512, H16), "ldi": (32, i32),
-    "phi": (NC * 2048, f32), "xd": (NC * 2048, bf), "ybf": (NC * 128, bf),
-    "ck": (NC * W, f32), "cki": (NC * W, i32), "cs": (NC * W, i32), "co": (NC * 128, f32),
+    "phi": (NC * 2048, f32), "xd": (NC * 2048, bf), "ybf": (NC * 128, bf), "ph2": (NC * 512, bf),
+    "ck": (NC * W, f32), "dk": (NC * W, f32), "cki": (NC * W, i32), "cs": (NC * W, i32), "co": (NC * 128, f32),
     "v1": (NC * 128, f32), "v2": (NC * 128, i32), "v3": (NC * 128, i32), "offa": (NC * 128, u16),
-    "ee": (NC * 128, H16), "be": (NC * 128, H16), "beat": (NC * 128, bf), "mat": (NC * W, bf), "oh": (2 * NC * W, bf),
-    "nn": (NC * W, f32), "m3": (NC * W, f32), "k3": (NC * W, f32), "so": (NC * 576, f32), "isl": (5 * NC * 8, bf),
-    "wd": (4 * NC * 8, i32), "zi": (NC * 32, i32), "zj": (NC * 8, i32), "zp": (NC * 48, i32), "offy": (NC * 8, u16),
-    "lb": (16 * NS * M, bf), "pc": (NC * 320, bf), "lt": (NC * 16, f32), "pb3": (NC * 24, bf), "zr": (NC * 192, f32),
-    "ri": (NC * 24, i32), "wl": (NC * 32, i32), "offs": (NC * 8, u16), "al": (NC * 192, f32), "pl": (NC * 32, f32),
-    "ci": (NC * 16, i32), "cj": (NC * 16, i32), "cf": (NC * 16, f32), "fd": (NC * 32, f32), "dl": (NC * 16, f32),
-    "sm": (NC * 48, f32), "x0": (NC * W, f32), "x1": (NC * W, f32), "cb": (NC * W, f32), "cc": (NC * W, H16),
-    "tr": (NC * 128, f32), "yo": (512, f32), "wo": (NC * 24, f32), "mi": (NC * 64, i32), "mz": (NC * 64, i32),
-    "mf": (NC * 64, f32), "mn": (NC * 64, f32), "mq": (NC * 64, f32), "rs": (NC * 64, f32),
-    "ia": (128, i32), "ib": (128, i32), "ic": (W, i32), "ie": (W, i32), "iff": (128, i32), "ig": (192, i32), "iz": (128, i32),
-    "ih": (16, i32), "ij": (16, i32), "im": (16, i32), "inn": (16, i32), "pi": (8, i32), "pj": (8, i32), "pf": (24, f32),
-    "c0": (W, f32), "c1": (W, f32), "c2": (W, f32), "c3": (W, f32),
-    "i32": (128, f32), "ibf": (8 * 128, bf), "sw": (4 * 128, H16), "gh": (8, f32), "same": (128, bf),
-    "pe": (W, H16), "pb": (W, bf), "pd": (W, H16), "kt": (W, f32), "ktc": (128, f32), "k0": (W, f32), "myc": (8, f32),
-    "zc": (192, bf), "ltc": (16, bf), "seg": (W, f32), "ckc": (W, bf), "one": (128, bf), "cen": (128, bf),
-    "rst": (192, f32), "sd": (64, f32), "lst": (128, u16),
+    "ee": (NC * 128, H16), "be": (NC * 128, H16), "beat": (NC * 128, bf), "mat": (NC * W, bf), "oh": (NC * 2 * W, bf),
+    "nn": (NC * W, f32), "m3": (NC * W, f32), "k3": (NC * W, f32), "so": ((NC + 1) * 576, f32), "isl": (5 * NC * 8, bf),
+    "zi": (NC * 32, i32), "zp": (NC * 48, i32), "offy": (NC * 8, u16),
+    "lb": (16 * NS * M, bf), "pc": (NC * 320, bf), "lt": (NC * 24, f32), "pb3": (4 * NC * 32, bf), "zr": (NC * 320, f32),
+    "wl": (NC * 16, i32), "offs": (NC * 8, u16), "al": (NC * 192, f32), "pl": (NC * 32, f32),
+    "cf": (NC * 16, f32), "fd": (NC * 32, f32), "gg": (NC * 32, f32), "dl": (NC * 16, f32),
+    "sm": (NC * 48, f32), "xx": (NC * 2 * W, f32), "cc": (NC * W, H16),
+    "tr": (NC * 128, f32), "yo": (512, f32), "wo": (NC * 24, f32), "mi": (NC * 40, i32),
+    "mf": (NC * 64, f32), "mn": (NC * 64, f32),
+    "ia": (128, i32), "ib": (128, i32), "ic": (W, i32), "ie": (W, i32), "iff": (128, i32), "ig": (320, i32),
+    "ih": (18, i32), "ij": (16, i32), "im": (18, i32), "inn": (18, i32), "pi": (8, i32), "pj": (8, i32), "pf": (32, f32),
+    "c0": (W, f32), "c1": (W, f32), "c2": (W, f32), "c3": (W, f32), "c4": (W, f32), "c5": (W, f32), "c6": (W, f32),
+    "i32": (3 * 128, f32), "ibf": (11 * 128, bf), "sw": (4 * 128, H16), "gh": (8, f32), "gh2": (16, bf), "two": (128, bf),
+    "same": (128, bf), "pe": (W, H16), "pb": (W, bf), "pd": (W, H16), "kt": (W, f32), "ktc": (128, f32), "k0": (W, f32),
+    "zc": (320, bf), "ltc": (24, bf), "seg": (W, f32), "ckc": (W, bf), "one": (128, bf), "cen": (128, bf),
+    "rst": (320, f32), "lst": (96, u16),
 }
 SCRATCH = {k: ("sbuf", [128, n], d) for k, (n, d) in SB.items()}
 for _b in range(8):
@@ -36,8 +36,9 @@ SEMAPHORES = (["nv", "ns", "nt", "ng", "loc", "dbk0", "dbk1", "dh0", "dh1", "dld
               + ["dw%d" % c for c in range(NC)] + ["rl%d" % n for n in range(4 * NC)]
               + ["rp%d" % c for c in range(NC)] + ["ra%d" % c for c in range(NC)])
 CNT = {"v": "nv", "s": "ns", "t": "nt", "g": "ng"}
-CY, PCY, GAT, CALL, HOP, ROW, BYTE, WAIT = 0.95, 0.48, 1.56, 750, 2000, 30, 0.05, 220.0
-WTS, SHAKES = (3000.0, 4000.0, 5000.0, 6000.0, 7000.0), 60
+CY, PCY, GAT, CALL, HOP, ROW, BYTE = 0.95, 0.475, 1.56, 750, 2000, 30, 0.05
+WTS, SHAKES = (3000.0, 4000.0, 5000.0, 6000.0, 7000.0), 100
+CASES = ((1.0, 1.0, 220, 1.0), (1.2, 1.0, 200, 1.0), (1.15, 0.7, 150, 1.1), (1.1, 1.25, 200, 1.0), (1.0, 1.0, 220, 1.5))
 PLAN = {}
 
 
@@ -67,6 +68,12 @@ def bits(engs):
     return sum(1 << e for e in engs)
 
 
+def write(g, T, topo, parts, src, dst, sem):
+    tl = [RemoteDMATransfer(dst_ids=[DstId(rid=topo.addr(q)[0], pnc=topo.addr(q)[1]) for q in qs], dma_engine_mask=bits(e),
+                            remote_sem=T.sem[sem], srcs=[ap(T, src)], dsts=[ap(T, dst) for q in qs]) for qs, e in parts]
+    return g.remote_dma_fused(tl, local_sem=T.sem.loc)
+
+
 def meet(r, d):
     if r[1] >= d[1] or d[0] >= r[2]:
         return False
@@ -75,7 +82,7 @@ def meet(r, d):
 
 def build(s, cores, topo, ops, sends, arrive):
     me = cores[s]
-    hist, bank, land, stage, seq = {}, {}, [], [99], [0]
+    hist, bank, land, stage, seq, lastq = {}, {}, {}, [99], [0], {}
 
     def op(eng, cost, outs, ins, fn, kind="c", sem=None, lat=0.0):
         o = {"s": s, "eng": eng, "cost": cost, "fn": fn, "kind": kind, "sem": sem, "lat": lat, "deps": {}, "rw": set(),
@@ -89,9 +96,8 @@ def build(s, cores, topo, ops, sends, arrive):
         for wr, rs in ((0, rd), (1, outs)):
             for r in rs:
                 b, c0, c1 = r[0], r[1], r[2]
-                for (lb_, l0, l1, sm_) in land:
-                    if lb_ == b and not wr and kind != "r" and c0 < l1 and l0 < c1:
-                        o["rw"].add(sm_)
+                if b in land and not wr and kind != "r":
+                    o["rw"].add(land[b][1] % (c0 // land[b][0]))
                 keep = []
                 for d in hist.get(b, []):
                     d0, d1, w, q, st = d
@@ -99,7 +105,8 @@ def build(s, cores, topo, ops, sends, arrive):
                         o["deps"][q["id"]] = not (eng == "t" and q["eng"] == "t")
                     if not (wr and r[3] == 1 and c0 <= d0 and d1 <= c1):
                         keep.append(d)
-                keep.append((c0, c1, wr, o, r[3]))
+                if wr or stage[0] == 99 or b not in fixed:
+                    keep.append((c0, c1, wr, o, r[3]))
                 hist[b] = keep
                 if b.startswith("ps"):
                     run = bank.setdefault(b, [[], []])
@@ -113,6 +120,8 @@ def build(s, cores, topo, ops, sends, arrive):
                         run[1].append(o)
         ops.append(o)
         return o
+
+    fixed = set(list(SB)[list(SB).index("ia"):] + ["book"])
 
     def vcost(out, in0, two=False):
         n = width(in0)
@@ -144,12 +153,10 @@ def build(s, cores, topo, ops, sends, arrive):
     def mset(out, v):
         op("v", max(64, width(out)) * CY, [out], [], lambda g, T: g.vector.memset(ap(T, out), v))
 
-    def act(out, a, f=F.Copy, bias=None):
+    def act(out, a, f=F.Copy, bias=None, scale=None):
         c = 80 + width(a) * CY * (GAT if a[0] == "ind" else 1)
-        if bias is None:
-            op("s", c, [out], [a], lambda g, T: g.scalar.activation(ap(T, out), ap(T, a), f))
-        else:
-            op("s", c, [out], [a, bias], lambda g, T: g.scalar.activation(ap(T, out), ap(T, a), f, bias=ap(T, bias)))
+        more = [(k, v) for k, v in (("bias", bias), ("scale", scale)) if v is not None]
+        op("s", c, [out], [a, bias, scale], lambda g, T: g.scalar.activation(ap(T, out), ap(T, a), f, **{k: ap(T, v) for k, v in more}))
 
     def mm(out, l, r, st, sp):
         c = max(min(64, width(l)), width(r)) * (4 if dty(l) == f32 else 1) * PCY
@@ -159,7 +166,10 @@ def build(s, cores, topo, ops, sends, arrive):
         op("g", 160 + 2 * width(out) * CY, [out], [], lambda g, T: g.iota(ap(T, out), pat, base, cm))
 
     def dma(q, sem, outs, ins, fn, lat):
-        op(q, 60, outs, ins, fn, "d", sem, lat)
+        o = op(q, 60, outs, ins, fn, "d", sem, lat)
+        if outs and q in lastq:
+            o["deps"][lastq[q]] = False
+        lastq[q] = o["id"]
 
     def ind(win, c0, n):
         return ("ind", win, R("lst", c0, c0 + n))
@@ -170,44 +180,33 @@ def build(s, cores, topo, ops, sends, arrive):
             if topo.chip(cores[q]) != topo.chip(me):
                 e = topo.engines(me, cores[q])
                 shared = e if shared is None else [x for x in shared if x in e]
-        near = [q for q in to if topo.chip(cores[q]) == topo.chip(me)]
-        far = [q for q in to if q not in near]
+        near = [cores[q] for q in to if topo.chip(cores[q]) == topo.chip(me)]
+        far = [cores[q] for q in to if cores[q] not in near]
         final = [(far, shared)] if far else []
         if near:
-            final.append((near, [x for x in topo.engines(me, cores[near[0]]) if x not in shared]))
-        rows = max(128 * len(qs) // len(e) for qs, e in final)
-
-        def fn(g, T):
-            tl = [RemoteDMATransfer(dst_ids=[DstId(rid=topo.addr(cores[q])[0], pnc=topo.addr(cores[q])[1]) for q in qs],
-                                    dma_engine_mask=bits(e), remote_sem=T.sem[sem], srcs=[ap(T, src)], dsts=[ap(T, dst) for q in qs])
-                  for (qs, e) in final]
-            return g.remote_dma_fused(tl, local_sem=T.sem.loc)
+            final.append((near, [x for x in topo.engines(me, near[0]) if x not in shared]))
         nb = width(src) * (2 if dty(src) == bf else 4)
-        o = op("g", CALL, [], [src], fn, "r", sem, HOP + rows * (ROW + nb * BYTE))
+        rows = max(128 * len(qs) // len(e) for qs, e in final)
+        o = op("g", CALL, [], [src], lambda g, T: write(g, T, topo, final, src, dst, sem), "r", sem, HOP + rows * (ROW + nb * BYTE))
         o["loc"] = sum(len(e) for qs, e in final)
         o["rows"], o["bytes"] = rows, nb
         for qs, e in final:
-            for q in qs:
+            for q in [cores.index(x) for x in qs]:
                 arrive[(q, sem)] = arrive.get((q, sem), 0) + len(e)
                 sends.setdefault((q, sem), []).append(o)
 
     others = [(s + k) % NS for k in range(1, NS)]
-    for k in range(4 * NC):
-        for q in others:
-            land.append(("lb", M * (NS * k + q), M * (NS * k + q) + 168, "rl%d" % k))
-    for c in range(NC):
-        land.append(("al", 192 * c, 192 * c + 192, "ra%d" % c))
-        land.append(("pl", 32 * c, 32 * c + 32, "rp%d" % c))
+    land.update({"lb": (M * NS, "rl%d"), "al": (192, "ra%d"), "pl": (32, "rp%d")})
 
     for h, q in enumerate("ys"):
         eng = lambda g, q=q: g.sync if q == "y" else g.scalar
         dma(q, "dh%d" % h, [R("handi", 256 * h, 256 * h + 256)], [],
             lambda g, T, h=h, eng=eng: eng(g).dma_start(T.handi[:, 256 * h:256 * h + 256], T.hand[:, 256 * h:256 * h + 256]), 2300)
+        for c in range(NC * (1 - h)):
+            dma(q, "dld", [R("ldi", 8 * c, 8 * c + 8)], [],
+                lambda g, T, c=c: g.sync.dma_start(T.ldi[:, 8 * c:8 * c + 8], T.ld[:, 128 * c:128 * c + 128]), 2800)
         dma(q, "dbk%d" % h, [R("book", 2048 * h, 2048 * h + 2048)], [],
             lambda g, T, h=h, eng=eng: eng(g).dma_start(T.book[:, 2048 * h:2048 * h + 2048], T.bk[:, 2048 * h:2048 * h + 2048]), 5500)
-    for c in range(NC):
-        dma("y", "dld", [R("ldi", 8 * c, 8 * c + 8)], [],
-            lambda g, T, c=c: g.sync.dma_start(T.ldi[:, 8 * c:8 * c + 8], T.ld[:, 128 * c:128 * c + 128]), 5500)
     LD = R("ldi", 0, 32)
     BOOK = R("book", 0, 4096)
 
@@ -222,45 +221,54 @@ def build(s, cores, topo, ops, sends, arrive):
     ts(col(10), P8, 18.0, A.mult, B3, A.add)
     ts(col(11), P8, 16.0, A.mult, B3, A.add)
     ts(col(12), P8, float(M), A.mult, B3, A.add)
-    ts(col(13), P8, -24.0, A.mult, B3, A.add)
+    ts(col(13), P8, 24.0, A.mult, B3, A.add)
     ts(col(14), P8, 18.0, A.mult, PK, A.add)
     ts(col(16), B4, -1.0, A.mult, 1.0, A.add)
     ts(col(17), PB, 8.0, A.mult)
-    ts(col(18), P8, 18.0, A.mult, 17.0, A.add)
+    ts(col(18), P8, 18.0, A.mult, 16.0, A.add)
     mset(col(19), -1.0 / 64)
     mset(col(20), 2048.0)
     ts(col(21), P, 0.0, A.is_equal)
     ts(col(22), P, 1.0, A.is_equal)
-    iota(R("ih", 0, 16), [[1, 16]])
+    iota(R("ih", 0, 18), [[1, 18]])
     IH = lambda n: R("ih", 0, n)
-    L_HP, L_OB, L_CO, L_YO, L_G, L_OH, L_M, L_AP, L_PC = 0, 8, 16, 24, 32, 42, 52, 56, 60
+    L_HP, L_OB, L_CO, L_YO, L_G, L_OH, L_M, L_AP, L_PC, L_PL, L_AL, L_D = 0, 8, 16, 24, 32, 50, 60, 64, 68, 88, 90, 92
     lst = lambda a, n: R("lst", a, a + n)
     ts(lst(L_HP, 8), IH(8), col(17), A.add)
     ts(lst(L_OB, 8), IH(8), 0.0, A.mult, P8, A.add)
     ts(R("ij", 0, 16), IH(16), 2.0, A.mult)
     ts(lst(L_CO, 8), R("ij", 0, 8), col(10), A.add)
     ts(lst(L_YO, 8), R("ij", 0, 8), col(11), A.add)
-    ts(lst(L_AP, 4), R("ij", 0, 4), col(13), A.add, 168.0, A.add)
+    ts(lst(L_AP, 4), R("ij", 0, 4), col(13), A.add)
     ts(col(15), B3, -1.0, A.mult, 1.0, A.add)
     for par in range(2):
         ts(lst(L_M + 2 * par, 1), col(15), float(W * (1 + par)), A.mult, col(18), A.add)
-        ts(lst(L_M + 2 * par + 1, 1), col(18), 3.0 * W - 2, A.add)
-    for j in range(168, M):
-        mset(R("lb", j, 16 * NS * M, M), 0.0)
+        ts(lst(L_M + 2 * par + 1, 1), col(18), 3.0 * W - 1, A.add)
     for k, a in enumerate((136, 152, 128, 144, 160)):
         ts(lst(L_PC + 4 * k, 4), R("ij", 0, 4), col(12), A.add, float(a), A.add)
-    ts(R("im", 0, 9), IH(9), 16.0, A.mult, PB, A.add)
-    ts(R("inn", 0, 9), R("im", 0, 9), 3641.0, A.mult)
-    ts(R("im", 0, 9), R("inn", 0, 9), 16, A.arith_shift_right)
-    cp(lst(L_G, 9), R("im", 0, 9))
-    ts(lst(L_OH, 9), R("im", 0, 9), 18.0, A.mult, 17.0, A.add)
+    ts(col(6), B3, 16.0, A.mult, P8, A.add)
+    ts(lst(L_PL, 2), IH(2), 8.0, A.mult, col(6), A.add)
+    ts(col(7), B3, 24.0, A.mult, P8, A.add)
+    ts(col(8), col(7), 24.0 * (2 * s % NS) + (8 if s < NS // 2 else 16), A.add)
+    ts(lst(L_AL, 2), IH(2), 8.0 if s < NS // 2 else -8.0, A.mult, col(8), A.add)
+    for k in range(2):
+        ts(lst(L_D + k, 1), P8, 8.0, A.mult, 7.0, A.add)
+    ts(R("im", 0, 18), IH(18), 16.0, A.mult, PB, A.add)
+    ts(R("inn", 0, 18), R("im", 0, 18), 3641.0, A.mult)
+    ts(R("im", 0, 18), R("inn", 0, 18), 16, A.arith_shift_right)
+    cp(lst(L_G, 18), R("im", 0, 18))
+    ts(lst(L_OH, 9), R("im", 0, 9), 18.0, A.mult, 16.0, A.add)
     iota(R("ia", 0, 128), [[-1, 128]], 0, 1)
     IA = R("ia", 0, 128)
     I32 = R("i32", 0, 128)
     ts(I32, IA, 0.0, A.is_equal)
-    IB = [R("ibf", 128 * k, 128 * k + 128) for k in range(8)]
-    for k, w in enumerate((1.0, -1.0, 2.0 ** 18, -2.0 ** 19, 2.0 ** 22, 256.0, 2048.0, 2.0 ** 19)):
-        ts(IB[k], IA, 0.0, A.is_equal, w, A.mult)
+    IB = {}
+    for k, w in enumerate((1, -1, 2 ** 18, -2 ** 19, 2 ** 22, -16, 2048, 2 ** 19, -1 / 16, M / 256, -2048)):
+        IB[w] = R("ibf", 128 * k, 128 * k + 128)
+        act(IB[w], I32, F.Copy, None, float(w))
+    IF = {w: R("i32", 128 * k, 128 * k + 128) for k, w in enumerate((1, 1 / 16, -1 / 16))}
+    for w in (1 / 16, -1 / 16):
+        act(IF[w], I32, F.Copy, None, w)
     SW = {}
     for a in range(2):
         for b in range(2):
@@ -268,41 +276,49 @@ def build(s, cores, topo, ops, sends, arrive):
             ts(SW[a, b], IA, 16.0 * (a - b), A.is_equal, B4 if a else col(16), A.mult)
     GH = R("gh", 0, 8)
     ts(GH, IH(8), PG, A.is_equal)
+    act(R("gh2", 0, 8), GH, F.Copy, None, 2.0)
+    act(R("gh2", 8, 16), GH, F.Copy, None, -1.0)
     iota(R("ib", 0, 128), [[0, 8], [1, 16]])
-    ts(R("same", 0, 128), R("ib", 0, 128), PB, A.is_equal, 416.0, A.mult)
+    ts(R("same", 0, 128), R("ib", 0, 128), PB, A.is_equal, -416.0, A.mult)
     iota(R("ic", 0, W), [[1, W]])
     for b, w in (("pe", 16.0), ("pb", 65536.0), ("pd", -32.0)):
         ts(R(b, 0, W), R("ic", 0, W), col(14), A.is_equal, w, A.mult)
     iota(R("ie", 0, W), [[0, 8], [1, 18]])
-    IE, C0, C1, C2, C3 = R("ie", 0, W), R("c0", 0, W), R("c1", 0, W), R("c2", 0, W), R("c3", 0, W)
-    ts(C1, IE, 16.0, A.is_lt)
-    ts(C0, IE, -8192.0, A.mult, 31 * 8192.0 + 2048, A.add)
-    tt(R("kt", 0, W), C0, C1, A.mult)
-    iota(R("iff", 0, 128), [[-1, 16], [0, 8]], 31)
-    ts(R("ktc", 0, 128), R("iff", 0, 128), 8192.0, A.mult, 2048.0, A.add)
+    IE = R("ie", 0, W)
+    C = [R("c%d" % k, 0, W) for k in range(7)]
+    ts(C[1], IE, 16.0, A.is_lt)
+    ts(C[0], IE, 0.5, A.mult, 2.0 ** 17 + 32768, A.add)
+    tt(R("kt", 0, W), C[0], C[1], A.mult)
+    iota(R("iff", 0, 128), [[1, 16], [0, 8]])
+    ts(R("ktc", 0, 128), R("iff", 0, 128), 0.5, A.mult, 2.0 ** 17 + 32768, A.add)
     SEG = R("seg", 0, W)
     ts(SEG, IE, 1.0, A.min)
-    ts(C2, IE, -1.0, A.mult, float(2 ** 19 + 65536 + 15), A.add)
-    tt(R("k0", 0, W), C2, C1, A.mult)
-    ts(C0, IE, 113.0, A.add, col(22), A.mult)
+    ts(C[2], IE, -1.0, A.mult, float(2 ** 19 + 65536 + 15), A.add)
+    tt(R("k0", 0, W), C[2], C[1], A.mult)
+    ts(C[3], IE, 113.0, A.add, col(22), A.mult)
     ts(col(23), col(21), 622592.0, A.mult)
-    ts(C2, C0, -1.0, A.mult, col(23), A.add)
-    tt(C3, C2, C1, A.mult)
+    ts(C[4], C[3], -1.0, A.mult, col(23), A.add)
+    tt(C[5], C[4], C[1], A.mult)
     ts(col(9), col(21), 65280.0, A.mult)
-    ts(C0, IE, 16.0, A.is_equal, col(9), A.mult)
-    tt(R("ckc", 0, W), C3, C0, A.add)
+    ts(C[6], IE, 16.0, A.is_equal, col(9), A.mult)
+    tt(R("ckc", 0, W), C[5], C[6], A.add)
     mset(R("one", 0, 128), 1.0)
     mset(R("cen", 0, 128), -2040.0)
-    iota(R("ig", 0, 192), [[0, 24], [1, 8]])
-    ts(R("rst", 0, 192), R("ig", 0, 192), 0.0, A.is_equal, 2.0 ** 24, A.mult)
-    ts(R("zc", 0, 128), R("ig", 0, 128), 256.0, A.mult)
-    iota(R("iz", 0, 64), [[1, 8], [M // 16, 8]])
-    ts(R("zc", 128, 192), R("iz", 0, 64), 16.0, A.mult)
-    iota(R("iz", 64, 128), [[1, 8], [-M // 16, 8]], 7 * M // 16)
-    cp(R("sd", 0, 64), R("iz", 64, 128))
-    ts(R("myc", 0, 8), IH(8), float(s * M // 16), A.add)
-    mset(R("ltc", 0, 8), 32.0)
+    ts(R("two", 0, 128), R("ic", 0, 128), 8.0 * KA, A.is_ge, -0.25, A.mult)
+    iota(R("ig", 0, 320), [[0, 40], [1, 8]])
+    ts(R("rst", 0, 320), R("ig", 0, 320), 0.0, A.is_equal, 2.0 ** 24, A.mult)
+    ts(R("zc", 0, 320), R("ig", 0, 320), 256.0, A.mult)
+    mset(R("zc", 192, 256), 0.0)
+    mset(R("dk", W - 1, NC * W, W), 0.0)
+    mset(R("ltc", 0, 8), 2.0)
     mset(R("ltc", 8, 16), float(65536 - 2 ** 23))
+    ts(R("ltc", 16, 24), IH(8), 16.0, A.mult, PB, A.add)
+    ZERO = R("so", NC * 576, NC * 576 + 576)
+    mset(ZERO, 0.0)
+
+    def halves(f, *rs):
+        for h in range(2):
+            f(*[(r[0], r[1] + h * (r[2] - r[1]) // 2, r[1] + (h + 1) * (r[2] - r[1]) // 2) + r[3:] if isinstance(r, tuple) else r for r in rs])
 
     def B(b, c, n, a=0, e=None, st=1, k=0):
         return R(b, (k * NC + c) * n + a, (k * NC + c) * n + (n if e is None else e), st)
@@ -315,153 +331,164 @@ def build(s, cores, topo, ops, sends, arrive):
 
     def derive(c):
         tt(B("co", c, 128), ind(B("ck", c, W), L_CO, 8), R("ktc", 0, 128), A.subtract)
+        tt(B("dk", c, W, 0, W - 1), B("ck", c, W, 0, W - 1), B("ck", c, W, 1, W), A.subtract)
         cp(B("cki", c, W), B("ck", c, W))
-        ts(B("cs", c, W), B("cki", c, W), 3, A.bitwise_and)
+        ts(B("cs", c, W), B("cki", c, W), 4, A.arith_shift_right, 3, A.bitwise_and)
 
     def offer(n, c):
         l0 = M * NS * (4 * n + c)
         m = l0 + M * s
-        zi, zp, wl, ri, pc, pb = [lambda a, e, b=b: B(b, c, SB[b][0] // NC, a, e) for b in ("zi", "zp", "wl", "ri", "pc", "pb3")]
+        zi, zp, wl, pc = [lambda a, e, b=b: B(b, c, SB[b][0] // NC, a, e) for b in ("zi", "zp", "wl", "pc")]
+        pb = lambda a, e: B("pb3", c, 32, a, e, k=n)
         cp(zi(0, 32), ind(B("so", c, 576), L_M + 2 * ((n + 1) % 2), 2))
-        ts(B("zj", c, 8), zi(16, 24), 4095, A.bitwise_and)
-        cp(B("offy", c, 8), B("zj", c, 8))
+        ts(B("offy", c, 8), SO(c, 3, 15, W, 18), 1 / 16, A.mult, -8192.0, A.add)
         act(R("lb", m, m + 128), ("ind", BOOK, B("offy", c, 8)))
-        ts(zi(8, 16), zi(8, 16), 4, A.arith_shift_right, 8191, A.bitwise_and)
-        ts(zp(0, 24), zi(0, 24), 255, A.bitwise_and)
-        ts(zp(24, 40), zi(8, 24), 8, A.arith_shift_right, 31, A.bitwise_and)
-        cp(R("lb", m + 128, m + 168), zp(0, 40))
-        send(R("lb", m, m + 168), R("lb", m, m + 168), others, "rl%d" % (4 * n + c))
+        ts(zp(0, 24), zi(0, 24), 4, A.arith_shift_right, 255, A.bitwise_and)
+        ts(zp(24, 40), zi(8, 24), 12, A.arith_shift_right, 31, A.bitwise_and)
+        cp(R("lb", m + 128, m + M), zp(0, 40))
+        send(R("lb", m, m + M), R("lb", m, m + M), others, "rl%d" % (4 * n + c))
         lb = R("lb", l0, l0 + M * NS)
         act(pc(0, 320), ind(lb, L_PC, 20))
-        mm(PS(c, 0, 192), R("one", 0, 128, 1, 1), R("zc", 0, 192, 1, 1), True, False)
-        for k in range(3):
-            mm(PS(c, 64 * k, 64 * k + 64), IB[6], pc(0, 64), False, False)
-            mm(PS(c, 64 * k, 64 * k + 64), IB[7], pc(64, 128), False, False)
-        mm(PS(c, 0, 192), IB[0], pc(128, 320), False, True)
-        scan(B("zr", c, 192), R("rst", 0, 192), PS(c, 0, 192), A.add, A.min)
-        cp(ri(0, 24), B("zr", c, 192, 7, 192, 8))
-        wd = B("wd", c, 8, k=n)
-        ts(wd, ri(16, 24), 4, A.arith_shift_right, 127, A.bitwise_and)
-        ts(B("offs", c, 8), wd, 16.0, A.mult, PB, A.add)
+        mm(PS(c, 0, 320), R("one", 0, 128, 1, 1), R("zc", 0, 320, 1, 1), True, False)
+        for k in range(5):
+            mm(PS(c, 64 * k, 64 * k + 64), IB[2048], pc(0, 64), False, False)
+            mm(PS(c, 64 * k, 64 * k + 64), IB[2 ** 19], pc(64, 128), False, False)
+        mm(PS(c, 0, 192), IB[1], pc(128, 320), False, True)
+        scan(B("zr", c, 320), R("rst", 0, 320), PS(c, 0, 320), A.add, A.min)
+        tt(pb(0, 32), ind(B("zr", c, 320, 256), L_D, 2), B("zr", c, 320, 7, 256, 8), A.subtract)
+        ts(wl(0, 8), pb(8, 16), -1.0, A.mult)
+        ts(wl(8, 16), wl(0, 8), 3, A.bitwise_and)
+        mm(PS(c, 432, 456), IB[1], R("ltc", 0, 24), True, False)
+        mm(PS(c, 432, 440), IB[-1 / 16], pb(8, 16), False, False)
+        mm(PS(c, 432, 440), IB[-16], pb(16, 24), False, False)
+        mm(PS(c, 440, 448), IB[-2048], pb(8, 16), False, False)
+        mm(PS(c, 440, 448), IB[-2 ** 19], pb(16, 24), False, False)
+        mm(PS(c, 440, 448), R("same", 0, 128), pb(0, 8), False, False)
+        mm(PS(c, 448, 456), IB[M / 256], pb(24, 32), False, True)
+        act(B("lt", c, 24), PS(c, 432, 456))
+        cp(B("offs", c, 8), B("lt", c, 24, 16, 24))
         act(B("ybf", c, 128), ("ind", lb, B("offs", c, 8)))
-        ts(wl(0, 16), ri(0, 16), 255, A.bitwise_and)
-        ts(wl(16, 24), ri(16, 24), 15, A.bitwise_and)
-        ts(wl(24, 32), ri(8, 16), 3, A.bitwise_and)
-        cp(pb(0, 24), wl(0, 24))
-        mm(PS(c, 432, 448), R("one", 0, 128, 1, 1), R("ltc", 0, 16, 1, 1), True, False)
-        mm(PS(c, 432, 440), IB[0], pb(8, 16), False, False)
-        mm(PS(c, 432, 440), IB[5], pb(16, 24), False, False)
-        mm(PS(c, 440, 448), IB[6], pb(8, 16), False, False)
-        mm(PS(c, 440, 448), IB[7], pb(16, 24), False, False)
-        mm(PS(c, 440, 448), R("same", 0, 128), pb(0, 8), False, True)
-        act(B("lt", c, 16), PS(c, 432, 448))
 
-    def cards(c, dst):
-        cp(B("ci", c, 16), SO(c, 1, 17, 2 * W, 18))
-        ts(B("cj", c, 16), B("ci", c, 16), 4095, A.bitwise_and)
-        cp(dst, B("cj", c, 16))
-
-    def diffs(c, mine, got):
-        for j in range(2):
-            g0, g1 = (R(got[j][0], got[j][1] + 8 * k, got[j][1] + 8 * k + 8) for k in range(2))
-            tt(B("fd", c, 32, 8 * j, 8 * j + 8), g1, R(mine[0], mine[1] + 8 * j, mine[1] + 8 * j + 8), A.subtract)
-            tt(B("fd", c, 32, 16 + 8 * j, 24 + 8 * j), g0, g1, A.subtract)
-
-    def deltas(c, src0):
-        for j in range(2):
-            tt(B("sm", c, 48, 8 + 8 * j, 16 + 8 * j), B("fd", c, 32, 16 + 8 * j, 24 + 8 * j), src0, A.mult)
-        tt(B("dl", c, 16), B("sm", c, 48, 8, 24), B("fd", c, 32, 0, 16), A.add)
-
+    MAG = 1.5 * 2.0 ** 23
     order = A.is_le if s < NS // 2 else A.is_gt
 
-    def redeal(c, w0, w1, out, old):
-        tt(B("sm", c, 48, 0, 8), w0, w1, order)
-        deltas(c, B("sm", c, 48, 0, 8))
-        for j, x in enumerate(("x0", "x1")):
-            tt(B(x, c, W), ind(B("dl", c, 16, 8 * j, 8 * j + 8), L_G, 9), B("oh", c, W, k=j), A.mult)
-            mm(PS(c, 2 * W, 3 * W), I32, B(x, c, W), j == 0, j == 1)
-        tt(out, PS(c, 2 * W, 3 * W), old, A.add)
+    def cards(c, dst):
+        ts(dst, SO(c, 1, 16, 2 * W, 18), 16 * MAG, A.add, 16 * MAG, A.subtract)
+
+    def diffs(c, mine, got):
+        act(B("gg", c, 32), got)
+        tt(B("fd", c, 32, 0, 16), B("gg", c, 32, 16, 32), mine, A.subtract)
+        tt(B("fd", c, 32, 16, 32), B("gg", c, 32, 0, 16), B("gg", c, 32, 16, 32), A.subtract)
+
+    def deltas(c, first):
+        tt(B("sm", c, 48, 8, 24), ind(first, L_OB, 1), B("fd", c, 32, 16, 32), A.mult)
+        tt(B("dl", c, 16), B("sm", c, 48, 8, 24), B("fd", c, 32, 0, 16), A.add)
+
+    def redeal(c, first, last):
+        deltas(c, first)
+        tt(B("xx", c, 2 * W), ind(B("dl", c, 16), L_G, 18), B("oh", c, 2 * W), A.mult)
+        new, ck = PS(c, 2 * W, 3 * W), B("ck", c, W)
+        if last:
+            mm(new, IF[-1 / 16], R("kt", 0, W), True, False)
+            mm(new, IF[1 / 16], ck, False, False)
+        for j in range(2):
+            mm(new, IF[1 / 16 if last else 1], B("xx", c, 2 * W, W * j, W * j + W), j == 0 and not last, j == 1)
+        if last:
+            cp(B("cc", c, W), new)
+        else:
+            tt(ck, new, ck, A.add)
 
     for c in range(NC):
         stage[0] = c
-        ts(B("hp", c, 128), ind(B("handi", c, 128), L_HP, 8), -2048.0, A.add)
+        ts(B("hp", c, 128), ind(B("handi", c, 128), L_HP, 8), -2048.0, A.add, 16.0, A.mult)
         turn(B("ht", c, 128), B("hp", c, 128))
-        mset(B("so", c, 576), 0.0)
+        act(B("so", c, 576), ZERO)
         mm(PS(c, 2 * W, 3 * W), I32, R("kt", 0, W), True, False)
         for n in range(8):
             for g_ in range(2):
                 a = 32 * (n // 2) + 16 * g_
                 mm(PS(c, 2 * W + 18 * n, 2 * W + 18 * n + 16), SW[n % 2, g_], B("ht", c, 128, a, a + 16), False, n == 7 and g_ == 1)
         act(B("ck", c, W), PS(c, 2 * W, 3 * W))
-        op("v", 64 * CY, [SO(c, 0, 17, W, 18)], [LD],
-           lambda g, T, c=c: g.vector.tensor_scalar(ap(T, SO(c, 0, 17, W, 18)), T.ldi[:, 8 * c:8 * c + 8], float(s), 16.0, A.not_equal, A.mult))
+        op("v", 64 * CY, [SO(c, 0, 16, W, 18)], [LD],
+           lambda g, T, c=c: g.vector.tensor_scalar(ap(T, SO(c, 0, 16, W, 18)), T.ldi[:, 8 * c:8 * c + 8], float(s), 16.0, A.not_equal, A.mult))
         cp(SO(c, 3, 15, W, 18), B("ck", c, W, 0, W, 18))
         offer(0, c)
         stage[0] = 4 + c
         derive(c)
 
-    MAG = 1.5 * 2.0 ** 23
     dbank = [0]
     for n in range(4):
-        KV = 16 - KSL[n]
         for c in range(NC):
             stage[0] = 4 + 4 * n + c
             y = B("ybf", c, 128)
-            wd = lambda k: B("wd", c, 8, k=k)
+            wd = lambda k: B("pb3", c, 32, 24, 32, k=k)
+            OH = lambda k: B("oh", c, 2 * W, W * k, W * k + W)
             isl = B("isl", c, 8, k=n)
-            tt(isl, wd(n), R("myc", 0, 8), A.is_equal)
+            ts(isl, wd(n), 256.0 * s, A.is_equal)
             if n == 2:
-                redeal(c, wd(1), wd(2), B("ck", c, W), B("ck", c, W))
+                tt(B("sm", c, 48, 0, 8), wd(1), wd(2), order)
+                redeal(c, B("sm", c, 48, 0, 8), False)
                 derive(c)
-            tt(B("ck", c, W, 16, W, 18), isl, SO(c, 3, 15, W, 18), A.mult)
-            tt(B("v1", c, 128), ind(B("lt", c, 16, 0, 8), L_OB, 8), B("co", c, 128), A.mult)
-            tt(B("v2", c, 128), ind(B("lt", c, 16, 8, 16), L_OB, 8), B("v1", c, 128), A.add)
-            ts(B("v3", c, 128), B("v2", c, 128), 5, A.arith_shift_right, 4095, A.bitwise_and)
-            cp(B("offa", c, 128), B("v3", c, 128))
-            tt(B("mat", c, W), ind(B("wl", c, 32, 24, 32), L_G, 9), B("cs", c, W), A.is_equal)
-            us = [(max(k - 4, KV), k, True) for k in range(16, KV, -4)][::-1]
-            uv = [(k, min(k + 4, KV), False) for k in range(0, KV, 4)]
+            tt(B("dk", c, W, 16, W, 18), isl, SO(c, 3, 15, W, 18), A.mult)
+            tt(B("v1", c, 128), ind(B("lt", c, 24, 0, 8), L_OB, 8), B("co", c, 128), A.mult)
+            tt(B("v2", c, 128), ind(B("lt", c, 24, 8, 16), L_OB, 8), B("v1", c, 128), A.add)
+            halves(ts, B("v3", c, 128), B("v2", c, 128), 5, A.arith_shift_right, 4095, A.bitwise_and)
+            halves(cp, B("offa", c, 128), B("v3", c, 128))
+            tt(B("mat", c, W), ind(B("wl", c, 16, 8, 16), L_G, 9), B("cs", c, W), A.is_equal)
+            KS = KSL[n]
+            xd = lambda a, e: B("xd", c, 2048, 128 * a, 128 * e)
+            off = lambda a, e: ("ind", BOOK, B("offa", c, 128, 8 * a, 8 * e))
+            us = [(k, min(k + 4, KS), True) for k in range(0, KS, 4)]
+            uv = [x for x in ((KS, KA, False), (KA, 16, False)) if x[0] < x[1]]
             for (k0, k1, onS) in us[:1] + uv + us[1:]:
-                xd = lambda a, e: B("xd", c, 2048, 128 * a, 128 * e)
-                off = lambda a, e: ("ind", BOOK, B("offa", c, 128, 8 * a, 8 * e))
                 ph = B("phi", c, 2048, 128 * k0, 128 * k1)
                 if onS:
                     d = "ps%d" % (0, 1, 2, 7)[dbank[0]]
                     dbank[0] = (dbank[0] + 1) % 4
                     act(xd(k0, k1), off(k0, k1))
-                    mm(R(d, 0, 128 * (k1 - k0)), IB[0], xd(k0, k1), True, False)
+                    mm(R(d, 0, 128 * (k1 - k0)), IB[1], xd(k0, k1), True, False)
                     for k in range(k0, k1):
-                        mm(R(d, 128 * (k - k0), 128 * (k + 1 - k0)), IB[1], y, False, k + 1 == k1)
+                        mm(R(d, 128 * (k - k0), 128 * (k + 1 - k0)), IB[-1], y, False, k + 1 == k1)
                     act(ph, R(d, 0, 128 * (k1 - k0)), F.Abs, col(19))
                 else:
                     for k in range(k0, k1):
                         tt(xd(k, k + 1), off(k, k + 1), y, A.subtract)
-                    act(ph, xd(k0, k1), F.Abs, col(19))
+                    if k0 < KA:
+                        act(ph, xd(k0, k1), F.Abs, col(19))
+                    else:
+                        ts(B("ph2", c, 512), xd(k0, k1), 1.0 / 64, A.max)
             P1 = PS(c, 0, 128)
-            mm(P1, IB[0], R("cen", 0, 128), True, False)
-            for k0, k1 in [x for x in ((0, 16 - LAST), (16 - LAST, 16)) if x[0] < x[1]]:
-                for b in range(16):
-                    mm(PS(c, b, 128, 16, 8 * k1, 8 * k0), B("phi", c, 2048, 128 * k0 + b, 128 * k1, 16), GH, False, b == 15 and k1 == 16)
-            ee, beat, ck, nn = B("ee", c, 128), B("beat", c, 128), B("ck", c, W), B("nn", c, W)
-            ts(ee, P1, MAG, A.add, MAG, A.subtract)
-            tt(beat, P1, ee, A.is_lt)
-            tt(B("be", c, 128), beat, ee, A.mult)
+            mm(P1, R("one", 0, 128, 1, 1), R("cen", 0, 128, 1, 1), True, False)
+            for b in range(16):
+                mm(PS(c, b, 128, 16, 128, 8 * KA), B("xd", c, 2048, 128 * KA + b, 2048, 16), R("gh2", 8, 16), False, False)
+                mm(PS(c, b, 128, 16, 128, 8 * KA), B("ph2", c, 512, b, 512, 16), R("gh2", 0, 8), False, False)
+            for b in range(16):
+                mm(PS(c, b, 128, 16, 8 * KA), B("phi", c, 2048, b, 128 * KA, 16), GH, False, False)
+            mm(P1, R("two", 0, 128, 1, 1), R("one", 0, 128, 1, 1), False, True)
+            ee, beat, ck, dk, nn = B("ee", c, 128), B("beat", c, 128), B("ck", c, W), B("dk", c, W), B("nn", c, W)
+            halves(ts, ee, P1, MAG, A.add, MAG, A.subtract)
+            halves(tt, beat, P1, ee, A.is_lt)
+            halves(tt, B("be", c, 128), beat, ee, A.mult)
             K = PS(c, W, 2 * W)
             const = lambda k: mm(k, R("one", 0, 128, 1, 2), R("ckc", 0, W, 1, 2), True, False)
             const(K)
-            mm(K, IB[2], B("mat", c, W), False, False)
-            mm(PS(c, W + 16, 2 * W, 18), IB[4], isl, False, False)
+            mm(K, IB[2 ** 18], B("mat", c, W), False, False)
+            mm(PS(c, W + 16, 2 * W, 18), IB[2 ** 22], isl, False, False)
             if n % 2:
-                mm(K, IB[3], B("oh", c, W, k=0), False, False)
+                mm(K, IB[-2 ** 19], OH(0), False, False)
             mm(K, ee, R("pe", 0, W), False, False)
             mm(K, beat, R("pb", 0, W), False, False)
             mm(K, B("be", c, 128), R("pd", 0, W), False, True)
-            scan(SO(c, 0), SEG, K, A.mult, A.max)
-            tt(nn, K, SO(c, 0), A.is_lt)
-            scan(SO(c, 1 + n % 2), nn, ck, A.mult, A.max)
+            halves(scan, SO(c, 0), SEG, K, A.mult, A.max)
+            halves(tt, nn, K, SO(c, 0), A.is_lt)
+            halves(scan, SO(c, 1 + n % 2), nn, dk, A.mult, A.add)
             if n == 3:
                 a0 = 192 * c + 24 * s
-                cp(R("al", a0, a0 + 8), SO(c, 0, 17, W, 18))
+                mi = lambda k: B("mi", c, 40, 8 * k, 8 * k + 8)
+                ts(B("sm", c, 48, 0, 8), wd(3), 256.0 * s, A.is_le, 2.0 * s, A.add)
+                cp(mi(0), SO(c, 0, 16, W, 18))
+                ts(mi(1), mi(0), 16 * 8191, A.bitwise_and)
+                tt(R("al", a0, a0 + 8), mi(1), B("sm", c, 48, 0, 8), A.add)
                 cards(c, R("al", a0 + 8, a0 + 24))
                 send(R("al", a0, a0 + 24), R("al", a0, a0 + 24), others, "ra%d" % c)
             if n == 1:
@@ -471,31 +498,26 @@ def build(s, cores, topo, ops, sends, arrive):
                 dst = B("pl", c, 32, 16 * (s % 2), 16 * (s % 2) + 16)
                 send(cf, dst, [q for q in to if q != s], "rp%d" % c)
                 if s in to:
-                    cp(dst, cf)
+                    op("v", 64 * CY, [B("pl", c, 32)], [cf], lambda g, T, dst=dst, cf=cf: g.vector.tensor_copy(ap(T, dst), ap(T, cf)))
                 else:
                     seq[0] += 1
-            oh = B("oh", c, W, k=n % 2)
+            oh = OH(n % 2)
             tt(oh, ind(SO(c, 1 + n % 2), L_OH, 9), ck, A.is_equal)
             if n == 3:
                 wo = lambda k: B("wo", c, 24, 8 * k, 8 * k + 8)
                 tt(wo(0), B("isl", c, 8, k=1), B("isl", c, 8, k=2), A.add)
                 tt(wo(1), wo(0), isl, A.add)
-                tt(B("cb", c, W), ck, R("kt", 0, W), A.subtract)
-                mset(B("cb", c, W, 16, W, 18), 0.0)
-                u = [192 * c + 24 * ((2 * s + j) % NS) + 8 for j in range(2)]
-                diffs(c, ("al", a0 + 8), [("al", x) for x in u])
-                cp(B("mi", c, 64), ind(B("al", c, 192), L_AP, 4))
-                ts(B("mz", c, 64), B("mi", c, 64), 4, A.arith_shift_right, 8191, A.bitwise_and)
-                cp(B("mf", c, 64), B("mz", c, 64))
+                diffs(c, R("al", a0 + 8, a0 + 24), ind(B("al", c, 192), L_AL, 2))
+                act(B("mf", c, 64), ind(B("al", c, 192), L_AP, 4))
                 scan(B("mn", c, 64), R("rst", 0, 64), B("mf", c, 64), A.add, A.min)
-                tt(B("mq", c, 64), B("mf", c, 64), B("mn", c, 64), A.is_gt)
-                scan(B("rs", c, 64), B("mq", c, 64), R("sd", 0, 64), A.mult, A.max)
-                w1 = B("rs", c, 64, 7, 64, 8)
-                tt(B("isl", c, 8, k=4), w1, R("myc", 0, 8), A.is_equal)
+                cp(mi(2), B("mn", c, 64, 7, 64, 8))
+                ts(mi(3), mi(2), 1, A.bitwise_and)
+                ts(mi(4), mi(2), 14, A.bitwise_and)
+                ts(B("isl", c, 8, k=4), mi(4), 2.0 * s, A.is_equal)
                 tt(wo(2), wo(1), B("isl", c, 8, k=4), A.add)
                 dma("y", "dw%d" % c, [], [wo(2)],
                     lambda g, T, c=c: g.sync.dma_start(T.yw[:, 128 * c:128 * c + 128], T.wo[:, 24 * c + 16:24 * c + 24]), 2000)
-                redeal(c, wd(3), w1, B("cc", c, W), B("cb", c, W))
+                redeal(c, mi(3), True)
                 for k in range(8):
                     for v in range(2):
                         a = 18 * (2 * (k // 2) + v)
@@ -509,24 +531,21 @@ def build(s, cores, topo, ops, sends, arrive):
             const(K3)
             mm(K3, ee, R("pe", 0, W), False, False)
             if n == 1:
-                mm(K3, IB[3], B("oh", c, W, k=0), False, False)
-            mm(K3, IB[3], oh, False, True)
-            row0 = B("ck", c, W, 0, W, 18)
+                mm(K3, IB[-2 ** 19], OH(0), False, False)
+            mm(K3, IB[-2 ** 19], oh, False, True)
             if n == 1:
+                row0 = B("dk", c, W, 0, W, 18)
                 tt(B("k3", c, W), K3, R("k0", 0, W), A.max)
                 K3 = B("k3", c, W)
-                diffs(c, ("cf", 16 * c), [("pl", 32 * c), ("pl", 32 * c + 16)])
-                tt(B("sm", c, 48, 0, 8), wd(1), R("myc", 0, 8), order)
+                diffs(c, B("cf", c, 16), ind(B("pl", c, 32), L_PL, 2))
+                ts(B("sm", c, 48, 0, 8), wd(1), 256.0 * s, order)
                 deltas(c, B("sm", c, 48, 0, 8))
-                for j in range(2):
-                    tt(B("sm", c, 48, 24 + 8 * j, 32 + 8 * j), B("dl", c, 16, 8 * j, 8 * j + 8), B("oh", c, W, 0, W, 18, k=j), A.mult)
+                tt(B("sm", c, 48, 24, 40), B("dl", c, 16), B("oh", c, 2 * W, 0, 2 * W, 18), A.mult)
                 tt(B("sm", c, 48, 40, 48), B("sm", c, 48, 24, 32), B("sm", c, 48, 32, 40), A.add)
                 tt(row0, row0, B("sm", c, 48, 40, 48), A.add)
-            scan(B("m3", c, W), SEG, K3, A.mult, A.max)
-            tt(nn, K3, B("m3", c, W), A.is_lt)
-            scan(SO(c, 3), nn, ck, A.mult, A.max)
-            if n == 1:
-                tt(row0, row0, B("sm", c, 48, 40, 48), A.subtract)
+            halves(scan, B("m3", c, W), SEG, K3, A.mult, A.max)
+            halves(tt, nn, K3, B("m3", c, W), A.is_lt)
+            halves(scan, SO(c, 3), nn, dk, A.mult, A.add)
             offer(n + 1, c)
 
 
@@ -555,46 +574,62 @@ def place(res, cost, pre, suc, head, key):
     return t0
 
 
-def plan(cores, topo):
-    every, sends, arrive = [], {}, {}
-    for s in range(NS):
-        build(s, cores, topo, every, sends, arrive)
-    ops = [o for o in every if o["s"] == 0]
-    res, cost, st = [o["eng"] for o in ops], [o["cost"] for o in ops], [o["st"] for o in ops]
+def graph(ops, case):
+    calc, gat, wait, slow = case
+    res, cost = [o["eng"] for o in ops], [(o["cost"] + o["gat"] * (gat - 1)) * (calc if o["eng"] in "vst" else 1) for o in ops]
     pre, dn = [[] for _ in ops], {}
     for o in ops:
         if o["kind"] == "r":
             dn[o["sem"]] = len(res)
             res.append("d")
-            cost.append(o["lat"] - HOP)
-            st.append(o["st"])
+            cost.append((o["lat"] - HOP) * slow)
             pre.append([(o["id"], 500.0)])
     for o in ops:
         p = pre[o["id"]]
         for q, w in o["deps"].items():
-            p.append((q, 0.0 if not w else (ops[q]["lat"] if ops[q]["kind"] == "d" else WAIT)))
-        p += [(dn[sm_], HOP - 500.0) for sm_ in o["rw"]]
-    n = len(res)
-    tail = [o["lat"] if o["kind"] == "d" else 0.0 for o in ops] + [0.0] * (n - len(ops))
+            p.append((q, 0.0 if not w else (ops[q]["lat"] if ops[q]["kind"] == "d" else wait)))
+        p += [(dn[sm_], HOP * (1 + slow) / 2 - 500.0) for sm_ in o["rw"]]
     suc = [[] for _ in res]
     for i, p in enumerate(pre):
         for q, l in p:
             suc[q].append((i, l))
+    return res, cost, pre, suc
+
+
+def length(t0, res, cost, pre, tail):
+    done, free = {}, {}
+    for i in sorted(range(len(res)), key=lambda i: (t0[i], i)):
+        done[i] = free[res[i]] = max([free.get(res[i], 0.0)] + [done[q] + l for q, l in pre[i]]) + cost[i]
+    return max(done[i] + tail[i] for i in done)
+
+
+def plan(cores, topo):
+    every, sends, arrive = [], {}, {}
+    for s in range(NS):
+        build(s, cores, topo, every, sends, arrive)
+    ops = [o for o in every if o["s"] == 0]
+    G = [graph(ops, x) for x in CASES]
+    base = [sum(c for c, e in zip(g[1], g[0]) if e == "v") + 40000.0 for g in G]
+    res, cost, pre, suc = G[0]
+    n = len(res)
+    st = [o["st"] for o in ops] + [o["st"] for o in ops if o["kind"] == "r"]
+    tail = [o["lat"] if o["kind"] == "d" else 0.0 for o in ops] + [0.0] * (n - len(ops))
     b = place(list(range(n)), cost, suc, pre, tail, list(range(n)))
     rank = [b[i] + cost[i] for i in range(n)]
     for i in sorted(range(n), key=lambda i: rank[i]):
         st[i] = min([st[i]] + [st[j] for j, l in suc[i]])
     best = None
     for k in range(len(WTS) + SHAKES):
+        res, cost, pre, suc = G[k % 4]
         if k < len(WTS):
             key = [WTS[k] * st[i] - rank[i] for i in range(n)]
         else:
             key = [best[1][i] + (300, 800, 1500)[k % 3] * ((i * 7919 + k * 104729) ** 2 % 1009) / 1009.0 for i in range(n)]
         t0 = place(res, cost, pre, suc, [0.0] * n, key)
-        for _ in range(3):
+        for _ in range(3 if k < len(WTS) else 2):
             b = place(res, cost, suc, pre, tail, [-(t0[i] + cost[i]) for i in range(n)])
             t0 = place(res, cost, pre, suc, [0.0] * n, [-(b[i] + cost[i]) for i in range(n)])
-            end = max(t0[i] + cost[i] + tail[i] for i in range(n))
+            end = sum(length(t0, g[0], g[1], g[2], tail) / x for x, g in zip(base, G))
             if best is None or end < best[0]:
                 best = (end, t0)
     queue, cnt = {}, {}

from concourse.bass import DstId, RemoteDMATransfer
from concourse.mybir import AluOpType as A, ActivationFunctionType as F

NS, NC, W = 8, 4, 144
KSL = [10, 10, 11, 10]
KA = 12
M = 168
H16 = "float16"
f32, i32, u16, bf = "float32", "int32", "uint16", "bfloat16"
SB = {
    "book": (4096, bf), "handi": (512, i32), "hp": (512, H16), "ht": (512, H16), "ldi": (32, i32),
    "phi": (NC * 2048, f32), "xd": (NC * 2048, bf), "ybf": (NC * 128, bf), "ph2": (NC * 512, bf),
    "ck": (NC * W, f32), "dk": (NC * W, f32), "cki": (NC * W, i32), "cs": (NC * W, i32), "co": (NC * 128, f32),
    "v1": (NC * 128, f32), "v2": (NC * 128, i32), "v3": (NC * 128, i32), "offa": (NC * 128, u16),
    "ee": (NC * 128, H16), "be": (NC * 128, H16), "beat": (NC * 128, bf), "mat": (NC * W, bf), "oh": (NC * 2 * W, bf),
    "nn": (NC * W, f32), "m3": (NC * W, f32), "k3": (NC * W, f32), "so": ((NC + 1) * 576, f32), "isl": (5 * NC * 8, bf),
    "zi": (NC * 32, i32), "zp": (NC * 48, i32), "offy": (NC * 8, u16),
    "lb": (16 * NS * M, bf), "pc": (NC * 320, bf), "lt": (NC * 24, f32), "pb3": (4 * NC * 32, bf), "zr": (NC * 320, f32),
    "wl": (NC * 16, i32), "offs": (NC * 8, u16), "al": (NC * 192, f32), "pl": (NC * 32, f32),
    "cf": (NC * 16, f32), "fd": (NC * 32, f32), "gg": (NC * 32, f32), "dl": (NC * 16, f32),
    "sm": (NC * 48, f32), "xx": (NC * 2 * W, f32), "cc": (NC * W, H16),
    "tr": (NC * 128, f32), "yo": (512, f32), "wo": (NC * 24, f32), "mi": (NC * 40, i32),
    "mf": (NC * 64, f32), "mn": (NC * 64, f32),
    "ia": (128, i32), "ib": (128, i32), "ic": (W, i32), "ie": (W, i32), "iff": (128, i32), "ig": (320, i32),
    "ih": (18, i32), "ij": (16, i32), "im": (18, i32), "inn": (18, i32), "pi": (8, i32), "pj": (8, i32), "pf": (32, f32),
    "c0": (W, f32), "c1": (W, f32), "c2": (W, f32), "c3": (W, f32), "c4": (W, f32), "c5": (W, f32), "c6": (W, f32),
    "i32": (3 * 128, f32), "ibf": (11 * 128, bf), "sw": (4 * 128, H16), "gh": (8, f32), "gh2": (16, bf), "two": (128, bf),
    "same": (128, bf), "pe": (W, H16), "pb": (W, bf), "pd": (W, H16), "kt": (W, f32), "ktc": (128, f32), "k0": (W, f32),
    "zc": (320, bf), "ltc": (24, bf), "seg": (W, f32), "ckc": (W, bf), "one": (128, bf), "cen": (128, bf),
    "rst": (320, f32), "lst": (96, u16),
}
SCRATCH = {k: ("sbuf", [128, n], d) for k, (n, d) in SB.items()}
for _b in range(8):
    SCRATCH["ps%d" % _b] = ("psum", [128, 512], f32)
SEMAPHORES = (["nv", "ns", "nt", "ng", "loc", "dbk0", "dbk1", "dh0", "dh1", "dld"] + ["dy%d" % c for c in range(NC)]
              + ["dw%d" % c for c in range(NC)] + ["rl%d" % n for n in range(4 * NC)]
              + ["rp%d" % c for c in range(NC)] + ["ra%d" % c for c in range(NC)])
CNT = {"v": "nv", "s": "ns", "t": "nt", "g": "ng"}
CY, PCY, GAT, CALL, HOP, ROW, BYTE = 0.95, 0.475, 1.56, 750, 2000, 30, 0.05
WTS, SHAKES = (3000.0, 4000.0, 5000.0, 6000.0, 7000.0), 100
CASES = ((1.0, 1.0, 220, 1.0), (1.2, 1.0, 200, 1.0), (1.15, 0.7, 150, 1.1), (1.1, 1.25, 200, 1.0), (1.0, 1.0, 220, 1.5))
PLAN = {}


def R(b, c0, c1, st=1, p=128, p0=0):
    return (b, c0, c1, st, p, p0)


def ap(T, r):
    if not isinstance(r, tuple):
        return r
    if r[0] == "ind":
        return ap(T, r[1]).indirect(ap(T, r[2]))
    b, c0, c1, st, p, p0 = r
    return T[b][p0:p, c0:c1:st] if st > 1 else T[b][p0:p, c0:c1]


def width(r):
    return 16 * (r[2][2] - r[2][1]) if r[0] == "ind" else (r[2] - r[1] + r[3] - 1) // r[3]


def dty(r):
    r = r[1] if r[0] == "ind" else r
    return f32 if r[0].startswith("ps") else SB[r[0]][1]


def bits(engs):
    return sum(1 << e for e in engs)


def write(g, T, topo, parts, src, dst, sem):
    tl = [RemoteDMATransfer(dst_ids=[DstId(rid=topo.addr(q)[0], pnc=topo.addr(q)[1]) for q in qs], dma_engine_mask=bits(e),
                            remote_sem=T.sem[sem], srcs=[ap(T, src)], dsts=[ap(T, dst) for q in qs]) for qs, e in parts]
    return g.remote_dma_fused(tl, local_sem=T.sem.loc)


def meet(r, d):
    if r[1] >= d[1] or d[0] >= r[2]:
        return False
    return r[3] != d[4] or (r[1] - d[0]) % r[3] == 0


def build(s, cores, topo, ops, sends, arrive):
    me = cores[s]
    hist, bank, land, stage, seq, lastq = {}, {}, {}, [99], [0], {}

    def op(eng, cost, outs, ins, fn, kind="c", sem=None, lat=0.0):
        o = {"s": s, "eng": eng, "cost": cost, "fn": fn, "kind": kind, "sem": sem, "lat": lat, "deps": {}, "rw": set(),
             "id": len(ops), "st": stage[0], "gat": cost if any(isinstance(r, tuple) and r[0] == "ind" for r in ins) else 0,
             "out": outs[0] if outs else None, "k": seq[0]}
        seq[0] += 1
        rd = []
        for r in ins:
            if isinstance(r, tuple):
                rd += [r[1], r[2]] if r[0] == "ind" else [r]
        for wr, rs in ((0, rd), (1, outs)):
            for r in rs:
                b, c0, c1 = r[0], r[1], r[2]
                if b in land and not wr and kind != "r":
                    o["rw"].add(land[b][1] % (c0 // land[b][0]))
                keep = []
                for d in hist.get(b, []):
                    d0, d1, w, q, st = d
                    if (w or wr) and q is not o and meet(r, d):
                        o["deps"][q["id"]] = not (eng == "t" and q["eng"] == "t")
                    if not (wr and r[3] == 1 and c0 <= d0 and d1 <= c1):
                        keep.append(d)
                if wr or stage[0] == 99 or b not in fixed:
                    keep.append((c0, c1, wr, o, r[3]))
                hist[b] = keep
                if b.startswith("ps"):
                    run = bank.setdefault(b, [[], []])
                    if run[1] and run[1][-1]["eng"] != eng:
                        run[0], run[1] = run[1], []
                    for q in run[0]:
                        o["deps"][q["id"]] = True
                    if eng == "t" and run[1] and run[1][-1] is not o:
                        o["deps"].setdefault(run[1][-1]["id"], False)
                    if not run[1] or run[1][-1] is not o:
                        run[1].append(o)
        ops.append(o)
        return o

    fixed = set(list(SB)[list(SB).index("ia"):] + ["book"])

    def vcost(out, in0, two=False):
        n = width(in0)
        if in0[0] == "ind":
            return 60 + n * GAT * CY
        half = dty(out) in (bf, H16, u16) and dty(in0) in (bf, H16, u16)
        return max(64, n * (2 if two else 1) * (0.5 if half else 1)) * CY

    def tt(out, a, b, o_):
        two = not (a[0].startswith("ps") or b[0].startswith("ps"))
        op("v", vcost(out, a, two), [out], [a, b], lambda g, T: g.vector.tensor_tensor(ap(T, out), ap(T, a), ap(T, b), o_))

    def ts(out, a, s1, o0, s2=None, o1=None):
        if o1 is None:
            fn = lambda g, T: g.vector.tensor_scalar(ap(T, out), ap(T, a), ap(T, s1), None, o0)
        else:
            fn = lambda g, T: g.vector.tensor_scalar(ap(T, out), ap(T, a), ap(T, s1), ap(T, s2), o0, o1)
        op("v", vcost(out, a), [out], [a, s1, s2], fn)

    def cp(out, a):
        op("v", vcost(out, a), [out], [a], lambda g, T: g.vector.tensor_copy(ap(T, out), ap(T, a)))

    def scan(out, d0, d1, o0, o1):
        op("v", vcost(out, d1), [out], [d0, d1], lambda g, T: g.vector.tensor_tensor_scan(ap(T, out), ap(T, d0), ap(T, d1), 0.0, o0, o1))

    def turn(out, a):
        op("v", vcost(out, a), [out], [a], lambda g, T: g.vector.transpose(ap(T, out), ap(T, a)))

    def mset(out, v):
        op("v", max(64, width(out)) * CY, [out], [], lambda g, T: g.vector.memset(ap(T, out), v))

    def act(out, a, f=F.Copy, bias=None, scale=None):
        c = 80 + width(a) * CY * (GAT if a[0] == "ind" else 1)
        more = [(k, v) for k, v in (("bias", bias), ("scale", scale)) if v is not None]
        op("s", c, [out], [a, bias, scale], lambda g, T: g.scalar.activation(ap(T, out), ap(T, a), f, **{k: ap(T, v) for k, v in more}))

    def mm(out, l, r, st, sp):
        c = max(min(64, width(l)), width(r)) * (4 if dty(l) == f32 else 1) * PCY
        op("t", c, [out], [l, r], lambda g, T: g.tensor.matmul(ap(T, out), ap(T, l), ap(T, r), st, sp))

    def iota(out, pat, base=0, cm=0):
        op("g", 160 + 2 * width(out) * CY, [out], [], lambda g, T: g.iota(ap(T, out), pat, base, cm))

    def dma(q, sem, outs, ins, fn, lat):
        o = op(q, 60, outs, ins, fn, "d", sem, lat)
        if outs and q in lastq:
            o["deps"][lastq[q]] = False
        lastq[q] = o["id"]

    def ind(win, c0, n):
        return ("ind", win, R("lst", c0, c0 + n))

    def send(src, dst, to, sem):
        shared = None
        for q in range(NS):
            if topo.chip(cores[q]) != topo.chip(me):
                e = topo.engines(me, cores[q])
                shared = e if shared is None else [x for x in shared if x in e]
        near = [cores[q] for q in to if topo.chip(cores[q]) == topo.chip(me)]
        far = [cores[q] for q in to if cores[q] not in near]
        final = [(far, shared)] if far else []
        if near:
            final.append((near, [x for x in topo.engines(me, near[0]) if x not in shared]))
        nb = width(src) * (2 if dty(src) == bf else 4)
        rows = max(128 * len(qs) // len(e) for qs, e in final)
        o = op("g", CALL, [], [src], lambda g, T: write(g, T, topo, final, src, dst, sem), "r", sem, HOP + rows * (ROW + nb * BYTE))
        o["loc"] = sum(len(e) for qs, e in final)
        o["rows"], o["bytes"] = rows, nb
        for qs, e in final:
            for q in [cores.index(x) for x in qs]:
                arrive[(q, sem)] = arrive.get((q, sem), 0) + len(e)
                sends.setdefault((q, sem), []).append(o)

    others = [(s + k) % NS for k in range(1, NS)]
    land.update({"lb": (M * NS, "rl%d"), "al": (192, "ra%d"), "pl": (32, "rp%d")})

    for h, q in enumerate("ys"):
        eng = lambda g, q=q: g.sync if q == "y" else g.scalar
        dma(q, "dh%d" % h, [R("handi", 256 * h, 256 * h + 256)], [],
            lambda g, T, h=h, eng=eng: eng(g).dma_start(T.handi[:, 256 * h:256 * h + 256], T.hand[:, 256 * h:256 * h + 256]), 2300)
        for c in range(NC * (1 - h)):
            dma(q, "dld", [R("ldi", 8 * c, 8 * c + 8)], [],
                lambda g, T, c=c: g.sync.dma_start(T.ldi[:, 8 * c:8 * c + 8], T.ld[:, 128 * c:128 * c + 128]), 2800)
        dma(q, "dbk%d" % h, [R("book", 2048 * h, 2048 * h + 2048)], [],
            lambda g, T, h=h, eng=eng: eng(g).dma_start(T.book[:, 2048 * h:2048 * h + 2048], T.bk[:, 2048 * h:2048 * h + 2048]), 5500)
    LD = R("ldi", 0, 32)
    BOOK = R("book", 0, 4096)

    def col(k):
        return R("pf", k, k + 1)
    iota(R("pi", 0, 1), [[0, 1]], 0, 1)
    P = R("pi", 0, 1)
    for k, (sh, m) in enumerate(((0, 15), (0, 7), (3, 1), (4, 1), (4, 7), (3, 15))):
        ts(R("pj", k, k + 1), P, sh, A.arith_shift_right, m, A.bitwise_and)
    cp(R("pf", 0, 6), R("pj", 0, 6))
    PB, P8, B3, B4, PG, PK = [col(k) for k in range(6)]
    ts(col(10), P8, 18.0, A.mult, B3, A.add)
    ts(col(11), P8, 16.0, A.mult, B3, A.add)
    ts(col(12), P8, float(M), A.mult, B3, A.add)
    ts(col(13), P8, 24.0, A.mult, B3, A.add)
    ts(col(14), P8, 18.0, A.mult, PK, A.add)
    ts(col(16), B4, -1.0, A.mult, 1.0, A.add)
    ts(col(17), PB, 8.0, A.mult)
    ts(col(18), P8, 18.0, A.mult, 16.0, A.add)
    mset(col(19), -1.0 / 64)
    mset(col(20), 2048.0)
    ts(col(21), P, 0.0, A.is_equal)
    ts(col(22), P, 1.0, A.is_equal)
    iota(R("ih", 0, 18), [[1, 18]])
    IH = lambda n: R("ih", 0, n)
    L_HP, L_OB, L_CO, L_YO, L_G, L_OH, L_M, L_AP, L_PC, L_PL, L_AL, L_D = 0, 8, 16, 24, 32, 50, 60, 64, 68, 88, 90, 92
    lst = lambda a, n: R("lst", a, a + n)
    ts(lst(L_HP, 8), IH(8), col(17), A.add)
    ts(lst(L_OB, 8), IH(8), 0.0, A.mult, P8, A.add)
    ts(R("ij", 0, 16), IH(16), 2.0, A.mult)
    ts(lst(L_CO, 8), R("ij", 0, 8), col(10), A.add)
    ts(lst(L_YO, 8), R("ij", 0, 8), col(11), A.add)
    ts(lst(L_AP, 4), R("ij", 0, 4), col(13), A.add)
    ts(col(15), B3, -1.0, A.mult, 1.0, A.add)
    for par in range(2):
        ts(lst(L_M + 2 * par, 1), col(15), float(W * (1 + par)), A.mult, col(18), A.add)
        ts(lst(L_M + 2 * par + 1, 1), col(18), 3.0 * W - 1, A.add)
    for k, a in enumerate((136, 152, 128, 144, 160)):
        ts(lst(L_PC + 4 * k, 4), R("ij", 0, 4), col(12), A.add, float(a), A.add)
    ts(col(6), B3, 16.0, A.mult, P8, A.add)
    ts(lst(L_PL, 2), IH(2), 8.0, A.mult, col(6), A.add)
    ts(col(7), B3, 24.0, A.mult, P8, A.add)
    ts(col(8), col(7), 24.0 * (2 * s % NS) + (8 if s < NS // 2 else 16), A.add)
    ts(lst(L_AL, 2), IH(2), 8.0 if s < NS // 2 else -8.0, A.mult, col(8), A.add)
    for k in range(2):
        ts(lst(L_D + k, 1), P8, 8.0, A.mult, 7.0, A.add)
    ts(R("im", 0, 18), IH(18), 16.0, A.mult, PB, A.add)
    ts(R("inn", 0, 18), R("im", 0, 18), 3641.0, A.mult)
    ts(R("im", 0, 18), R("inn", 0, 18), 16, A.arith_shift_right)
    cp(lst(L_G, 18), R("im", 0, 18))
    ts(lst(L_OH, 9), R("im", 0, 9), 18.0, A.mult, 16.0, A.add)
    iota(R("ia", 0, 128), [[-1, 128]], 0, 1)
    IA = R("ia", 0, 128)
    I32 = R("i32", 0, 128)
    ts(I32, IA, 0.0, A.is_equal)
    IB = {}
    for k, w in enumerate((1, -1, 2 ** 18, -2 ** 19, 2 ** 22, -16, 2048, 2 ** 19, -1 / 16, M / 256, -2048)):
        IB[w] = R("ibf", 128 * k, 128 * k + 128)
        act(IB[w], I32, F.Copy, None, float(w))
    IF = {w: R("i32", 128 * k, 128 * k + 128) for k, w in enumerate((1, 1 / 16, -1 / 16))}
    for w in (1 / 16, -1 / 16):
        act(IF[w], I32, F.Copy, None, w)
    SW = {}
    for a in range(2):
        for b in range(2):
            SW[a, b] = R("sw", 128 * (2 * a + b), 128 * (2 * a + b) + 128)
            ts(SW[a, b], IA, 16.0 * (a - b), A.is_equal, B4 if a else col(16), A.mult)
    GH = R("gh", 0, 8)
    ts(GH, IH(8), PG, A.is_equal)
    act(R("gh2", 0, 8), GH, F.Copy, None, 2.0)
    act(R("gh2", 8, 16), GH, F.Copy, None, -1.0)
    iota(R("ib", 0, 128), [[0, 8], [1, 16]])
    ts(R("same", 0, 128), R("ib", 0, 128), PB, A.is_equal, -416.0, A.mult)
    iota(R("ic", 0, W), [[1, W]])
    for b, w in (("pe", 16.0), ("pb", 65536.0), ("pd", -32.0)):
        ts(R(b, 0, W), R("ic", 0, W), col(14), A.is_equal, w, A.mult)
    iota(R("ie", 0, W), [[0, 8], [1, 18]])
    IE = R("ie", 0, W)
    C = [R("c%d" % k, 0, W) for k in range(7)]
    ts(C[1], IE, 16.0, A.is_lt)
    ts(C[0], IE, 0.5, A.mult, 2.0 ** 17 + 32768, A.add)
    tt(R("kt", 0, W), C[0], C[1], A.mult)
    iota(R("iff", 0, 128), [[1, 16], [0, 8]])
    ts(R("ktc", 0, 128), R("iff", 0, 128), 0.5, A.mult, 2.0 ** 17 + 32768, A.add)
    SEG = R("seg", 0, W)
    ts(SEG, IE, 1.0, A.min)
    ts(C[2], IE, -1.0, A.mult, float(2 ** 19 + 65536 + 15), A.add)
    tt(R("k0", 0, W), C[2], C[1], A.mult)
    ts(C[3], IE, 113.0, A.add, col(22), A.mult)
    ts(col(23), col(21), 622592.0, A.mult)
    ts(C[4], C[3], -1.0, A.mult, col(23), A.add)
    tt(C[5], C[4], C[1], A.mult)
    ts(col(9), col(21), 65280.0, A.mult)
    ts(C[6], IE, 16.0, A.is_equal, col(9), A.mult)
    tt(R("ckc", 0, W), C[5], C[6], A.add)
    mset(R("one", 0, 128), 1.0)
    mset(R("cen", 0, 128), -2040.0)
    ts(R("two", 0, 128), R("ic", 0, 128), 8.0 * KA, A.is_ge, -0.25, A.mult)
    iota(R("ig", 0, 320), [[0, 40], [1, 8]])
    ts(R("rst", 0, 320), R("ig", 0, 320), 0.0, A.is_equal, 2.0 ** 24, A.mult)
    ts(R("zc", 0, 320), R("ig", 0, 320), 256.0, A.mult)
    mset(R("zc", 192, 256), 0.0)
    mset(R("dk", W - 1, NC * W, W), 0.0)
    mset(R("ltc", 0, 8), 2.0)
    mset(R("ltc", 8, 16), float(65536 - 2 ** 23))
    ts(R("ltc", 16, 24), IH(8), 16.0, A.mult, PB, A.add)
    ZERO = R("so", NC * 576, NC * 576 + 576)
    mset(ZERO, 0.0)

    def halves(f, *rs):
        for h in range(2):
            f(*[(r[0], r[1] + h * (r[2] - r[1]) // 2, r[1] + (h + 1) * (r[2] - r[1]) // 2) + r[3:] if isinstance(r, tuple) else r for r in rs])

    def B(b, c, n, a=0, e=None, st=1, k=0):
        return R(b, (k * NC + c) * n + a, (k * NC + c) * n + (n if e is None else e), st)

    def PS(c, a, e, st=1, p=128, p0=0):
        return R("ps%d" % (3 + c), a, e, st, p, p0)

    def SO(c, j, a=0, e=W, st=1):
        return B("so", c, 576, W * j + a, W * j + e, st)

    def derive(c):
        tt(B("co", c, 128), ind(B("ck", c, W), L_CO, 8), R("ktc", 0, 128), A.subtract)
        tt(B("dk", c, W, 0, W - 1), B("ck", c, W, 0, W - 1), B("ck", c, W, 1, W), A.subtract)
        cp(B("cki", c, W), B("ck", c, W))
        ts(B("cs", c, W), B("cki", c, W), 4, A.arith_shift_right, 3, A.bitwise_and)

    def offer(n, c):
        l0 = M * NS * (4 * n + c)
        m = l0 + M * s
        zi, zp, wl, pc = [lambda a, e, b=b: B(b, c, SB[b][0] // NC, a, e) for b in ("zi", "zp", "wl", "pc")]
        pb = lambda a, e: B("pb3", c, 32, a, e, k=n)
        cp(zi(0, 32), ind(B("so", c, 576), L_M + 2 * ((n + 1) % 2), 2))
        ts(B("offy", c, 8), SO(c, 3, 15, W, 18), 1 / 16, A.mult, -8192.0, A.add)
        act(R("lb", m, m + 128), ("ind", BOOK, B("offy", c, 8)))
        ts(zp(0, 24), zi(0, 24), 4, A.arith_shift_right, 255, A.bitwise_and)
        ts(zp(24, 40), zi(8, 24), 12, A.arith_shift_right, 31, A.bitwise_and)
        cp(R("lb", m + 128, m + M), zp(0, 40))
        send(R("lb", m, m + M), R("lb", m, m + M), others, "rl%d" % (4 * n + c))
        lb = R("lb", l0, l0 + M * NS)
        act(pc(0, 320), ind(lb, L_PC, 20))
        mm(PS(c, 0, 320), R("one", 0, 128, 1, 1), R("zc", 0, 320, 1, 1), True, False)
        for k in range(5):
            mm(PS(c, 64 * k, 64 * k + 64), IB[2048], pc(0, 64), False, False)
            mm(PS(c, 64 * k, 64 * k + 64), IB[2 ** 19], pc(64, 128), False, False)
        mm(PS(c, 0, 192), IB[1], pc(128, 320), False, True)
        scan(B("zr", c, 320), R("rst", 0, 320), PS(c, 0, 320), A.add, A.min)
        tt(pb(0, 32), ind(B("zr", c, 320, 256), L_D, 2), B("zr", c, 320, 7, 256, 8), A.subtract)
        ts(wl(0, 8), pb(8, 16), -1.0, A.mult)
        ts(wl(8, 16), wl(0, 8), 3, A.bitwise_and)
        mm(PS(c, 432, 456), IB[1], R("ltc", 0, 24), True, False)
        mm(PS(c, 432, 440), IB[-1 / 16], pb(8, 16), False, False)
        mm(PS(c, 432, 440), IB[-16], pb(16, 24), False, False)
        mm(PS(c, 440, 448), IB[-2048], pb(8, 16), False, False)
        mm(PS(c, 440, 448), IB[-2 ** 19], pb(16, 24), False, False)
        mm(PS(c, 440, 448), R("same", 0, 128), pb(0, 8), False, False)
        mm(PS(c, 448, 456), IB[M / 256], pb(24, 32), False, True)
        act(B("lt", c, 24), PS(c, 432, 456))
        cp(B("offs", c, 8), B("lt", c, 24, 16, 24))
        act(B("ybf", c, 128), ("ind", lb, B("offs", c, 8)))

    MAG = 1.5 * 2.0 ** 23
    order = A.is_le if s < NS // 2 else A.is_gt

    def cards(c, dst):
        ts(dst, SO(c, 1, 16, 2 * W, 18), 16 * MAG, A.add, 16 * MAG, A.subtract)

    def diffs(c, mine, got):
        act(B("gg", c, 32), got)
        tt(B("fd", c, 32, 0, 16), B("gg", c, 32, 16, 32), mine, A.subtract)
        tt(B("fd", c, 32, 16, 32), B("gg", c, 32, 0, 16), B("gg", c, 32, 16, 32), A.subtract)

    def deltas(c, first):
        tt(B("sm", c, 48, 8, 24), ind(first, L_OB, 1), B("fd", c, 32, 16, 32), A.mult)
        tt(B("dl", c, 16), B("sm", c, 48, 8, 24), B("fd", c, 32, 0, 16), A.add)

    def redeal(c, first, last):
        deltas(c, first)
        tt(B("xx", c, 2 * W), ind(B("dl", c, 16), L_G, 18), B("oh", c, 2 * W), A.mult)
        new, ck = PS(c, 2 * W, 3 * W), B("ck", c, W)
        if last:
            mm(new, IF[-1 / 16], R("kt", 0, W), True, False)
            mm(new, IF[1 / 16], ck, False, False)
        for j in range(2):
            mm(new, IF[1 / 16 if last else 1], B("xx", c, 2 * W, W * j, W * j + W), j == 0 and not last, j == 1)
        if last:
            cp(B("cc", c, W), new)
        else:
            tt(ck, new, ck, A.add)

    for c in range(NC):
        stage[0] = c
        ts(B("hp", c, 128), ind(B("handi", c, 128), L_HP, 8), -2048.0, A.add, 16.0, A.mult)
        turn(B("ht", c, 128), B("hp", c, 128))
        act(B("so", c, 576), ZERO)
        mm(PS(c, 2 * W, 3 * W), I32, R("kt", 0, W), True, False)
        for n in range(8):
            for g_ in range(2):
                a = 32 * (n // 2) + 16 * g_
                mm(PS(c, 2 * W + 18 * n, 2 * W + 18 * n + 16), SW[n % 2, g_], B("ht", c, 128, a, a + 16), False, n == 7 and g_ == 1)
        act(B("ck", c, W), PS(c, 2 * W, 3 * W))
        op("v", 64 * CY, [SO(c, 0, 16, W, 18)], [LD],
           lambda g, T, c=c: g.vector.tensor_scalar(ap(T, SO(c, 0, 16, W, 18)), T.ldi[:, 8 * c:8 * c + 8], float(s), 16.0, A.not_equal, A.mult))
        cp(SO(c, 3, 15, W, 18), B("ck", c, W, 0, W, 18))
        offer(0, c)
        stage[0] = 4 + c
        derive(c)

    dbank = [0]
    for n in range(4):
        for c in range(NC):
            stage[0] = 4 + 4 * n + c
            y = B("ybf", c, 128)
            wd = lambda k: B("pb3", c, 32, 24, 32, k=k)
            OH = lambda k: B("oh", c, 2 * W, W * k, W * k + W)
            isl = B("isl", c, 8, k=n)
            ts(isl, wd(n), 256.0 * s, A.is_equal)
            if n == 2:
                tt(B("sm", c, 48, 0, 8), wd(1), wd(2), order)
                redeal(c, B("sm", c, 48, 0, 8), False)
                derive(c)
            tt(B("dk", c, W, 16, W, 18), isl, SO(c, 3, 15, W, 18), A.mult)
            tt(B("v1", c, 128), ind(B("lt", c, 24, 0, 8), L_OB, 8), B("co", c, 128), A.mult)
            tt(B("v2", c, 128), ind(B("lt", c, 24, 8, 16), L_OB, 8), B("v1", c, 128), A.add)
            halves(ts, B("v3", c, 128), B("v2", c, 128), 5, A.arith_shift_right, 4095, A.bitwise_and)
            halves(cp, B("offa", c, 128), B("v3", c, 128))
            tt(B("mat", c, W), ind(B("wl", c, 16, 8, 16), L_G, 9), B("cs", c, W), A.is_equal)
            KS = KSL[n]
            xd = lambda a, e: B("xd", c, 2048, 128 * a, 128 * e)
            off = lambda a, e: ("ind", BOOK, B("offa", c, 128, 8 * a, 8 * e))
            us = [(k, min(k + 4, KS), True) for k in range(0, KS, 4)]
            uv = [x for x in ((KS, KA, False), (KA, 16, False)) if x[0] < x[1]]
            for (k0, k1, onS) in us[:1] + uv + us[1:]:
                ph = B("phi", c, 2048, 128 * k0, 128 * k1)
                if onS:
                    d = "ps%d" % (0, 1, 2, 7)[dbank[0]]
                    dbank[0] = (dbank[0] + 1) % 4
                    act(xd(k0, k1), off(k0, k1))
                    mm(R(d, 0, 128 * (k1 - k0)), IB[1], xd(k0, k1), True, False)
                    for k in range(k0, k1):
                        mm(R(d, 128 * (k - k0), 128 * (k + 1 - k0)), IB[-1], y, False, k + 1 == k1)
                    act(ph, R(d, 0, 128 * (k1 - k0)), F.Abs, col(19))
                else:
                    for k in range(k0, k1):
                        tt(xd(k, k + 1), off(k, k + 1), y, A.subtract)
                    if k0 < KA:
                        act(ph, xd(k0, k1), F.Abs, col(19))
                    else:
                        ts(B("ph2", c, 512), xd(k0, k1), 1.0 / 64, A.max)
            P1 = PS(c, 0, 128)
            mm(P1, R("one", 0, 128, 1, 1), R("cen", 0, 128, 1, 1), True, False)
            for b in range(16):
                mm(PS(c, b, 128, 16, 128, 8 * KA), B("xd", c, 2048, 128 * KA + b, 2048, 16), R("gh2", 8, 16), False, False)
                mm(PS(c, b, 128, 16, 128, 8 * KA), B("ph2", c, 512, b, 512, 16), R("gh2", 0, 8), False, False)
            for b in range(16):
                mm(PS(c, b, 128, 16, 8 * KA), B("phi", c, 2048, b, 128 * KA, 16), GH, False, False)
            mm(P1, R("two", 0, 128, 1, 1), R("one", 0, 128, 1, 1), False, True)
            ee, beat, ck, dk, nn = B("ee", c, 128), B("beat", c, 128), B("ck", c, W), B("dk", c, W), B("nn", c, W)
            halves(ts, ee, P1, MAG, A.add, MAG, A.subtract)
            halves(tt, beat, P1, ee, A.is_lt)
            halves(tt, B("be", c, 128), beat, ee, A.mult)
            K = PS(c, W, 2 * W)
            const = lambda k: mm(k, R("one", 0, 128, 1, 2), R("ckc", 0, W, 1, 2), True, False)
            const(K)
            mm(K, IB[2 ** 18], B("mat", c, W), False, False)
            mm(PS(c, W + 16, 2 * W, 18), IB[2 ** 22], isl, False, False)
            if n % 2:
                mm(K, IB[-2 ** 19], OH(0), False, False)
            mm(K, ee, R("pe", 0, W), False, False)
            mm(K, beat, R("pb", 0, W), False, False)
            mm(K, B("be", c, 128), R("pd", 0, W), False, True)
            halves(scan, SO(c, 0), SEG, K, A.mult, A.max)
            halves(tt, nn, K, SO(c, 0), A.is_lt)
            halves(scan, SO(c, 1 + n % 2), nn, dk, A.mult, A.add)
            if n == 3:
                a0 = 192 * c + 24 * s
                mi = lambda k: B("mi", c, 40, 8 * k, 8 * k + 8)
                ts(B("sm", c, 48, 0, 8), wd(3), 256.0 * s, A.is_le, 2.0 * s, A.add)
                cp(mi(0), SO(c, 0, 16, W, 18))
                ts(mi(1), mi(0), 16 * 8191, A.bitwise_and)
                tt(R("al", a0, a0 + 8), mi(1), B("sm", c, 48, 0, 8), A.add)
                cards(c, R("al", a0 + 8, a0 + 24))
                send(R("al", a0, a0 + 24), R("al", a0, a0 + 24), others, "ra%d" % c)
            if n == 1:
                cf = B("cf", c, 16)
                cards(c, cf)
                to = [s // 2, NS // 2 + s // 2]
                dst = B("pl", c, 32, 16 * (s % 2), 16 * (s % 2) + 16)
                send(cf, dst, [q for q in to if q != s], "rp%d" % c)
                if s in to:
                    op("v", 64 * CY, [B("pl", c, 32)], [cf], lambda g, T, dst=dst, cf=cf: g.vector.tensor_copy(ap(T, dst), ap(T, cf)))
                else:
                    seq[0] += 1
            oh = OH(n % 2)
            tt(oh, ind(SO(c, 1 + n % 2), L_OH, 9), ck, A.is_equal)
            if n == 3:
                wo = lambda k: B("wo", c, 24, 8 * k, 8 * k + 8)
                tt(wo(0), B("isl", c, 8, k=1), B("isl", c, 8, k=2), A.add)
                tt(wo(1), wo(0), isl, A.add)
                diffs(c, R("al", a0 + 8, a0 + 24), ind(B("al", c, 192), L_AL, 2))
                act(B("mf", c, 64), ind(B("al", c, 192), L_AP, 4))
                scan(B("mn", c, 64), R("rst", 0, 64), B("mf", c, 64), A.add, A.min)
                cp(mi(2), B("mn", c, 64, 7, 64, 8))
                ts(mi(3), mi(2), 1, A.bitwise_and)
                ts(mi(4), mi(2), 14, A.bitwise_and)
                ts(B("isl", c, 8, k=4), mi(4), 2.0 * s, A.is_equal)
                tt(wo(2), wo(1), B("isl", c, 8, k=4), A.add)
                dma("y", "dw%d" % c, [], [wo(2)],
                    lambda g, T, c=c: g.sync.dma_start(T.yw[:, 128 * c:128 * c + 128], T.wo[:, 24 * c + 16:24 * c + 24]), 2000)
                redeal(c, mi(3), True)
                for k in range(8):
                    for v in range(2):
                        a = 18 * (2 * (k // 2) + v)
                        mm(PS(c, 16 * k, 16 * k + 16), SW[k % 2, v], B("cc", c, W, a, a + 16), v == 0, v == 1)
                turn(B("tr", c, 128), P1)
                act(B("yo", c, 128), ind(B("tr", c, 128), L_YO, 8), F.Identity, col(20))
                dma("y", "dy%d" % c, [], [B("yo", c, 128)],
                    lambda g, T, c=c: g.sync.dma_start(T.yc[:, 128 * c:128 * c + 128], T.yo[:, 128 * c:128 * c + 128]), 2000)
                continue
            K3 = PS(c, 2 * W, 3 * W)
            const(K3)
            mm(K3, ee, R("pe", 0, W), False, False)
            if n == 1:
                mm(K3, IB[-2 ** 19], OH(0), False, False)
            mm(K3, IB[-2 ** 19], oh, False, True)
            if n == 1:
                row0 = B("dk", c, W, 0, W, 18)
                tt(B("k3", c, W), K3, R("k0", 0, W), A.max)
                K3 = B("k3", c, W)
                diffs(c, B("cf", c, 16), ind(B("pl", c, 32), L_PL, 2))
                ts(B("sm", c, 48, 0, 8), wd(1), 256.0 * s, order)
                deltas(c, B("sm", c, 48, 0, 8))
                tt(B("sm", c, 48, 24, 40), B("dl", c, 16), B("oh", c, 2 * W, 0, 2 * W, 18), A.mult)
                tt(B("sm", c, 48, 40, 48), B("sm", c, 48, 24, 32), B("sm", c, 48, 32, 40), A.add)
                tt(row0, row0, B("sm", c, 48, 40, 48), A.add)
            halves(scan, B("m3", c, W), SEG, K3, A.mult, A.max)
            halves(tt, nn, K3, B("m3", c, W), A.is_lt)
            halves(scan, SO(c, 3), nn, dk, A.mult, A.add)
            offer(n + 1, c)


def place(res, cost, pre, suc, head, key):
    left, at, t0, lines = [len(p) for p in pre], list(head), [0.0] * len(res), {}
    todo = [(key[i], i) for i in range(len(res)) if not left[i]]
    while todo:
        x = min(todo)
        todo.remove(x)
        i = x[1]
        S, E = lines.setdefault(res[i], ([], []))
        t, c, pos = at[i], cost[i], len(S)
        while pos and E[pos - 1] > t:
            pos -= 1
        while pos < len(S) and S[pos] < t + c:
            t = max(t, E[pos])
            pos += 1
        S.insert(pos, t)
        E.insert(pos, t + c)
        t0[i] = t
        for j, l in suc[i]:
            at[j] = max(at[j], t + c + l)
            left[j] -= 1
            if not left[j]:
                todo.append((key[j], j))
    return t0


def graph(ops, case):
    calc, gat, wait, slow = case
    res, cost = [o["eng"] for o in ops], [(o["cost"] + o["gat"] * (gat - 1)) * (calc if o["eng"] in "vst" else 1) for o in ops]
    pre, dn = [[] for _ in ops], {}
    for o in ops:
        if o["kind"] == "r":
            dn[o["sem"]] = len(res)
            res.append("d")
            cost.append((o["lat"] - HOP) * slow)
            pre.append([(o["id"], 500.0)])
    for o in ops:
        p = pre[o["id"]]
        for q, w in o["deps"].items():
            p.append((q, 0.0 if not w else (ops[q]["lat"] if ops[q]["kind"] == "d" else wait)))
        p += [(dn[sm_], HOP * (1 + slow) / 2 - 500.0) for sm_ in o["rw"]]
    suc = [[] for _ in res]
    for i, p in enumerate(pre):
        for q, l in p:
            suc[q].append((i, l))
    return res, cost, pre, suc


def length(t0, res, cost, pre, tail):
    done, free = {}, {}
    for i in sorted(range(len(res)), key=lambda i: (t0[i], i)):
        done[i] = free[res[i]] = max([free.get(res[i], 0.0)] + [done[q] + l for q, l in pre[i]]) + cost[i]
    return max(done[i] + tail[i] for i in done)


def plan(cores, topo):
    every, sends, arrive = [], {}, {}
    for s in range(NS):
        build(s, cores, topo, every, sends, arrive)
    ops = [o for o in every if o["s"] == 0]
    G = [graph(ops, x) for x in CASES]
    base = [sum(c for c, e in zip(g[1], g[0]) if e == "v") + 40000.0 for g in G]
    res, cost, pre, suc = G[0]
    n = len(res)
    st = [o["st"] for o in ops] + [o["st"] for o in ops if o["kind"] == "r"]
    tail = [o["lat"] if o["kind"] == "d" else 0.0 for o in ops] + [0.0] * (n - len(ops))
    b = place(list(range(n)), cost, suc, pre, tail, list(range(n)))
    rank = [b[i] + cost[i] for i in range(n)]
    for i in sorted(range(n), key=lambda i: rank[i]):
        st[i] = min([st[i]] + [st[j] for j, l in suc[i]])
    best = None
    for k in range(len(WTS) + SHAKES):
        res, cost, pre, suc = G[k % 4]
        if k < len(WTS):
            key = [WTS[k] * st[i] - rank[i] for i in range(n)]
        else:
            key = [best[1][i] + (300, 800, 1500)[k % 3] * ((i * 7919 + k * 104729) ** 2 % 1009) / 1009.0 for i in range(n)]
        t0 = place(res, cost, pre, suc, [0.0] * n, key)
        for _ in range(3 if k < len(WTS) else 2):
            b = place(res, cost, suc, pre, tail, [-(t0[i] + cost[i]) for i in range(n)])
            t0 = place(res, cost, pre, suc, [0.0] * n, [-(b[i] + cost[i]) for i in range(n)])
            end = sum(length(t0, g[0], g[1], g[2], tail) / x for x, g in zip(base, G))
            if best is None or end < best[0]:
                best = (end, t0)
    queue, cnt = {}, {}
    for o in sorted(every, key=lambda o: (best[1][o["k"]], o["id"])):
        o["t0"] = best[1][o["k"]]
        e = (o["s"], o["eng"])
        queue.setdefault(e, []).append(o["id"])
        if o["kind"] == "c":
            cnt[e] = o["n"] = cnt.get(e, 0) + 1
    return every, queue, arrive, best[0], sends


def rank_program(g, core, T, topo):
    s = T.rank_of(core)
    if s is None:
        return
    if "p" not in PLAN:
        PLAN["p"] = plan(list(T.cores), topo)
    ops, queue, arrive, end, sends = PLAN["p"]
    eng = {"v": g.vector, "s": g.scalar, "t": g.tensor, "g": g, "y": g.sync}
    total, dmas = {}, {}
    for o in ops:
        if o["s"] == s and o["kind"] == "d":
            dmas[o["sem"]] = dmas.get(o["sem"], 0) + 16
    for e in "ygvst":
        seen = {}
        for i in queue.get((s, e), []):
            o = ops[i]
            need = {sm_: arrive[(s, sm_)] for sm_ in o["rw"]}
            for q, w in o["deps"].items():
                p = ops[q]
                if w and p["kind"] == "c":
                    need[CNT[p["eng"]]] = max(need.get(CNT[p["eng"]], 0), p["n"])
                elif w and p["kind"] == "d":
                    need[p["sem"]] = dmas[p["sem"]]
            for sm_, v in sorted(need.items()):
                if seen.get(sm_, 0) < v:
                    eng[e].wait_ge(T.sem[sm_], v)
                    seen[sm_] = v
            ins = o["fn"](g, T)
            if o["kind"] == "c":
                ins.then_inc(T.sem[CNT[e]], 1)
                total[CNT[e]] = o["n"]
            elif o["kind"] == "d":
                ins.then_inc(T.sem[o["sem"]], 16)
            else:
                total["loc"] = total.get("loc", 0) + o["loc"]
    total.update(dmas)
    for (q, sm_), v in arrive.items():
        if q == s:
            total[sm_] = v
    for sm_, v in sorted(total.items()):
        g.wait_ge(T.sem[sm_], v)
